import numpy as np
import ml_dtypes


def mxq(x, axis, fmt="e4m3"):
    dtype, down = {"e4m3": (ml_dtypes.float8_e4m3fn, 7), "e5m2": (ml_dtypes.float8_e5m2, 14)}[fmt]
    v = np.moveaxis(np.asarray(x, np.float32).astype(ml_dtypes.bfloat16).astype(np.float64), axis, -1)
    blocks = v.reshape(v.shape[:-1] + (-1, 32))
    amax = np.abs(blocks).max(-1, keepdims=True)
    byte = np.maximum(np.where(amax > 0, np.frexp(amax)[1] - 1 + 127, 0) - down, 1)
    scale = np.exp2(byte - 127.0)
    codes = (blocks / scale).astype(np.float32).astype(dtype).astype(np.float64)
    return np.moveaxis((codes * scale).reshape(v.shape), -1, axis)


WIDE = False


def mx_kscale(k):
    if not WIDE:
        return np.ones(k)
    levels = np.array([10, -10, 5, -5, 0])
    if k % 512:
        return np.exp2(np.random.permutation(np.resize(levels, k // 32))).repeat(32)
    a = np.empty((k // 512, 16))
    for p in range(k // 512):
        a[p, :8] = np.random.permutation(np.resize(levels, 8))
        for g in range(8):
            far = levels[np.abs(levels - a[p, g]) >= 10]
            a[p, g + 8] = far[np.random.randint(len(far))]
    return np.exp2(a.ravel()).repeat(32)


def f64(x):
    return np.asarray(x).astype(np.float64)


def striped(idx):
    return np.tile(idx.reshape(-1, 16).T, (8, 1)).astype(np.uint16)


def unstriped(offs):
    return offs[:16].T.reshape(-1).astype(np.int64)


E2M1 = np.array([0.0, 0.5, 1.0, 1.5, 2.0, 3.0, 4.0, 6.0, -0.0, -0.5, -1.0, -1.5, -2.0, -3.0, -4.0, -6.0])


def pack_fp4(w):
    k, n = w.shape
    w = f64(np.asarray(w, np.float32).astype(ml_dtypes.bfloat16)).reshape(k // 32, 32, n)
    amax = np.abs(w).max(1)
    mant, ex = np.frexp(amax / 6.0)
    byte = np.clip(np.where(amax > 0, np.where(mant > 0.5, ex, ex - 1) + 127, 1), 1, 254)
    scaled = (w * np.exp2(127.0 - byte)[:, None, :]).reshape(k, n).astype(np.float32)
    c = np.ascontiguousarray(scaled.reshape(k // 512, 128, 4, n).transpose(0, 1, 3, 2)).astype(ml_dtypes.float4_e2m1fn).view(np.uint8) & 0xF
    words = (c[..., 0::2] | (c[..., 1::2] << 4)).reshape(k // 512, 128, 2 * n)
    return np.ascontiguousarray(words), np.ascontiguousarray(byte.astype(np.uint8).reshape(k // 512, 16, n))


def unpack_fp4(words, scales):
    g, _, n = scales.shape
    words = np.ascontiguousarray(words).reshape(g, 128, n, 2)
    nib = np.empty((g, 128, n, 4), np.uint8)
    nib[..., 0::2] = words & 0xF
    nib[..., 1::2] = words >> 4
    vals = E2M1[nib] * np.repeat(np.exp2(scales.astype(np.float64) - 127.0), 8, axis=1)[..., None]
    return vals.transpose(0, 1, 3, 2).reshape(g * 512, n)


def relu(v):
    return np.maximum(v, 0.0)


K, T, S, H, N, U = 512, 2048, 512, 512, 256, 1024


def setup_inputs():
    n = np.random.standard_normal
    s = mx_kscale(K)[:, None]
    u = mx_kscale(H)
    packed_w2 = pack_fp4(n((H, N)) / np.sqrt(H) / u[:, None])
    return {
        "xT": (n((K, T)) * s).astype(np.float32),
        "w1": (n((K, H)) / np.sqrt(K) / s * u).astype(np.float32),
        "w2_words": packed_w2[0],
        "w2_scales": packed_w2[1],
        "skip": (n((H, U)) * u[:, None]).astype(np.float32),
        "offs": striped(np.random.permutation(T)[:S]),
        "cell": striped(np.random.permutation(U)[:S]),
    }


def reference(xT, w1, w2_words, w2_scales, skip, offs, cell):
    xq = mxq(f64(xT)[:, unstriped(offs)], 0, "e4m3")
    up = np.zeros((H, U))
    up[:, unstriped(cell)] = relu(mxq(f64(w1), 0, "e4m3").T @ xq)
    z = up + f64(skip)
    return unpack_fp4(w2_words, w2_scales).T @ mxq(z, 0, "e4m3")

@@ -1,0 +1,156 @@
+from contextlib import ExitStack
+
+import concourse.mybir as mybir
+
+K, T, S, H, N, U = 512, 2048, 512, 512, 256, 1024
+FLOPS = 2 * K * H * S + 2 * H * N * U
+
+F32 = mybir.dt.float32
+BF16 = mybir.dt.bfloat16
+I32 = mybir.dt.int32
+U32 = mybir.dt.uint32
+U16 = mybir.dt.uint16
+U8 = mybir.dt.uint8
+FP8X4 = mybir.dt.float8_e4m3fn_x4
+FP4X4 = mybir.dt.float4_e2m1fn_x4
+ACT = mybir.ActivationFunctionType
+ADD = mybir.AluOpType.add
+
+P = 128
+PACK = 4
+ORDER = (3, 0, 1, 2)
+CHUNK = 256
+
+
+def tile_picked_unet_relu_e_kernel(tc, xT, w1, w2_words, w2_scales, skip, offs, cell, out):
+    nc = tc.nc
+    with ExitStack() as ctx:
+        keep = ctx.enter_context(tc.tile_pool(name="keep", bufs=1))
+        psum = ctx.enter_context(tc.psum_pool(name="psum", bufs=4))
+
+        offs_t = keep.tile([P, S // 16], U16, name="offs_t")
+        cell_t = keep.tile([P, S // 16], U16, name="cell_t")
+        x_rows = xT.rearrange("(p j) c -> j p c", j=PACK)
+        w_rows = w1.rearrange("(p u e) c -> u p e c", u=2, e=2)
+        s_rows = skip.rearrange("(p t) c -> t p c", t=PACK)
+
+        x_plane = [keep.tile([P, T], F32, name="x_plane%d" % j) for j in range(PACK)]
+        w_raw = [keep.tile([P, 2, H], F32, name="w_raw%d" % u) for u in range(2)]
+        s_plane = [keep.tile([P, U], F32, name="s_plane%d" % t) for t in range(PACK)]
+        w2_codes = keep.tile([P, 2 * N], U8, name="w2_codes", align_bytes=64)
+        w2_exp = keep.tile([P, N], U8, name="w2_exp", align_bytes=64)
+
+        nc.sync.dma_start(x_plane[0][:], x_rows[0])
+        nc.sync.dma_start(offs_t[:], offs)
+        nc.sync.dma_start(x_plane[1][:], x_rows[1])
+        nc.sync.dma_start(cell_t[:], cell)
+        nc.sync.dma_start(x_plane[2][:], x_rows[2])
+        nc.sync.dma_start(x_plane[3][:], x_rows[3])
+        for u in range(2):
+            nc.sync.dma_start(w_raw[u][:], w_rows[u])
+        for t in ORDER:
+            nc.sync.dma_start(s_plane[t][:], s_rows[t])
+        nc.sync.dma_start(w2_codes[:], w2_words[0])
+        nc.vector.memset(w2_exp[:].bitcast(I32), 0)
+        for q in range(4):
+            nc.sync.dma_start(w2_exp[32 * q : 32 * q + 4, :].bitcast(I32), w2_scales[0, 4 * q : 4 * q + 4, :].bitcast(I32))
+
+        window = {}
+        for t in ORDER[:3]:
+            window[t] = keep.tile([P, U], F32, name="window", tag="window%d" % t)
+            nc.vector.memset(window[t][:], 0.0)
+
+        x_bf = keep.tile([P, S, PACK], BF16, name="x_bf", align_bytes=64)
+        for j in range(PACK):
+            nc.vector.tensor_copy(x_bf[:, :, j], x_plane[j][:].indirect(offs_t[:]))
+        x_codes = keep.tile([P, S], U32, name="x_codes", align_bytes=64)
+        x_exp = keep.tile([P, S], U8, name="x_exp", align_bytes=64)
+        nc.vector.quantize_mx(out=x_codes[:].bitcast(FP8X4), scales=x_exp[:], in_=x_bf[:].rearrange("p n j -> p (n j)"))
+
+        groups = ((3, 4), (0, 1), (1, 3))
+        w_codes, w_exp = {}, {}
+        w_bf = [keep.tile([P, hi - lo, P, PACK], BF16, name="w_bf%d" % lo, align_bytes=64) for lo, hi in groups]
+        for u in range(2):
+            src = w_raw[u][:].rearrange("p e (m t) -> p m e t", t=PACK)
+            for g, (lo, hi) in enumerate(groups):
+                dst = w_bf[g][:, :, :, 2 * u : 2 * u + 2].rearrange("p t m e -> p m e t")
+                if u == 1 and g < 2:
+                    nc.vector.tensor_copy(dst, src[:, :, :, lo:hi])
+                else:
+                    nc.scalar.activation(dst, src[:, :, :, lo:hi], ACT.Copy)
+        for g, (lo, hi) in enumerate(groups):
+            codes = keep.tile([P, (hi - lo) * P], U32, name="w_codes%d" % lo, align_bytes=64)
+            exps = keep.tile([P, (hi - lo) * P], U8, name="w_exp%d" % lo, align_bytes=64)
+            nc.vector.quantize_mx(out=codes[:].bitcast(FP8X4), scales=exps[:], in_=w_bf[g][:].rearrange("p t m j -> p (t m j)"))
+            for t in range(lo, hi):
+                w_codes[t] = codes[:, (t - lo) * P : (t - lo + 1) * P]
+                w_exp[t] = exps[:, (t - lo) * P : (t - lo + 1) * P]
+
+        def hidden(t, lo, hi):
+            acc = psum.tile([P, hi - lo], F32, name="acc", tag="acc")
+            nc.tensor.matmul_mx(out=acc[:], lhsT=w_codes[t].bitcast(FP8X4), lhsT_scale=w_exp[t],
+                                rhs=x_codes[:, lo:hi].bitcast(FP8X4), rhs_scale=x_exp[:, lo:hi], start=True, stop=True)
+            h = keep.tile([P, hi - lo], F32, name="h%d_%d" % (t, lo))
+            nc.scalar.activation(h[:], acc[:], ACT.Relu)
+            return h
+
+        def scatter(t, h, lo, hi):
+            nc.vector.tensor_copy(window[t][:].indirect(cell_t[:, lo // 16 : hi // 16]), h)
+
+        chunks = U // CHUNK
+        pairs = [keep.tile([P, 2, CHUNK, 2], BF16, name="pairs%d" % c) for c in range(chunks)]
+
+        def add_skip(engine, t, c):
+            cols = slice(c * CHUNK, (c + 1) * CHUNK)
+            engine.tensor_tensor(pairs[c][:, t // 2, :, t % 2], window[t][:, cols], s_plane[t][:, cols], ADD)
+
+        first, second, third, last = ORDER
+        half = S // 2
+        h_a = hidden(first, 0, half)
+        h_b = hidden(first, half, S)
+        h_second = hidden(second, 0, S)
+        h_third = hidden(third, 0, S)
+        h_last = hidden(last, 0, S)
+        scatter(first, h_a[:], 0, half)
+        scatter(second, h_second[:, :half], 0, half)
+        scatter(first, h_b[:], half, S)
+        scatter(second, h_second[:, half:], half, S)
+        for c in range(chunks):
+            add_skip(nc.gpsimd, first, c)
+        window[last] = keep.tile([P, U], F32, name="window", tag="window%d" % first)
+        nc.gpsimd.memset(window[last][:], 0.0)
+        for c in range(chunks):
+            add_skip(nc.gpsimd, second, c)
+        scatter(third, h_third[:], 0, S)
+        for c in range(chunks):
+            add_skip(nc.gpsimd, third, c)
+        scatter(last, h_last[:], 0, S)
+
+        out_rows = out.rearrange("(g p) v -> p g v", p=P)
+        z_bf = [keep.tile([P, CHUNK, 2], F32, name="z_bf%d" % c, align_bytes=64) for c in range(chunks)]
+
+        def weave(c):
+            words = pairs[c][:].rearrange("p u v e -> p (u v e)").bitcast(F32)
+            nc.vector.tensor_copy(z_bf[c][:], words.rearrange("p (u v) -> p v u", u=2))
+
+        def finish(c):
+            codes = keep.tile([P, CHUNK], U32, name="z_codes%d" % c, align_bytes=64)
+            exps = keep.tile([P, CHUNK], U8, name="z_exp%d" % c, align_bytes=64)
+            nc.vector.quantize_mx(out=codes[:].bitcast(FP8X4), scales=exps[:],
+                                  in_=z_bf[c][:].rearrange("p v u -> p (v u)").bitcast(BF16))
+            acc = psum.tile([P, 2, CHUNK], F32, name="acc", tag="acc")
+            for g in range(2):
+                nc.tensor.matmul_mx(out=acc[:, g, :], lhsT=w2_codes[:, 2 * P * g : 2 * P * (g + 1)].bitcast(FP4X4),
+                                    lhsT_scale=w2_exp[:, P * g : P * (g + 1)],
+                                    rhs=codes[:].bitcast(FP8X4), rhs_scale=exps[:], start=True, stop=True)
+            res = keep.tile([P, 2, CHUNK], F32, name="res%d" % c)
+            nc.scalar.copy(res[:], acc[:])
+            nc.sync.dma_start(out_rows[:, :, c * CHUNK : (c + 1) * CHUNK], res[:])
+
+        for step in range(chunks + 2):
+            if step < chunks:
+                add_skip(nc.vector, last, step)
+            if 1 <= step <= chunks:
+                weave(step - 1)
+            if step >= 2:
+                finish(step - 2)

@@ -36,7 +36,7 @@ def tile_picked_unet_relu_e_kernel(tc, xT, w1, w2_words, w2_scales, skip, offs, 
 
         x_plane = [keep.tile([P, T], F32, name="x_plane%d" % j) for j in range(PACK)]
         w_raw = [keep.tile([P, 2, H], F32, name="w_raw%d" % u) for u in range(2)]
-        s_plane = [keep.tile([P, U], F32, name="s_plane%d" % t) for t in range(PACK)]
+        s_plane = [keep.tile([P, U], F32, name="s_plane", tag="s_plane%d" % t) for t in range(PACK)]
         w2_codes = keep.tile([P, 2 * N], U8, name="w2_codes", align_bytes=64)
         w2_exp = keep.tile([P, N], U8, name="w2_exp", align_bytes=64)
 
@@ -56,7 +56,7 @@ def tile_picked_unet_relu_e_kernel(tc, xT, w1, w2_words, w2_scales, skip, offs, 
             nc.sync.dma_start(w2_exp[32 * q : 32 * q + 4, :].bitcast(I32), w2_scales[0, 4 * q : 4 * q + 4, :].bitcast(I32))
 
         window = {}
-        for t in ORDER[:3]:
+        for t in ORDER:
             window[t] = keep.tile([P, U], F32, name="window", tag="window%d" % t)
             nc.vector.memset(window[t][:], 0.0)
 
@@ -86,71 +86,71 @@ def tile_picked_unet_relu_e_kernel(tc, xT, w1, w2_words, w2_scales, skip, offs, 
                 w_codes[t] = codes[:, (t - lo) * P : (t - lo + 1) * P]
                 w_exp[t] = exps[:, (t - lo) * P : (t - lo + 1) * P]
 
-        def hidden(t, lo, hi):
+        def hidden(t, edges, tag):
+            lo, hi = edges[0], edges[-1]
             acc = psum.tile([P, hi - lo], F32, name="acc", tag="acc")
-            nc.tensor.matmul_mx(out=acc[:], lhsT=w_codes[t].bitcast(FP8X4), lhsT_scale=w_exp[t],
-                                rhs=x_codes[:, lo:hi].bitcast(FP8X4), rhs_scale=x_exp[:, lo:hi], start=True, stop=True)
-            h = keep.tile([P, hi - lo], F32, name="h%d_%d" % (t, lo))
+            for a, b in zip(edges, edges[1:]):
+                nc.tensor.matmul_mx(out=acc[:, a - lo : b - lo], lhsT=w_codes[t].bitcast(FP8X4), lhsT_scale=w_exp[t],
+                                    rhs=x_codes[:, a:b].bitcast(FP8X4), rhs_scale=x_exp[:, a:b], start=True, stop=True)
+            h = keep.tile([P, hi - lo], F32, name="h", tag=tag)
             nc.scalar.activation(h[:], acc[:], ACT.Relu)
-            return h
+            nc.vector.tensor_copy(window[t][:].indirect(cell_t[:, lo // 16 : hi // 16]), h[:])
 
-        def scatter(t, h, lo, hi):
-            nc.vector.tensor_copy(window[t][:].indirect(cell_t[:, lo // 16 : hi // 16]), h)
+        pairs = keep.tile([P, PACK * U], BF16, name="pairs")
+        pair_vals = pairs[:].rearrange("p (u v e) -> p u v e", u=2, e=2)
+        pair_words = pairs[:].bitcast(F32).rearrange("p (u v) -> p v u", u=2)
 
-        chunks = U // CHUNK
-        pairs = [keep.tile([P, 2, CHUNK, 2], BF16, name="pairs%d" % c) for c in range(chunks)]
-
-        def add_skip(engine, t, c):
-            cols = slice(c * CHUNK, (c + 1) * CHUNK)
-            engine.tensor_tensor(pairs[c][:, t // 2, :, t % 2], window[t][:, cols], s_plane[t][:, cols], ADD)
+        def add_skip(engine, t, cols):
+            engine.tensor_tensor(pair_vals[:, t // 2, cols, t % 2], window[t][:, cols], s_plane[t][:, cols], ADD)
 
         first, second, third, last = ORDER
-        half = S // 2
-        h_a = hidden(first, 0, half)
-        h_b = hidden(first, half, S)
-        h_second = hidden(second, 0, S)
-        h_third = hidden(third, 0, S)
-        h_last = hidden(last, 0, S)
-        scatter(first, h_a[:], 0, half)
-        scatter(second, h_second[:, :half], 0, half)
-        scatter(first, h_b[:], half, S)
-        scatter(second, h_second[:, half:], half, S)
-        for c in range(chunks):
-            add_skip(nc.gpsimd, first, c)
-        window[last] = keep.tile([P, U], F32, name="window", tag="window%d" % first)
-        nc.gpsimd.memset(window[last][:], 0.0)
-        for c in range(chunks):
-            add_skip(nc.gpsimd, second, c)
-        scatter(third, h_third[:], 0, S)
-        for c in range(chunks):
-            add_skip(nc.gpsimd, third, c)
-        scatter(last, h_last[:], 0, S)
+        hidden(first, (0, 128), "h_head")
+        hidden(first, (128, 256, 512), "h_first")
+        add_skip(nc.gpsimd, first, slice(0, U))
+        hidden(second, (0, S), "h_second")
+        add_skip(nc.gpsimd, second, slice(0, U))
+        hidden(third, (0, S), "h_third")
+        add_skip(nc.gpsimd, third, slice(0, U))
+        hidden(last, (0, S), "s_plane%d" % first)
 
         out_rows = out.rearrange("(g p) v -> p g v", p=P)
-        z_bf = [keep.tile([P, CHUNK, 2], F32, name="z_bf%d" % c, align_bytes=64) for c in range(chunks)]
+        edges = (0, 256, 512, 768, 896, 1024)
+        chunks = [slice(lo, hi) for lo, hi in zip(edges, edges[1:])]
+        z_bf = {}
 
         def weave(c):
-            words = pairs[c][:].rearrange("p u v e -> p (u v e)").bitcast(F32)
-            nc.vector.tensor_copy(z_bf[c][:], words.rearrange("p (u v) -> p v u", u=2))
+            z_bf[c] = keep.tile([P, chunks[c].stop - chunks[c].start, 2], F32, name="z_bf", tag="z_bf%d" % (c % 3), align_bytes=64)
+            if c < 3:
+                nc.scalar.copy(z_bf[c][:], pair_words[:, chunks[c], :])
+            else:
+                nc.vector.tensor_copy(z_bf[c][:], pair_words[:, chunks[c], :])
 
         def finish(c):
-            codes = keep.tile([P, CHUNK], U32, name="z_codes%d" % c, align_bytes=64)
-            exps = keep.tile([P, CHUNK], U8, name="z_exp%d" % c, align_bytes=64)
+            width = chunks[c].stop - chunks[c].start
+            codes = keep.tile([P, width], U32, name="z_codes%d" % c, align_bytes=64)
+            exps = keep.tile([P, width], U8, name="z_exp%d" % c, align_bytes=64)
             nc.vector.quantize_mx(out=codes[:].bitcast(FP8X4), scales=exps[:],
                                   in_=z_bf[c][:].rearrange("p v u -> p (v u)").bitcast(BF16))
-            acc = psum.tile([P, 2, CHUNK], F32, name="acc", tag="acc")
+            acc = psum.tile([P, 2, width], F32, name="acc", tag="acc")
             for g in range(2):
                 nc.tensor.matmul_mx(out=acc[:, g, :], lhsT=w2_codes[:, 2 * P * g : 2 * P * (g + 1)].bitcast(FP4X4),
                                     lhsT_scale=w2_exp[:, P * g : P * (g + 1)],
                                     rhs=codes[:].bitcast(FP8X4), rhs_scale=exps[:], start=True, stop=True)
-            res = keep.tile([P, 2, CHUNK], F32, name="res%d" % c)
-            nc.scalar.copy(res[:], acc[:])
-            nc.sync.dma_start(out_rows[:, :, c * CHUNK : (c + 1) * CHUNK], res[:])
+            res = keep.tile([P, 2, width], F32, name="res%d" % c)
+            if c in (2, 4):
+                nc.vector.tensor_copy(res[:], acc[:])
+            else:
+                nc.scalar.copy(res[:], acc[:])
+            nc.sync.dma_start(out_rows[:, :, chunks[c]], res[:])
 
-        for step in range(chunks + 2):
-            if step < chunks:
-                add_skip(nc.vector, last, step)
-            if 1 <= step <= chunks:
-                weave(step - 1)
-            if step >= 2:
-                finish(step - 2)
+        for c in range(3):
+            add_skip(nc.vector, last, chunks[c])
+            weave(c)
+        add_skip(nc.vector, last, slice(768, 1024))
+        finish(0)
+        finish(1)
+        weave(3)
+        weave(4)
+        finish(2)
+        finish(3)
+        finish(4)

@@ -26,7 +26,7 @@ def tile_picked_unet_relu_e_kernel(tc, xT, w1, w2_words, w2_scales, skip, offs, 
     nc = tc.nc
     with ExitStack() as ctx:
         keep = ctx.enter_context(tc.tile_pool(name="keep", bufs=1))
-        psum = ctx.enter_context(tc.psum_pool(name="psum", bufs=4))
+        psum = ctx.enter_context(tc.psum_pool(name="psum", bufs=8))
 
         offs_t = keep.tile([P, S // 16], U16, name="offs_t")
         cell_t = keep.tile([P, S // 16], U16, name="cell_t")
@@ -36,20 +36,24 @@ def tile_picked_unet_relu_e_kernel(tc, xT, w1, w2_words, w2_scales, skip, offs, 
 
         x_plane = [keep.tile([P, T], F32, name="x_plane%d" % j) for j in range(PACK)]
         w_raw = [keep.tile([P, 2, H], F32, name="w_raw%d" % u) for u in range(2)]
-        s_plane = [keep.tile([P, U], F32, name="s_plane", tag="s_plane%d" % t) for t in range(PACK)]
+        first, second, third, last = ORDER
+        parts = {first: (0, U), second: (0, 640, U), third: (0, U), last: (0, U)}
+        s_part = {(t, lo): keep.tile([P, hi - lo], F32, name="s_part", tag="s_part%d_%d" % (t, lo))
+                  for t in ORDER for lo, hi in zip(parts[t], parts[t][1:])}
         w2_codes = keep.tile([P, 2 * N], U8, name="w2_codes", align_bytes=64)
         w2_exp = keep.tile([P, N], U8, name="w2_exp", align_bytes=64)
 
         nc.sync.dma_start(x_plane[0][:], x_rows[0])
         nc.sync.dma_start(offs_t[:], offs)
         nc.sync.dma_start(x_plane[1][:], x_rows[1])
-        nc.sync.dma_start(cell_t[:], cell)
         nc.sync.dma_start(x_plane[2][:], x_rows[2])
         nc.sync.dma_start(x_plane[3][:], x_rows[3])
         for u in range(2):
             nc.sync.dma_start(w_raw[u][:], w_rows[u])
+        nc.sync.dma_start(cell_t[:], cell)
         for t in ORDER:
-            nc.sync.dma_start(s_plane[t][:], s_rows[t])
+            for lo, hi in zip(parts[t], parts[t][1:]):
+                nc.sync.dma_start(s_part[t, lo][:], s_rows[t][:, lo:hi])
         nc.sync.dma_start(w2_codes[:], w2_words[0])
         nc.vector.memset(w2_exp[:].bitcast(I32), 0)
         for q in range(4):
@@ -69,19 +73,17 @@ def tile_picked_unet_relu_e_kernel(tc, xT, w1, w2_words, w2_scales, skip, offs, 
 
         groups = ((3, 4), (0, 1), (1, 3))
         w_codes, w_exp = {}, {}
-        w_bf = [keep.tile([P, hi - lo, P, PACK], BF16, name="w_bf%d" % lo, align_bytes=64) for lo, hi in groups]
-        for u in range(2):
-            src = w_raw[u][:].rearrange("p e (m t) -> p m e t", t=PACK)
-            for g, (lo, hi) in enumerate(groups):
-                dst = w_bf[g][:, :, :, 2 * u : 2 * u + 2].rearrange("p t m e -> p m e t")
-                if u == 1 and g < 2:
-                    nc.vector.tensor_copy(dst, src[:, :, :, lo:hi])
-                else:
-                    nc.scalar.activation(dst, src[:, :, :, lo:hi], ACT.Copy)
+        w_bf = keep.tile([P, PACK, P, PACK], BF16, name="w_bf", align_bytes=64)
+        w_dst = w_bf[:].rearrange("p t m (u e) -> p u m e t", u=2)
+        w_src = [w_raw[u][:].rearrange("p e (m t) -> p m e t", t=PACK) for u in range(2)]
+        nc.scalar.activation(w_dst[:, 0], w_src[0], ACT.Copy)
+        for lo, hi in groups[:2]:
+            nc.vector.tensor_copy(w_dst[:, 1, :, :, lo:hi], w_src[1][:, :, :, lo:hi])
+        nc.scalar.activation(w_dst[:, 1, :, :, 1:3], w_src[1][:, :, :, 1:3], ACT.Copy)
         for g, (lo, hi) in enumerate(groups):
             codes = keep.tile([P, (hi - lo) * P], U32, name="w_codes%d" % lo, align_bytes=64)
             exps = keep.tile([P, (hi - lo) * P], U8, name="w_exp%d" % lo, align_bytes=64)
-            nc.vector.quantize_mx(out=codes[:].bitcast(FP8X4), scales=exps[:], in_=w_bf[g][:].rearrange("p t m j -> p (t m j)"))
+            nc.vector.quantize_mx(out=codes[:].bitcast(FP8X4), scales=exps[:], in_=w_bf[:, lo:hi].rearrange("p t m j -> p (t m j)"))
             for t in range(lo, hi):
                 w_codes[t] = codes[:, (t - lo) * P : (t - lo + 1) * P]
                 w_exp[t] = exps[:, (t - lo) * P : (t - lo + 1) * P]
@@ -101,56 +103,78 @@ def tile_picked_unet_relu_e_kernel(tc, xT, w1, w2_words, w2_scales, skip, offs, 
         pair_words = pairs[:].bitcast(F32).rearrange("p (u v) -> p v u", u=2)
 
         def add_skip(engine, t, cols):
-            engine.tensor_tensor(pair_vals[:, t // 2, cols, t % 2], window[t][:, cols], s_plane[t][:, cols], ADD)
+            lo = max(edge for edge in parts[t] if edge <= cols.start)
+            engine.tensor_tensor(pair_vals[:, t // 2, cols, t % 2], window[t][:, cols],
+                                 s_part[t, lo][:, cols.start - lo : cols.stop - lo], ADD)
 
-        first, second, third, last = ORDER
         hidden(first, (0, 128), "h_head")
         hidden(first, (128, 256, 512), "h_first")
         add_skip(nc.gpsimd, first, slice(0, U))
         hidden(second, (0, S), "h_second")
-        add_skip(nc.gpsimd, second, slice(0, U))
+        add_skip(nc.gpsimd, second, slice(0, 640))
+        add_skip(nc.gpsimd, second, slice(640, U))
         hidden(third, (0, S), "h_third")
-        add_skip(nc.gpsimd, third, slice(0, U))
-        hidden(last, (0, S), "s_plane%d" % first)
+        for lo, hi in ((0, 128), (128, U)):
+            add_skip(nc.gpsimd, third, slice(lo, hi))
+        hidden(last, (0, S), "s_part%d_0" % second)
 
         out_rows = out.rearrange("(g p) v -> p g v", p=P)
-        edges = (0, 256, 512, 768, 896, 1024)
+        edges = (0, 128, 384, 640, 896, 1024)
         chunks = [slice(lo, hi) for lo, hi in zip(edges, edges[1:])]
         z_bf = {}
 
         def weave(c):
-            z_bf[c] = keep.tile([P, chunks[c].stop - chunks[c].start, 2], F32, name="z_bf", tag="z_bf%d" % (c % 3), align_bytes=64)
-            if c < 3:
+            z_bf[c] = keep.tile([P, chunks[c].stop - chunks[c].start, 2], F32, name="z_bf", tag="z_bf%d" % c, align_bytes=64)
+            if c < 4:
                 nc.scalar.copy(z_bf[c][:], pair_words[:, chunks[c], :])
             else:
                 nc.vector.tensor_copy(z_bf[c][:], pair_words[:, chunks[c], :])
 
-        def finish(c):
+        z_q = {}
+
+        def quant(c):
             width = chunks[c].stop - chunks[c].start
             codes = keep.tile([P, width], U32, name="z_codes%d" % c, align_bytes=64)
             exps = keep.tile([P, width], U8, name="z_exp%d" % c, align_bytes=64)
             nc.vector.quantize_mx(out=codes[:].bitcast(FP8X4), scales=exps[:],
                                   in_=z_bf[c][:].rearrange("p v u -> p (v u)").bitcast(BF16))
-            acc = psum.tile([P, 2, width], F32, name="acc", tag="acc")
+            z_q[c] = codes, exps
+
+        def finish(c):
+            width = chunks[c].stop - chunks[c].start
+            codes, exps = z_q[c]
+            res = keep.tile([P, 2, width], F32, name="res%d" % c)
+            whole = psum.tile([P, 2, width], F32, name="acc", tag="acc") if c < 2 else None
             for g in range(2):
-                nc.tensor.matmul_mx(out=acc[:, g, :], lhsT=w2_codes[:, 2 * P * g : 2 * P * (g + 1)].bitcast(FP4X4),
+                acc = whole[:, g, :] if c < 2 else psum.tile([P, width], F32, name="acc", tag="acc")[:]
+                nc.tensor.matmul_mx(out=acc, lhsT=w2_codes[:, 2 * P * g : 2 * P * (g + 1)].bitcast(FP4X4),
                                     lhsT_scale=w2_exp[:, P * g : P * (g + 1)],
                                     rhs=codes[:].bitcast(FP8X4), rhs_scale=exps[:], start=True, stop=True)
-            res = keep.tile([P, 2, width], F32, name="res%d" % c)
-            if c in (2, 4):
-                nc.vector.tensor_copy(res[:], acc[:])
-            else:
-                nc.scalar.copy(res[:], acc[:])
+                if c >= 2 and g == 0:
+                    nc.scalar.copy(res[:, g, :], acc)
+                if c >= 2 and g == 1:
+                    nc.vector.tensor_copy(res[:, g, :], acc)
+            if c < 2:
+                nc.scalar.copy(res[:], whole[:])
             nc.sync.dma_start(out_rows[:, :, chunks[c]], res[:])
 
-        for c in range(3):
-            add_skip(nc.vector, last, chunks[c])
-            weave(c)
-        add_skip(nc.vector, last, slice(768, 1024))
+        add_skip(nc.vector, last, chunks[0])
+        weave(0)
+        add_skip(nc.vector, last, chunks[1])
+        weave(1)
+        quant(0)
+        add_skip(nc.vector, last, chunks[2])
+        weave(2)
+        quant(1)
+        add_skip(nc.vector, last, chunks[3])
         finish(0)
-        finish(1)
         weave(3)
+        add_skip(nc.vector, last, chunks[4])
+        quant(2)
         weave(4)
+        finish(1)
+        quant(3)
+        quant(4)
         finish(2)
         finish(3)
         finish(4)

@@ -1,6 +1,7 @@
 from contextlib import ExitStack
 
 import concourse.mybir as mybir
+from concourse.masks import make_identity
 
 K, T, S, H, N, U = 512, 2048, 512, 512, 256, 1024
 FLOPS = 2 * K * H * S + 2 * H * N * U
@@ -118,8 +119,15 @@ def tile_picked_unet_relu_e_kernel(tc, xT, w1, w2_words, w2_scales, skip, offs, 
             add_skip(nc.gpsimd, third, slice(lo, hi))
         hidden(last, (0, S), "s_part%d_0" % second)
 
+        ident = keep.tile([P, P], F32, name="ident")
+        make_identity(nc, ident[:])
+        warm = psum.tile([P, S], F32, name="acc", tag="acc")
+        nc.tensor.transpose(warm[:, :P], window[last][:, :P], ident[:])
+        for t in (first, second):
+            nc.tensor.matmul_mx(out=warm[:], lhsT=w_codes[t].bitcast(FP8X4), lhsT_scale=w_exp[t],
+                                rhs=x_codes[:].bitcast(FP8X4), rhs_scale=x_exp[:], start=True, stop=True)
         out_rows = out.rearrange("(g p) v -> p g v", p=P)
-        edges = (0, 128, 384, 640, 896, 1024)
+        edges = (0, 128, 256, 512, 768, 896, 1024)
         chunks = [slice(lo, hi) for lo, hi in zip(edges, edges[1:])]
         z_bf = {}
 
@@ -144,37 +152,49 @@ def tile_picked_unet_relu_e_kernel(tc, xT, w1, w2_words, w2_scales, skip, offs, 
             width = chunks[c].stop - chunks[c].start
             codes, exps = z_q[c]
             res = keep.tile([P, 2, width], F32, name="res%d" % c)
-            whole = psum.tile([P, 2, width], F32, name="acc", tag="acc") if c < 2 else None
+            joint = width == P
+            whole = psum.tile([P, 2, width], F32, name="acc", tag="acc") if joint else None
             for g in range(2):
-                acc = whole[:, g, :] if c < 2 else psum.tile([P, width], F32, name="acc", tag="acc")[:]
+                acc = whole[:, g, :] if joint else psum.tile([P, width], F32, name="acc", tag="acc")[:]
                 nc.tensor.matmul_mx(out=acc, lhsT=w2_codes[:, 2 * P * g : 2 * P * (g + 1)].bitcast(FP4X4),
                                     lhsT_scale=w2_exp[:, P * g : P * (g + 1)],
                                     rhs=codes[:].bitcast(FP8X4), rhs_scale=exps[:], start=True, stop=True)
-                if c >= 2 and g == 0:
-                    nc.scalar.copy(res[:, g, :], acc)
-                if c >= 2 and g == 1:
-                    nc.vector.tensor_copy(res[:, g, :], acc)
-            if c < 2:
-                nc.scalar.copy(res[:], whole[:])
-            nc.sync.dma_start(out_rows[:, :, chunks[c]], res[:])
+                if not joint:
+                    if (c, g) in ((3, 1), (5, 0)):
+                        nc.vector.tensor_copy(res[:, g, :], acc)
+                    else:
+                        nc.scalar.copy(res[:, g, :], acc)
+                    if c in (2,):
+                        nc.sync.dma_start(out_rows[:, g, chunks[c]], res[:, g, :])
+            if joint:
+                if (c, 0) in ((3, 1), (5, 0)):
+                    nc.vector.tensor_copy(res[:], whole[:])
+                else:
+                    nc.scalar.copy(res[:], whole[:])
+            if c not in (2,):
+                nc.sync.dma_start(out_rows[:, :, chunks[c]], res[:])
 
         add_skip(nc.vector, last, chunks[0])
         weave(0)
         add_skip(nc.vector, last, chunks[1])
         weave(1)
         quant(0)
+        finish(0)
         add_skip(nc.vector, last, chunks[2])
         weave(2)
         quant(1)
-        add_skip(nc.vector, last, chunks[3])
-        finish(0)
-        weave(3)
-        add_skip(nc.vector, last, chunks[4])
-        quant(2)
-        weave(4)
         finish(1)
-        quant(3)
-        quant(4)
+        add_skip(nc.vector, last, chunks[3])
+        weave(3)
+        quant(2)
         finish(2)
+        add_skip(nc.vector, last, chunks[4])
+        add_skip(nc.vector, last, chunks[5])
+        weave(4)
+        weave(5)
+        quant(3)
         finish(3)
+        quant(4)
         finish(4)
+        quant(5)
+        finish(5)

@@ -1,7 +1,6 @@
 from contextlib import ExitStack
 
 import concourse.mybir as mybir
-from concourse.masks import make_identity
 
 K, T, S, H, N, U = 512, 2048, 512, 512, 256, 1024
 FLOPS = 2 * K * H * S + 2 * H * N * U
@@ -20,6 +19,7 @@ ADD = mybir.AluOpType.add
 P = 128
 PACK = 4
 ORDER = (3, 0, 1, 2)
+GATE = 768
 CHUNK = 256
 
 
@@ -38,7 +38,7 @@ def tile_picked_unet_relu_e_kernel(tc, xT, w1, w2_words, w2_scales, skip, offs, 
         x_plane = [keep.tile([P, T], F32, name="x_plane%d" % j) for j in range(PACK)]
         w_raw = [keep.tile([P, 2, H], F32, name="w_raw%d" % u) for u in range(2)]
         first, second, third, last = ORDER
-        parts = {first: (0, U), second: (0, 640, U), third: (0, U), last: (0, U)}
+        parts = {first: (0, U), second: (0, GATE, U), third: (0, U), last: (0, U)}
         s_part = {(t, lo): keep.tile([P, hi - lo], F32, name="s_part", tag="s_part%d_%d" % (t, lo))
                   for t in ORDER for lo, hi in zip(parts[t], parts[t][1:])}
         w2_codes = keep.tile([P, 2 * N], U8, name="w2_codes", align_bytes=64)
@@ -66,28 +66,48 @@ def tile_picked_unet_relu_e_kernel(tc, xT, w1, w2_words, w2_scales, skip, offs, 
             nc.vector.memset(window[t][:], 0.0)
 
         x_bf = keep.tile([P, S, PACK], BF16, name="x_bf", align_bytes=64)
-        for j in range(PACK):
-            nc.vector.tensor_copy(x_bf[:, :, j], x_plane[j][:].indirect(offs_t[:]))
         x_codes = keep.tile([P, S], U32, name="x_codes", align_bytes=64)
         x_exp = keep.tile([P, S], U8, name="x_exp", align_bytes=64)
-        nc.vector.quantize_mx(out=x_codes[:].bitcast(FP8X4), scales=x_exp[:], in_=x_bf[:].rearrange("p n j -> p (n j)"))
+        halves = (slice(0, S // 2), slice(S // 2, S))
+        for j in range(PACK - 1):
+            nc.vector.tensor_copy(x_bf[:, :, j], x_plane[j][:].indirect(offs_t[:]))
+        for half in halves:
+            nc.vector.tensor_copy(x_bf[:, half, PACK - 1], x_plane[PACK - 1][:].indirect(offs_t[:, half.start // 16 : half.stop // 16]))
+        for half in halves:
+            nc.vector.quantize_mx(out=x_codes[:, half].bitcast(FP8X4), scales=x_exp[:, half],
+                                  in_=x_bf[:, half].rearrange("p n j -> p (n j)"))
 
-        groups = ((3, 4), (0, 1), (1, 3))
+        groups = ((second, second + 1), (first, first + 1), (third, last + 1))
         w_codes, w_exp = {}, {}
-        w_bf = keep.tile([P, PACK, P, PACK], BF16, name="w_bf", align_bytes=64)
-        w_dst = w_bf[:].rearrange("p t m (u e) -> p u m e t", u=2)
         w_src = [w_raw[u][:].rearrange("p e (m t) -> p m e t", t=PACK) for u in range(2)]
-        nc.scalar.activation(w_dst[:, 0], w_src[0], ACT.Copy)
-        for lo, hi in groups[:2]:
-            nc.vector.tensor_copy(w_dst[:, 1, :, :, lo:hi], w_src[1][:, :, :, lo:hi])
-        nc.scalar.activation(w_dst[:, 1, :, :, 1:3], w_src[1][:, :, :, 1:3], ACT.Copy)
-        for g, (lo, hi) in enumerate(groups):
+        w_bf = [keep.tile([P, hi - lo, P, PACK], BF16, name="w_bf%d" % lo, align_bytes=64) for lo, hi in groups]
+
+        def deal(engine, g, u):
+            lo, hi = groups[g]
+            dst = w_bf[g][:].rearrange("p t m (u e) -> p u m e t", u=2)[:, u]
+            if engine is nc.scalar:
+                nc.scalar.activation(dst, w_src[u][:, :, :, lo:hi], ACT.Copy)
+            else:
+                engine.tensor_copy(dst, w_src[u][:, :, :, lo:hi])
+
+        def quant_w(g):
+            lo, hi = groups[g]
             codes = keep.tile([P, (hi - lo) * P], U32, name="w_codes%d" % lo, align_bytes=64)
             exps = keep.tile([P, (hi - lo) * P], U8, name="w_exp%d" % lo, align_bytes=64)
-            nc.vector.quantize_mx(out=codes[:].bitcast(FP8X4), scales=exps[:], in_=w_bf[:, lo:hi].rearrange("p t m j -> p (t m j)"))
+            nc.vector.quantize_mx(out=codes[:].bitcast(FP8X4), scales=exps[:], in_=w_bf[g][:].rearrange("p t m j -> p (t m j)"))
             for t in range(lo, hi):
                 w_codes[t] = codes[:, (t - lo) * P : (t - lo + 1) * P]
                 w_exp[t] = exps[:, (t - lo) * P : (t - lo + 1) * P]
+
+        deal(nc.scalar, 0, 0)
+        deal(nc.scalar, 1, 0)
+        deal(nc.vector, 0, 1)
+        deal(nc.scalar, 1, 1)
+        deal(nc.scalar, 2, 0)
+        quant_w(0)
+        deal(nc.vector, 2, 1)
+        quant_w(1)
+        quant_w(2)
 
         def hidden(t, edges, tag):
             lo, hi = edges[0], edges[-1]
@@ -108,24 +128,17 @@ def tile_picked_unet_relu_e_kernel(tc, xT, w1, w2_words, w2_scales, skip, offs, 
             engine.tensor_tensor(pair_vals[:, t // 2, cols, t % 2], window[t][:, cols],
                                  s_part[t, lo][:, cols.start - lo : cols.stop - lo], ADD)
 
-        hidden(first, (0, 128), "h_head")
-        hidden(first, (128, 256, 512), "h_first")
+        hidden(second, (0, 128), "h_head")
+        hidden(first, (0, S), "h_first")
+        hidden(second, (128, 256, 512), "h_second")
         add_skip(nc.gpsimd, first, slice(0, U))
-        hidden(second, (0, S), "h_second")
-        add_skip(nc.gpsimd, second, slice(0, 640))
-        add_skip(nc.gpsimd, second, slice(640, U))
+        add_skip(nc.gpsimd, second, slice(0, GATE))
+        add_skip(nc.gpsimd, second, slice(GATE, U))
         hidden(third, (0, S), "h_third")
         for lo, hi in ((0, 128), (128, U)):
             add_skip(nc.gpsimd, third, slice(lo, hi))
         hidden(last, (0, S), "s_part%d_0" % second)
 
-        ident = keep.tile([P, P], F32, name="ident")
-        make_identity(nc, ident[:])
-        warm = psum.tile([P, S], F32, name="acc", tag="acc")
-        nc.tensor.transpose(warm[:, :P], window[last][:, :P], ident[:])
-        for t in (first, second):
-            nc.tensor.matmul_mx(out=warm[:], lhsT=w_codes[t].bitcast(FP8X4), lhsT_scale=w_exp[t],
-                                rhs=x_codes[:].bitcast(FP8X4), rhs_scale=x_exp[:], start=True, stop=True)
         out_rows = out.rearrange("(g p) v -> p g v", p=P)
         edges = (0, 128, 256, 512, 768, 896, 1024)
         chunks = [slice(lo, hi) for lo, hi in zip(edges, edges[1:])]

@@ -1,6 +1,7 @@
 from contextlib import ExitStack
 
 import concourse.mybir as mybir
+from concourse.masks import make_identity
 
 K, T, S, H, N, U = 512, 2048, 512, 512, 256, 1024
 FLOPS = 2 * K * H * S + 2 * H * N * U
@@ -19,7 +20,8 @@ ADD = mybir.AluOpType.add
 P = 128
 PACK = 4
 ORDER = (3, 0, 1, 2)
-GATE = 768
+GATE = 640
+SHARE = 768
 CHUNK = 256
 
 
@@ -27,7 +29,8 @@ def tile_picked_unet_relu_e_kernel(tc, xT, w1, w2_words, w2_scales, skip, offs, 
     nc = tc.nc
     with ExitStack() as ctx:
         keep = ctx.enter_context(tc.tile_pool(name="keep", bufs=1))
-        psum = ctx.enter_context(tc.psum_pool(name="psum", bufs=8))
+        psum = ctx.enter_context(tc.psum_pool(name="psum", bufs=6))
+        held = ctx.enter_context(tc.psum_pool(name="held", bufs=1))
 
         offs_t = keep.tile([P, S // 16], U16, name="offs_t")
         cell_t = keep.tile([P, S // 16], U16, name="cell_t")
@@ -137,21 +140,38 @@ def tile_picked_unet_relu_e_kernel(tc, xT, w1, w2_words, w2_scales, skip, offs, 
         hidden(third, (0, S), "h_third")
         for lo, hi in ((0, 128), (128, U)):
             add_skip(nc.gpsimd, third, slice(lo, hi))
+
+        ident = keep.tile([P, P], F32, name="ident")
+        make_identity(nc, ident[:])
+        s_bank = {}
+        for lo, hi in ((0, 2 * P), (2 * P, SHARE)):
+            turned_ps = psum.tile([P, hi - lo], F32, name="acc", tag="acc")
+            turned = keep.tile([P, hi - lo], F32, name="turned%d" % lo)
+            s_bank[lo] = held.tile([P, hi - lo], F32, name="s_bank", tag="s_bank%d" % lo)
+            for at in range(0, hi - lo, P):
+                nc.tensor.transpose(turned_ps[:, at : at + P], s_part[last, 0][:, lo + at : lo + at + P], ident[:])
+            nc.scalar.copy(turned[:], turned_ps[:])
+            for at in range(0, hi - lo, P):
+                nc.tensor.transpose(s_bank[lo][:, at : at + P], turned[:, at : at + P], ident[:])
+
         hidden(last, (0, S), "s_part%d_0" % second)
 
         out_rows = out.rearrange("(g p) v -> p g v", p=P)
         edges = (0, 128, 256, 512, 768, 896, 1024)
         chunks = [slice(lo, hi) for lo, hi in zip(edges, edges[1:])]
-        z_bf = {}
+        z_bf, z_q = {}, {}
 
-        def weave(c):
+        def add_last(cols):
+            lo = 0 if cols.start < 2 * P else 2 * P
+            nc.vector.tensor_tensor(pair_vals[:, last // 2, cols, last % 2], window[last][:, cols],
+                                    s_bank[lo][:, cols.start - lo : cols.stop - lo], ADD)
+
+        def weave(c, engine):
             z_bf[c] = keep.tile([P, chunks[c].stop - chunks[c].start, 2], F32, name="z_bf", tag="z_bf%d" % c, align_bytes=64)
-            if c < 4:
+            if engine == "scalar":
                 nc.scalar.copy(z_bf[c][:], pair_words[:, chunks[c], :])
             else:
                 nc.vector.tensor_copy(z_bf[c][:], pair_words[:, chunks[c], :])
-
-        z_q = {}
 
         def quant(c):
             width = chunks[c].stop - chunks[c].start
@@ -161,11 +181,10 @@ def tile_picked_unet_relu_e_kernel(tc, xT, w1, w2_words, w2_scales, skip, offs, 
                                   in_=z_bf[c][:].rearrange("p v u -> p (v u)").bitcast(BF16))
             z_q[c] = codes, exps
 
-        def finish(c):
+        def finish(c, on_vector, joint):
             width = chunks[c].stop - chunks[c].start
             codes, exps = z_q[c]
             res = keep.tile([P, 2, width], F32, name="res%d" % c)
-            joint = width == P
             whole = psum.tile([P, 2, width], F32, name="acc", tag="acc") if joint else None
             for g in range(2):
                 acc = whole[:, g, :] if joint else psum.tile([P, width], F32, name="acc", tag="acc")[:]
@@ -173,41 +192,47 @@ def tile_picked_unet_relu_e_kernel(tc, xT, w1, w2_words, w2_scales, skip, offs, 
                                     lhsT_scale=w2_exp[:, P * g : P * (g + 1)],
                                     rhs=codes[:].bitcast(FP8X4), rhs_scale=exps[:], start=True, stop=True)
                 if not joint:
-                    if (c, g) in ((3, 1), (5, 0)):
+                    if g in on_vector:
                         nc.vector.tensor_copy(res[:, g, :], acc)
                     else:
                         nc.scalar.copy(res[:, g, :], acc)
-                    if c in (2,):
+                    if width > P:
                         nc.sync.dma_start(out_rows[:, g, chunks[c]], res[:, g, :])
             if joint:
-                if (c, 0) in ((3, 1), (5, 0)):
+                if on_vector:
                     nc.vector.tensor_copy(res[:], whole[:])
                 else:
                     nc.scalar.copy(res[:], whole[:])
-            if c not in (2,):
+            if width == P:
                 nc.sync.dma_start(out_rows[:, :, chunks[c]], res[:])
 
-        add_skip(nc.vector, last, chunks[0])
-        weave(0)
-        add_skip(nc.vector, last, chunks[1])
-        weave(1)
+        def warm_up():
+            warm = held.tile([P, S], F32, name="s_bank", tag="s_bank0")
+            for t in (first, second):
+                nc.tensor.matmul_mx(out=warm[:], lhsT=w_codes[t].bitcast(FP8X4), lhsT_scale=w_exp[t],
+                                    rhs=x_codes[:].bitcast(FP8X4), rhs_scale=x_exp[:], start=True, stop=True)
+
+        add_last(chunks[0])
+        add_skip(nc.gpsimd, last, slice(SHARE, U))
+        weave(0, "scalar")
+        add_last(chunks[1])
+        warm_up()
+        weave(1, "scalar")
         quant(0)
-        finish(0)
-        add_skip(nc.vector, last, chunks[2])
-        weave(2)
+        finish(0, (), True)
+        add_last(chunks[2])
+        weave(2, "scalar")
         quant(1)
-        finish(1)
-        add_skip(nc.vector, last, chunks[3])
-        weave(3)
+        finish(1, (), True)
+        add_last(chunks[3])
+        weave(3, "scalar")
         quant(2)
-        finish(2)
-        add_skip(nc.vector, last, chunks[4])
-        add_skip(nc.vector, last, chunks[5])
-        weave(4)
-        weave(5)
+        finish(2, (), False)
+        weave(4, "vector")
+        weave(5, "vector")
         quant(3)
-        finish(3)
+        finish(3, (1,), False)
         quant(4)
-        finish(4)
+        finish(4, (), True)
         quant(5)
-        finish(5)
+        finish(5, (0,), True)

@@ -21,7 +21,7 @@ P = 128
 PACK = 4
 ORDER = (3, 0, 1, 2)
 GATE = 640
-SHARE = 768
+SHARE = 384
 CHUNK = 256
 
 
@@ -55,7 +55,7 @@ def tile_picked_unet_relu_e_kernel(tc, xT, w1, w2_words, w2_scales, skip, offs, 
         for u in range(2):
             nc.sync.dma_start(w_raw[u][:], w_rows[u])
         nc.sync.dma_start(cell_t[:], cell)
-        for t in ORDER:
+        for t in (last, first, second, third):
             for lo, hi in zip(parts[t], parts[t][1:]):
                 nc.sync.dma_start(s_part[t, lo][:], s_rows[t][:, lo:hi])
         nc.sync.dma_start(w2_codes[:], w2_words[0])
@@ -123,13 +123,21 @@ def tile_picked_unet_relu_e_kernel(tc, xT, w1, w2_words, w2_scales, skip, offs, 
             nc.vector.tensor_copy(window[t][:].indirect(cell_t[:, lo // 16 : hi // 16]), h[:])
 
         pairs = keep.tile([P, PACK * U], BF16, name="pairs")
-        pair_vals = pairs[:].rearrange("p (u v e) -> p u v e", u=2, e=2)
-        pair_words = pairs[:].bitcast(F32).rearrange("p (u v) -> p v u", u=2)
+        pair_vals = pairs[:].rearrange("p (b u v e) -> p b u v e", u=2, v=P, e=2)
+        pair_words = pairs[:].bitcast(F32).rearrange("p (b u v) -> p b v u", u=2, v=P)
+
+        def blocks(ap):
+            return ap.rearrange("p (b v) -> p b v", v=P)
+
+        def pair_slots(t, cols):
+            return pair_vals[:, cols.start // P : cols.stop // P, t // 2, :, t % 2]
+
+        nc.vector.memset(pair_vals[:, : SHARE // P, last // 2], 0.0)
 
         def add_skip(engine, t, cols):
             lo = max(edge for edge in parts[t] if edge <= cols.start)
-            engine.tensor_tensor(pair_vals[:, t // 2, cols, t % 2], window[t][:, cols],
-                                 s_part[t, lo][:, cols.start - lo : cols.stop - lo], ADD)
+            engine.tensor_tensor(pair_slots(t, cols), blocks(window[t][:, cols]),
+                                 blocks(s_part[t, lo][:, cols.start - lo : cols.stop - lo]), ADD)
 
         hidden(second, (0, 128), "h_head")
         hidden(first, (0, S), "h_first")
@@ -138,13 +146,14 @@ def tile_picked_unet_relu_e_kernel(tc, xT, w1, w2_words, w2_scales, skip, offs, 
         add_skip(nc.gpsimd, second, slice(0, GATE))
         add_skip(nc.gpsimd, second, slice(GATE, U))
         hidden(third, (0, S), "h_third")
-        for lo, hi in ((0, 128), (128, U)):
+        for lo, hi in ((0, SHARE), (SHARE, U)):
             add_skip(nc.gpsimd, third, slice(lo, hi))
+        hidden(last, (0, S), "s_part%d_0" % second)
 
         ident = keep.tile([P, P], F32, name="ident")
         make_identity(nc, ident[:])
         s_bank = {}
-        for lo, hi in ((0, 2 * P), (2 * P, SHARE)):
+        for lo, hi in ((SHARE, SHARE + P), (SHARE + P, U)):
             turned_ps = psum.tile([P, hi - lo], F32, name="acc", tag="acc")
             turned = keep.tile([P, hi - lo], F32, name="turned%d" % lo)
             s_bank[lo] = held.tile([P, hi - lo], F32, name="s_bank", tag="s_bank%d" % lo)
@@ -154,24 +163,29 @@ def tile_picked_unet_relu_e_kernel(tc, xT, w1, w2_words, w2_scales, skip, offs, 
             for at in range(0, hi - lo, P):
                 nc.tensor.transpose(s_bank[lo][:, at : at + P], turned[:, at : at + P], ident[:])
 
-        hidden(last, (0, S), "s_part%d_0" % second)
 
         out_rows = out.rearrange("(g p) v -> p g v", p=P)
-        edges = (0, 128, 256, 512, 768, 896, 1024)
+        edges = (0, 256, 384, 512, 768, 1024)
         chunks = [slice(lo, hi) for lo, hi in zip(edges, edges[1:])]
         z_bf, z_q = {}, {}
 
         def add_last(cols):
-            lo = 0 if cols.start < 2 * P else 2 * P
-            nc.vector.tensor_tensor(pair_vals[:, last // 2, cols, last % 2], window[last][:, cols],
-                                    s_bank[lo][:, cols.start - lo : cols.stop - lo], ADD)
+            lo = SHARE if cols.start < SHARE + P else SHARE + P
+            nc.vector.tensor_tensor(pair_slots(last, cols), blocks(window[last][:, cols]),
+                                    blocks(s_bank[lo][:, cols.start - lo : cols.stop - lo]), ADD)
 
         def weave(c, engine):
             z_bf[c] = keep.tile([P, chunks[c].stop - chunks[c].start, 2], F32, name="z_bf", tag="z_bf%d" % c, align_bytes=64)
             if engine == "scalar":
-                nc.scalar.copy(z_bf[c][:], pair_words[:, chunks[c], :])
+                nc.scalar.copy(z_bf[c][:].rearrange("p (b v) u -> p b v u", v=P), pair_words[:, chunks[c].start // P : chunks[c].stop // P])
             else:
-                nc.vector.tensor_copy(z_bf[c][:], pair_words[:, chunks[c], :])
+                nc.vector.tensor_copy(z_bf[c][:].rearrange("p (b v) u -> p b v u", v=P), pair_words[:, chunks[c].start // P : chunks[c].stop // P])
+
+        def weave_ahead():
+            ahead = keep.tile([P, SHARE, 2], F32, name="ahead", align_bytes=64)
+            nc.scalar.copy(ahead[:].rearrange("p (b v) u -> p b v u", v=P), pair_words[:, : SHARE // P])
+            z_bf[0], z_bf[1] = ahead[:, chunks[0]], ahead[:, chunks[1]]
+            return ahead[:].rearrange("p v u -> p (v u)").bitcast(BF16).rearrange("p (v t) -> p v t", t=PACK)
 
         def quant(c):
             width = chunks[c].stop - chunks[c].start
@@ -207,32 +221,27 @@ def tile_picked_unet_relu_e_kernel(tc, xT, w1, w2_words, w2_scales, skip, offs, 
                 nc.sync.dma_start(out_rows[:, :, chunks[c]], res[:])
 
         def warm_up():
-            warm = held.tile([P, S], F32, name="s_bank", tag="s_bank0")
+            warm = held.tile([P, S], F32, name="s_bank", tag="s_bank%d" % SHARE)
             for t in (first, second):
                 nc.tensor.matmul_mx(out=warm[:], lhsT=w_codes[t].bitcast(FP8X4), lhsT_scale=w_exp[t],
                                     rhs=x_codes[:].bitcast(FP8X4), rhs_scale=x_exp[:], start=True, stop=True)
 
-        add_last(chunks[0])
-        add_skip(nc.gpsimd, last, slice(SHARE, U))
-        weave(0, "scalar")
-        add_last(chunks[1])
-        warm_up()
-        weave(1, "scalar")
-        quant(0)
-        finish(0, (), True)
+        ahead_vals = weave_ahead()
         add_last(chunks[2])
+        nc.gpsimd.tensor_tensor(ahead_vals[:, :, last], window[last][:, :SHARE], s_part[last, 0][:, :SHARE], ADD)
+        warm_up()
         weave(2, "scalar")
-        quant(1)
-        finish(1, (), True)
         add_last(chunks[3])
         weave(3, "scalar")
+        add_last(chunks[4])
+        weave(4, "scalar")
         quant(2)
-        finish(2, (), False)
-        weave(4, "vector")
-        weave(5, "vector")
+        quant(0)
+        quant(1)
+        finish(2, (), True)
         quant(3)
-        finish(3, (1,), False)
+        finish(0, (), False)
         quant(4)
-        finish(4, (), True)
-        quant(5)
-        finish(5, (0,), True)
+        finish(1, (), True)
+        finish(3, (), False)
+        finish(4, (0,), False)

@@ -19,10 +19,13 @@ ADD = mybir.AluOpType.add
 
 P = 128
 PACK = 4
-ORDER = (3, 0, 1, 2)
+PER_COLUMN = 16
+
+FIRST, SECOND, THIRD, LAST = 3, 0, 1, 2
+HEAD = 128
 GATE = 640
-SHARE = 384
-CHUNK = 256
+AHEAD = 384
+EDGES = (0, 256, AHEAD, 512, 768, U)
 
 
 def tile_picked_unet_relu_e_kernel(tc, xT, w1, w2_words, w2_scales, skip, offs, cell, out):
@@ -32,30 +35,28 @@ def tile_picked_unet_relu_e_kernel(tc, xT, w1, w2_words, w2_scales, skip, offs, 
         psum = ctx.enter_context(tc.psum_pool(name="psum", bufs=6))
         held = ctx.enter_context(tc.psum_pool(name="held", bufs=1))
 
-        offs_t = keep.tile([P, S // 16], U16, name="offs_t")
-        cell_t = keep.tile([P, S // 16], U16, name="cell_t")
+        offs_t = keep.tile([P, S // PER_COLUMN], U16, name="offs_t")
+        cell_t = keep.tile([P, S // PER_COLUMN], U16, name="cell_t")
         x_rows = xT.rearrange("(p j) c -> j p c", j=PACK)
         w_rows = w1.rearrange("(p u e) c -> u p e c", u=2, e=2)
         s_rows = skip.rearrange("(p t) c -> t p c", t=PACK)
 
         x_plane = [keep.tile([P, T], F32, name="x_plane%d" % j) for j in range(PACK)]
         w_raw = [keep.tile([P, 2, H], F32, name="w_raw%d" % u) for u in range(2)]
-        first, second, third, last = ORDER
-        parts = {first: (0, U), second: (0, GATE, U), third: (0, U), last: (0, U)}
+        parts = {FIRST: (0, U), SECOND: (0, GATE, U), THIRD: (0, U), LAST: (0, U)}
         s_part = {(t, lo): keep.tile([P, hi - lo], F32, name="s_part", tag="s_part%d_%d" % (t, lo))
-                  for t in ORDER for lo, hi in zip(parts[t], parts[t][1:])}
+                  for t in parts for lo, hi in zip(parts[t], parts[t][1:])}
         w2_codes = keep.tile([P, 2 * N], U8, name="w2_codes", align_bytes=64)
         w2_exp = keep.tile([P, N], U8, name="w2_exp", align_bytes=64)
 
         nc.sync.dma_start(x_plane[0][:], x_rows[0])
         nc.sync.dma_start(offs_t[:], offs)
-        nc.sync.dma_start(x_plane[1][:], x_rows[1])
-        nc.sync.dma_start(x_plane[2][:], x_rows[2])
-        nc.sync.dma_start(x_plane[3][:], x_rows[3])
+        for j in range(1, PACK):
+            nc.sync.dma_start(x_plane[j][:], x_rows[j])
         for u in range(2):
             nc.sync.dma_start(w_raw[u][:], w_rows[u])
         nc.sync.dma_start(cell_t[:], cell)
-        for t in (last, first, second, third):
+        for t in (LAST, FIRST, SECOND, THIRD):
             for lo, hi in zip(parts[t], parts[t][1:]):
                 nc.sync.dma_start(s_part[t, lo][:], s_rows[t][:, lo:hi])
         nc.sync.dma_start(w2_codes[:], w2_words[0])
@@ -64,36 +65,33 @@ def tile_picked_unet_relu_e_kernel(tc, xT, w1, w2_words, w2_scales, skip, offs, 
             nc.sync.dma_start(w2_exp[32 * q : 32 * q + 4, :].bitcast(I32), w2_scales[0, 4 * q : 4 * q + 4, :].bitcast(I32))
 
         window = {}
-        for t in ORDER:
+        for t in parts:
             window[t] = keep.tile([P, U], F32, name="window", tag="window%d" % t)
             nc.vector.memset(window[t][:], 0.0)
 
         x_bf = keep.tile([P, S, PACK], BF16, name="x_bf", align_bytes=64)
         x_codes = keep.tile([P, S], U32, name="x_codes", align_bytes=64)
         x_exp = keep.tile([P, S], U8, name="x_exp", align_bytes=64)
-        halves = (slice(0, S // 2), slice(S // 2, S))
         for j in range(PACK - 1):
             nc.vector.tensor_copy(x_bf[:, :, j], x_plane[j][:].indirect(offs_t[:]))
+        halves = (slice(0, S // 2), slice(S // 2, S))
         for half in halves:
-            nc.vector.tensor_copy(x_bf[:, half, PACK - 1], x_plane[PACK - 1][:].indirect(offs_t[:, half.start // 16 : half.stop // 16]))
+            nc.vector.tensor_copy(x_bf[:, half, PACK - 1],
+                                  x_plane[PACK - 1][:].indirect(offs_t[:, half.start // PER_COLUMN : half.stop // PER_COLUMN]))
         for half in halves:
             nc.vector.quantize_mx(out=x_codes[:, half].bitcast(FP8X4), scales=x_exp[:, half],
                                   in_=x_bf[:, half].rearrange("p n j -> p (n j)"))
 
-        groups = ((second, second + 1), (first, first + 1), (third, last + 1))
-        w_codes, w_exp = {}, {}
+        groups = ((SECOND, SECOND + 1), (FIRST, FIRST + 1), (THIRD, LAST + 1))
         w_src = [w_raw[u][:].rearrange("p e (m t) -> p m e t", t=PACK) for u in range(2)]
         w_bf = [keep.tile([P, hi - lo, P, PACK], BF16, name="w_bf%d" % lo, align_bytes=64) for lo, hi in groups]
+        w_codes, w_exp = {}, {}
 
-        def deal(engine, g, u):
+        def dealt(g, u):
             lo, hi = groups[g]
-            dst = w_bf[g][:].rearrange("p t m (u e) -> p u m e t", u=2)[:, u]
-            if engine is nc.scalar:
-                nc.scalar.activation(dst, w_src[u][:, :, :, lo:hi], ACT.Copy)
-            else:
-                engine.tensor_copy(dst, w_src[u][:, :, :, lo:hi])
+            return w_bf[g][:].rearrange("p t m (u e) -> p u m e t", u=2)[:, u], w_src[u][:, :, :, lo:hi]
 
-        def quant_w(g):
+        def quantise_w(g):
             lo, hi = groups[g]
             codes = keep.tile([P, (hi - lo) * P], U32, name="w_codes%d" % lo, align_bytes=64)
             exps = keep.tile([P, (hi - lo) * P], U8, name="w_exp%d" % lo, align_bytes=64)
@@ -102,25 +100,28 @@ def tile_picked_unet_relu_e_kernel(tc, xT, w1, w2_words, w2_scales, skip, offs, 
                 w_codes[t] = codes[:, (t - lo) * P : (t - lo + 1) * P]
                 w_exp[t] = exps[:, (t - lo) * P : (t - lo + 1) * P]
 
-        deal(nc.scalar, 0, 0)
-        deal(nc.scalar, 1, 0)
-        deal(nc.vector, 0, 1)
-        deal(nc.scalar, 1, 1)
-        deal(nc.scalar, 2, 0)
-        quant_w(0)
-        deal(nc.vector, 2, 1)
-        quant_w(1)
-        quant_w(2)
+        nc.scalar.activation(*dealt(0, 0), ACT.Copy)
+        nc.scalar.activation(*dealt(1, 0), ACT.Copy)
+        nc.vector.tensor_copy(*dealt(0, 1))
+        nc.scalar.activation(*dealt(1, 1), ACT.Copy)
+        nc.scalar.activation(*dealt(2, 0), ACT.Copy)
+        quantise_w(0)
+        nc.vector.tensor_copy(*dealt(2, 1))
+        quantise_w(1)
+        quantise_w(2)
 
-        def hidden(t, edges, tag):
-            lo, hi = edges[0], edges[-1]
+        def product(acc, t, entries):
+            nc.tensor.matmul_mx(out=acc, lhsT=w_codes[t].bitcast(FP8X4), lhsT_scale=w_exp[t],
+                                rhs=x_codes[:, entries].bitcast(FP8X4), rhs_scale=x_exp[:, entries], start=True, stop=True)
+
+        def hidden(t, cuts, tag):
+            lo, hi = cuts[0], cuts[-1]
             acc = psum.tile([P, hi - lo], F32, name="acc", tag="acc")
-            for a, b in zip(edges, edges[1:]):
-                nc.tensor.matmul_mx(out=acc[:, a - lo : b - lo], lhsT=w_codes[t].bitcast(FP8X4), lhsT_scale=w_exp[t],
-                                    rhs=x_codes[:, a:b].bitcast(FP8X4), rhs_scale=x_exp[:, a:b], start=True, stop=True)
+            for a, b in zip(cuts, cuts[1:]):
+                product(acc[:, a - lo : b - lo], t, slice(a, b))
             h = keep.tile([P, hi - lo], F32, name="h", tag=tag)
             nc.scalar.activation(h[:], acc[:], ACT.Relu)
-            nc.vector.tensor_copy(window[t][:].indirect(cell_t[:, lo // 16 : hi // 16]), h[:])
+            nc.vector.tensor_copy(window[t][:].indirect(cell_t[:, lo // PER_COLUMN : hi // PER_COLUMN]), h[:])
 
         pairs = keep.tile([P, PACK * U], BF16, name="pairs")
         pair_vals = pairs[:].rearrange("p (b u v e) -> p b u v e", u=2, v=P, e=2)
@@ -129,119 +130,106 @@ def tile_picked_unet_relu_e_kernel(tc, xT, w1, w2_words, w2_scales, skip, offs, 
         def blocks(ap):
             return ap.rearrange("p (b v) -> p b v", v=P)
 
-        def pair_slots(t, cols):
-            return pair_vals[:, cols.start // P : cols.stop // P, t // 2, :, t % 2]
+        def add_into_pairs(engine, t, cells, skip_ap):
+            engine.tensor_tensor(pair_vals[:, cells.start // P : cells.stop // P, t // 2, :, t % 2],
+                                 blocks(window[t][:, cells]), blocks(skip_ap), ADD)
 
-        nc.vector.memset(pair_vals[:, : SHARE // P, last // 2], 0.0)
+        def add_skip(t, lo, hi):
+            base = max(edge for edge in parts[t] if edge <= lo)
+            add_into_pairs(nc.gpsimd, t, slice(lo, hi), s_part[t, base][:, lo - base : hi - base])
 
-        def add_skip(engine, t, cols):
-            lo = max(edge for edge in parts[t] if edge <= cols.start)
-            engine.tensor_tensor(pair_slots(t, cols), blocks(window[t][:, cols]),
-                                 blocks(s_part[t, lo][:, cols.start - lo : cols.stop - lo]), ADD)
+        nc.vector.memset(pair_vals[:, : AHEAD // P, LAST // 2], 0.0)
 
-        hidden(second, (0, 128), "h_head")
-        hidden(first, (0, S), "h_first")
-        hidden(second, (128, 256, 512), "h_second")
-        add_skip(nc.gpsimd, first, slice(0, U))
-        add_skip(nc.gpsimd, second, slice(0, GATE))
-        add_skip(nc.gpsimd, second, slice(GATE, U))
-        hidden(third, (0, S), "h_third")
-        for lo, hi in ((0, SHARE), (SHARE, U)):
-            add_skip(nc.gpsimd, third, slice(lo, hi))
-        hidden(last, (0, S), "s_part%d_0" % second)
+        hidden(SECOND, (0, HEAD), "h_head")
+        h_first = keep.tile([P, S], F32, name="h_first")
+        for half in halves:
+            acc = psum.tile([P, S // 2], F32, name="acc", tag="acc")
+            product(acc[:], FIRST, half)
+            nc.scalar.activation(h_first[:, half], acc[:], ACT.Relu)
+        nc.vector.tensor_copy(window[FIRST][:].indirect(cell_t[:]), h_first[:])
+        hidden(SECOND, (HEAD, S // 2, S), "h_second")
+        add_skip(FIRST, 0, U)
+        add_skip(SECOND, 0, GATE)
+        add_skip(SECOND, GATE, U)
+        hidden(THIRD, (0, S), "h_third")
+        add_skip(THIRD, 0, AHEAD)
+        add_skip(THIRD, AHEAD, U)
+        hidden(LAST, (0, S), "s_part%d_0" % SECOND)
 
         ident = keep.tile([P, P], F32, name="ident")
         make_identity(nc, ident[:])
         s_bank = {}
-        for lo, hi in ((SHARE, SHARE + P), (SHARE + P, U)):
+        for lo, hi in ((AHEAD, AHEAD + P), (AHEAD + P, U)):
             turned_ps = psum.tile([P, hi - lo], F32, name="acc", tag="acc")
             turned = keep.tile([P, hi - lo], F32, name="turned%d" % lo)
             s_bank[lo] = held.tile([P, hi - lo], F32, name="s_bank", tag="s_bank%d" % lo)
             for at in range(0, hi - lo, P):
-                nc.tensor.transpose(turned_ps[:, at : at + P], s_part[last, 0][:, lo + at : lo + at + P], ident[:])
+                nc.tensor.transpose(turned_ps[:, at : at + P], s_part[LAST, 0][:, lo + at : lo + at + P], ident[:])
             nc.scalar.copy(turned[:], turned_ps[:])
             for at in range(0, hi - lo, P):
                 nc.tensor.transpose(s_bank[lo][:, at : at + P], turned[:, at : at + P], ident[:])
 
-
         out_rows = out.rearrange("(g p) v -> p g v", p=P)
-        edges = (0, 256, 384, 512, 768, 1024)
-        chunks = [slice(lo, hi) for lo, hi in zip(edges, edges[1:])]
-        z_bf, z_q = {}, {}
+        chunks = [slice(lo, hi) for lo, hi in zip(EDGES, EDGES[1:])]
+        z_bf, z_mx = {}, {}
 
-        def add_last(cols):
-            lo = SHARE if cols.start < SHARE + P else SHARE + P
-            nc.vector.tensor_tensor(pair_slots(last, cols), blocks(window[last][:, cols]),
-                                    blocks(s_bank[lo][:, cols.start - lo : cols.stop - lo]), ADD)
+        def weave(cells, name):
+            woven = keep.tile([P, cells.stop - cells.start, 2], F32, name=name, align_bytes=64)
+            nc.scalar.copy(woven[:].rearrange("p (b v) u -> p b v u", v=P), pair_words[:, cells.start // P : cells.stop // P])
+            return woven
 
-        def weave(c, engine):
-            z_bf[c] = keep.tile([P, chunks[c].stop - chunks[c].start, 2], F32, name="z_bf", tag="z_bf%d" % c, align_bytes=64)
-            if engine == "scalar":
-                nc.scalar.copy(z_bf[c][:].rearrange("p (b v) u -> p b v u", v=P), pair_words[:, chunks[c].start // P : chunks[c].stop // P])
-            else:
-                nc.vector.tensor_copy(z_bf[c][:].rearrange("p (b v) u -> p b v u", v=P), pair_words[:, chunks[c].start // P : chunks[c].stop // P])
+        def add_last(c):
+            base = max(edge for edge in s_bank if edge <= chunks[c].start)
+            add_into_pairs(nc.vector, LAST, chunks[c], s_bank[base][:, chunks[c].start - base : chunks[c].stop - base])
 
-        def weave_ahead():
-            ahead = keep.tile([P, SHARE, 2], F32, name="ahead", align_bytes=64)
-            nc.scalar.copy(ahead[:].rearrange("p (b v) u -> p b v u", v=P), pair_words[:, : SHARE // P])
-            z_bf[0], z_bf[1] = ahead[:, chunks[0]], ahead[:, chunks[1]]
-            return ahead[:].rearrange("p v u -> p (v u)").bitcast(BF16).rearrange("p (v t) -> p v t", t=PACK)
-
-        def quant(c):
+        def quantise_z(c):
             width = chunks[c].stop - chunks[c].start
             codes = keep.tile([P, width], U32, name="z_codes%d" % c, align_bytes=64)
             exps = keep.tile([P, width], U8, name="z_exp%d" % c, align_bytes=64)
             nc.vector.quantize_mx(out=codes[:].bitcast(FP8X4), scales=exps[:],
-                                  in_=z_bf[c][:].rearrange("p v u -> p (v u)").bitcast(BF16))
-            z_q[c] = codes, exps
+                                  in_=z_bf[c].rearrange("p v u -> p (v u)").bitcast(BF16))
+            z_mx[c] = codes, exps
 
-        def finish(c, on_vector, joint):
-            width = chunks[c].stop - chunks[c].start
-            codes, exps = z_q[c]
-            res = keep.tile([P, 2, width], F32, name="res%d" % c)
-            whole = psum.tile([P, 2, width], F32, name="acc", tag="acc") if joint else None
+        def second_product(acc, g, c):
+            codes, exps = z_mx[c]
+            nc.tensor.matmul_mx(out=acc, lhsT=w2_codes[:, 2 * P * g : 2 * P * (g + 1)].bitcast(FP4X4),
+                                lhsT_scale=w2_exp[:, P * g : P * (g + 1)],
+                                rhs=codes[:].bitcast(FP8X4), rhs_scale=exps[:], start=True, stop=True)
+
+        def finish_narrow(c):
+            res = keep.tile([P, 2, P], F32, name="res%d" % c)
+            acc = psum.tile([P, 2, P], F32, name="acc", tag="acc")
             for g in range(2):
-                acc = whole[:, g, :] if joint else psum.tile([P, width], F32, name="acc", tag="acc")[:]
-                nc.tensor.matmul_mx(out=acc, lhsT=w2_codes[:, 2 * P * g : 2 * P * (g + 1)].bitcast(FP4X4),
-                                    lhsT_scale=w2_exp[:, P * g : P * (g + 1)],
-                                    rhs=codes[:].bitcast(FP8X4), rhs_scale=exps[:], start=True, stop=True)
-                if not joint:
-                    if g in on_vector:
-                        nc.vector.tensor_copy(res[:, g, :], acc)
-                    else:
-                        nc.scalar.copy(res[:, g, :], acc)
-                    if width > P:
-                        nc.sync.dma_start(out_rows[:, g, chunks[c]], res[:, g, :])
-            if joint:
-                if on_vector:
-                    nc.vector.tensor_copy(res[:], whole[:])
-                else:
-                    nc.scalar.copy(res[:], whole[:])
-            if width == P:
-                nc.sync.dma_start(out_rows[:, :, chunks[c]], res[:])
+                second_product(acc[:, g, :], g, c)
+            nc.scalar.copy(res[:], acc[:])
+            nc.sync.dma_start(out_rows[:, :, chunks[c]], res[:])
 
-        def warm_up():
-            warm = held.tile([P, S], F32, name="s_bank", tag="s_bank%d" % SHARE)
-            for t in (first, second):
-                nc.tensor.matmul_mx(out=warm[:], lhsT=w_codes[t].bitcast(FP8X4), lhsT_scale=w_exp[t],
-                                    rhs=x_codes[:].bitcast(FP8X4), rhs_scale=x_exp[:], start=True, stop=True)
+        def finish_wide(c, copies):
+            res = keep.tile([P, 2, 2 * P], F32, name="res%d" % c)
+            for g in range(2):
+                acc = psum.tile([P, 2 * P], F32, name="acc", tag="acc")
+                second_product(acc[:], g, c)
+                copies[g](res[:, g, :], acc[:])
+                nc.sync.dma_start(out_rows[:, g, chunks[c]], res[:, g, :])
 
-        ahead_vals = weave_ahead()
-        add_last(chunks[2])
-        nc.gpsimd.tensor_tensor(ahead_vals[:, :, last], window[last][:, :SHARE], s_part[last, 0][:, :SHARE], ADD)
-        warm_up()
-        weave(2, "scalar")
-        add_last(chunks[3])
-        weave(3, "scalar")
-        add_last(chunks[4])
-        weave(4, "scalar")
-        quant(2)
-        quant(0)
-        quant(1)
-        finish(2, (), True)
-        quant(3)
-        finish(0, (), False)
-        quant(4)
-        finish(1, (), True)
-        finish(3, (), False)
-        finish(4, (0,), False)
+        ahead = weave(slice(0, AHEAD), "ahead")
+        z_bf[0], z_bf[1] = ahead[:, chunks[0]], ahead[:, chunks[1]]
+        ahead_vals = ahead[:].rearrange("p v u -> p (v u)").bitcast(BF16).rearrange("p (v t) -> p v t", t=PACK)
+        add_last(2)
+        nc.gpsimd.tensor_tensor(ahead_vals[:, :, LAST], window[LAST][:, :AHEAD], s_part[LAST, 0][:, :AHEAD], ADD)
+        z_bf[2] = weave(chunks[2], "z_bf2")[:]
+        for c in (3, 4):
+            add_last(c)
+            z_bf[c] = weave(chunks[c], "z_bf%d" % c)[:]
+
+        by_scalar = (nc.scalar.copy, nc.scalar.copy)
+        quantise_z(2)
+        quantise_z(0)
+        quantise_z(1)
+        finish_narrow(2)
+        quantise_z(3)
+        finish_wide(0, by_scalar)
+        quantise_z(4)
+        finish_narrow(1)
+        finish_wide(3, by_scalar)
+        finish_wide(4, (nc.vector.tensor_copy, nc.scalar.copy))

@@ -20,10 +20,12 @@ ADD = mybir.AluOpType.add
 P = 128
 PACK = 4
 PER_COLUMN = 16
+HALF = H // 2
+BANK = 512
 
-FIRST, SECOND, THIRD, LAST = 3, 0, 1, 2
+EVEN_LO, EVEN_HI, ODD, LAST = 0, 1, 2, 3
 HEAD = 128
-GATE = 640
+HEAD_WINDOW = 4
 AHEAD = 384
 EDGES = (0, 256, AHEAD, 512, 768, U)
 
@@ -32,20 +34,23 @@ def tile_picked_unet_relu_e_kernel(tc, xT, w1, w2_words, w2_scales, skip, offs, 
     nc = tc.nc
     with ExitStack() as ctx:
         keep = ctx.enter_context(tc.tile_pool(name="keep", bufs=1))
-        psum = ctx.enter_context(tc.psum_pool(name="psum", bufs=6))
-        held = ctx.enter_context(tc.psum_pool(name="held", bufs=1))
+        psum = ctx.enter_context(tc.psum_pool(name="psum", bufs=1))
+
+        def bank(number, shape):
+            return psum.tile([P] + shape, F32, name="bank", tag="bank%d" % number)
 
         offs_t = keep.tile([P, S // PER_COLUMN], U16, name="offs_t")
         cell_t = keep.tile([P, S // PER_COLUMN], U16, name="cell_t")
         x_rows = xT.rearrange("(p j) c -> j p c", j=PACK)
-        w_rows = w1.rearrange("(p u e) c -> u p e c", u=2, e=2)
-        s_rows = skip.rearrange("(p t) c -> t p c", t=PACK)
+        w_rows = w1.rearrange("(p j) (a c) -> a p j c", j=PACK, a=2)
+        w_cuts = ((0, slice(0, 2)), (0, slice(2, PACK)), (1, slice(0, PACK)))
+        s_even = skip.rearrange("(a q e) c -> e a q c", a=2, e=2)[0]
+        s_slot = skip.rearrange("(p t) c -> t p c", t=PACK)
+        s_rows = {EVEN_LO: s_even[0], EVEN_HI: s_even[1], ODD: s_slot[1], LAST: s_slot[3]}
 
-        x_plane = [keep.tile([P, T], F32, name="x_plane%d" % j) for j in range(PACK)]
-        w_raw = [keep.tile([P, 2, H], F32, name="w_raw%d" % u) for u in range(2)]
-        parts = {FIRST: (0, U), SECOND: (0, GATE, U), THIRD: (0, U), LAST: (0, U)}
-        s_part = {(t, lo): keep.tile([P, hi - lo], F32, name="s_part", tag="s_part%d_%d" % (t, lo))
-                  for t in parts for lo, hi in zip(parts[t], parts[t][1:])}
+        x_plane = [keep.tile([P, T], F32, name="x_plane", tag="x_plane%d" % j) for j in range(PACK)]
+        w_raw = [keep.tile([P, PACK, HALF], F32, name="w_raw%d" % a) for a in range(2)]
+        s_plane = {t: keep.tile([P, U], F32, name="s_plane%d" % t) for t in s_rows}
         w2_codes = keep.tile([P, 2 * N], U8, name="w2_codes", align_bytes=64)
         w2_exp = keep.tile([P, N], U8, name="w2_exp", align_bytes=64)
 
@@ -53,130 +58,174 @@ def tile_picked_unet_relu_e_kernel(tc, xT, w1, w2_words, w2_scales, skip, offs, 
         nc.sync.dma_start(offs_t[:], offs)
         for j in range(1, PACK):
             nc.sync.dma_start(x_plane[j][:], x_rows[j])
-        for u in range(2):
-            nc.sync.dma_start(w_raw[u][:], w_rows[u])
+        for a, js in w_cuts:
+            nc.sync.dma_start(w_raw[a][:, js], w_rows[a][:, js])
         nc.sync.dma_start(cell_t[:], cell)
-        for t in (LAST, FIRST, SECOND, THIRD):
-            for lo, hi in zip(parts[t], parts[t][1:]):
-                nc.sync.dma_start(s_part[t, lo][:], s_rows[t][:, lo:hi])
+        for t in (LAST, EVEN_LO, EVEN_HI, ODD):
+            nc.sync.dma_start(s_plane[t][:], s_rows[t])
         nc.sync.dma_start(w2_codes[:], w2_words[0])
         nc.vector.memset(w2_exp[:].bitcast(I32), 0)
         for q in range(4):
             nc.sync.dma_start(w2_exp[32 * q : 32 * q + 4, :].bitcast(I32), w2_scales[0, 4 * q : 4 * q + 4, :].bitcast(I32))
 
         window = {}
-        for t in parts:
-            window[t] = keep.tile([P, U], F32, name="window", tag="window%d" % t)
+        for t in (HEAD_WINDOW, EVEN_LO, EVEN_HI, ODD):
+            window[t] = keep.tile([P, U], F32, name="window%d" % t)
             nc.vector.memset(window[t][:], 0.0)
+        ident = keep.tile([P, P], F32, name="ident")
+        make_identity(nc, ident[:])
+
+        even_bf = {0: keep.tile([P, P, PACK], BF16, name="even_bf", tag="even_bf", align_bytes=64)}
+        odd_bf = [keep.tile([P, 2, P // 2, PACK], BF16, name="odd_bf%d" % a, align_bytes=64) for a in range(2)]
+        w_codes = {t: keep.tile([P, P], U32, name="w_codes%d" % t, align_bytes=64) for t in s_rows}
+        w_exp = {t: keep.tile([P, P], U8, name="w_exp%d" % t, align_bytes=64) for t in s_rows}
+
+        def even_dealt(a, js):
+            return (even_bf[a][:, :, js].rearrange("p (m i) j -> p m j i", i=2),
+                    w_raw[a][:, js].rearrange("p j (m i e) -> p e m j i", i=2, e=2)[:, 0])
+
+        def odd_dealt(a):
+            return (odd_bf[a][:].rearrange("p i m j -> p m j i"),
+                    w_raw[a][:].rearrange("p j (m i e) -> p e m j i", i=2, e=2)[:, 1])
+
+        def quantise(codes, exps, values):
+            nc.vector.quantize_mx(out=codes.bitcast(FP8X4), scales=exps, in_=values)
+
+        def quantise_even(a):
+            quantise(w_codes[a][:], w_exp[a][:], even_bf[a][:].rearrange("p q j -> p (q j)"))
+
+        def quantise_odd(a):
+            cols = slice(a * P // 2, (a + 1) * P // 2)
+            for i, t in enumerate((ODD, LAST)):
+                quantise(w_codes[t][:, cols], w_exp[t][:, cols], odd_bf[a][:, i].rearrange("p m j -> p (m j)"))
 
         x_bf = keep.tile([P, S, PACK], BF16, name="x_bf", align_bytes=64)
         x_codes = keep.tile([P, S], U32, name="x_codes", align_bytes=64)
         x_exp = keep.tile([P, S], U8, name="x_exp", align_bytes=64)
+
+        def columns(entries):
+            return slice(entries.start // PER_COLUMN, entries.stop // PER_COLUMN)
+
+        def gather(j, entries):
+            nc.vector.tensor_copy(x_bf[:, entries, j], x_plane[j][:].indirect(offs_t[:, columns(entries)]))
+
+        def quantise_x(entries):
+            quantise(x_codes[:, entries], x_exp[:, entries], x_bf[:, entries].rearrange("p n j -> p (n j)"))
+
         for j in range(PACK - 1):
-            nc.vector.tensor_copy(x_bf[:, :, j], x_plane[j][:].indirect(offs_t[:]))
+            gather(j, slice(0, S))
+        pieces = (slice(0, HEAD), slice(HEAD, 2 * HEAD), slice(2 * HEAD, S))
+        turned_both = keep.tile([P, 2 * U], F32, name="turned_both", tag="x_plane0")
+        nc.gpsimd.memset(turned_both[:], 0.0)
+        turned_z = [turned_both[:, U * g : U * (g + 1)] for g in range(2)]
+        window[LAST] = keep.tile([P, U], F32, name="window_last", tag="x_plane1")
+        nc.gpsimd.memset(window[LAST][:], 0.0)
         halves = (slice(0, S // 2), slice(S // 2, S))
         for half in halves:
-            nc.vector.tensor_copy(x_bf[:, half, PACK - 1],
-                                  x_plane[PACK - 1][:].indirect(offs_t[:, half.start // PER_COLUMN : half.stop // PER_COLUMN]))
-        for half in halves:
-            nc.vector.quantize_mx(out=x_codes[:, half].bitcast(FP8X4), scales=x_exp[:, half],
-                                  in_=x_bf[:, half].rearrange("p n j -> p (n j)"))
-
-        groups = ((SECOND, SECOND + 1), (FIRST, FIRST + 1), (THIRD, LAST + 1))
-        w_src = [w_raw[u][:].rearrange("p e (m t) -> p m e t", t=PACK) for u in range(2)]
-        w_bf = [keep.tile([P, hi - lo, P, PACK], BF16, name="w_bf%d" % lo, align_bytes=64) for lo, hi in groups]
-        w_codes, w_exp = {}, {}
-
-        def dealt(g, u):
-            lo, hi = groups[g]
-            return w_bf[g][:].rearrange("p t m (u e) -> p u m e t", u=2)[:, u], w_src[u][:, :, :, lo:hi]
-
-        def quantise_w(g):
-            lo, hi = groups[g]
-            codes = keep.tile([P, (hi - lo) * P], U32, name="w_codes%d" % lo, align_bytes=64)
-            exps = keep.tile([P, (hi - lo) * P], U8, name="w_exp%d" % lo, align_bytes=64)
-            nc.vector.quantize_mx(out=codes[:].bitcast(FP8X4), scales=exps[:], in_=w_bf[g][:].rearrange("p t m j -> p (t m j)"))
-            for t in range(lo, hi):
-                w_codes[t] = codes[:, (t - lo) * P : (t - lo + 1) * P]
-                w_exp[t] = exps[:, (t - lo) * P : (t - lo + 1) * P]
-
-        nc.scalar.activation(*dealt(0, 0), ACT.Copy)
-        nc.scalar.activation(*dealt(1, 0), ACT.Copy)
-        nc.vector.tensor_copy(*dealt(0, 1))
-        nc.scalar.activation(*dealt(1, 1), ACT.Copy)
-        nc.scalar.activation(*dealt(2, 0), ACT.Copy)
-        quantise_w(0)
-        nc.vector.tensor_copy(*dealt(2, 1))
-        quantise_w(1)
-        quantise_w(2)
+            gather(3, half)
+        for cut in w_cuts[:2]:
+            nc.scalar.activation(*even_dealt(*cut), ACT.Copy)
+        nc.scalar.activation(*odd_dealt(0), ACT.Copy)
+        quantise_x(halves[0])
+        quantise_even(0)
+        quantise_x(halves[1])
+        even_bf[1] = keep.tile([P, P, PACK], BF16, name="even_bf", tag="even_bf", align_bytes=64)
+        nc.vector.tensor_copy(*even_dealt(*w_cuts[2]))
+        quantise_odd(0)
 
         def product(acc, t, entries):
-            nc.tensor.matmul_mx(out=acc, lhsT=w_codes[t].bitcast(FP8X4), lhsT_scale=w_exp[t],
+            nc.tensor.matmul_mx(out=acc, lhsT=w_codes[t][:].bitcast(FP8X4), lhsT_scale=w_exp[t][:],
                                 rhs=x_codes[:, entries].bitcast(FP8X4), rhs_scale=x_exp[:, entries], start=True, stop=True)
 
-        def hidden(t, cuts, tag):
-            lo, hi = cuts[0], cuts[-1]
-            acc = psum.tile([P, hi - lo], F32, name="acc", tag="acc")
-            for a, b in zip(cuts, cuts[1:]):
-                product(acc[:, a - lo : b - lo], t, slice(a, b))
-            h = keep.tile([P, hi - lo], F32, name="h", tag=tag)
-            nc.scalar.activation(h[:], acc[:], ACT.Relu)
-            nc.vector.tensor_copy(window[t][:].indirect(cell_t[:, lo // PER_COLUMN : hi // PER_COLUMN]), h[:])
+        hidden = {t: keep.tile([P, S], F32, name="hidden%d" % t) for t in s_rows}
+        h_head = keep.tile([P, HEAD], F32, name="h_head")
 
-        pairs = keep.tile([P, PACK * U], BF16, name="pairs")
-        pair_vals = pairs[:].rearrange("p (b u v e) -> p b u v e", u=2, v=P, e=2)
-        pair_words = pairs[:].bitcast(F32).rearrange("p (b u v) -> p b v u", u=2, v=P)
+        def layer(t, entries, number, target):
+            acc = bank(number, [entries.stop - entries.start])
+            product(acc[:], t, entries)
+            nc.scalar.activation(target, acc[:], ACT.Relu)
 
-        def blocks(ap):
-            return ap.rearrange("p (b v) -> p b v", v=P)
+        def scatter(t, entries, source):
+            nc.vector.tensor_copy(window[t][:].indirect(cell_t[:, columns(entries)]), source)
 
-        def add_into_pairs(engine, t, cells, skip_ap):
-            engine.tensor_tensor(pair_vals[:, cells.start // P : cells.stop // P, t // 2, :, t % 2],
-                                 blocks(window[t][:, cells]), blocks(skip_ap), ADD)
+        layer(EVEN_LO, pieces[0], 0, h_head[:])
+        layer(EVEN_LO, pieces[1], 1, hidden[EVEN_LO][:, pieces[1]])
+        layer(EVEN_LO, pieces[2], 2, hidden[EVEN_LO][:, pieces[2]])
+        nc.scalar.activation(*odd_dealt(1), ACT.Copy)
+        scatter(HEAD_WINDOW, pieces[0], h_head[:])
+        quantise_even(1)
+        scatter(EVEN_LO, slice(HEAD, S), hidden[EVEN_LO][:, HEAD:])
+        quantise_odd(1)
+        for number, t in ((3, EVEN_HI), (4, ODD), (5, LAST)):
+            layer(t, slice(0, S), number, hidden[t][:])
+            scatter(t, slice(0, S), hidden[t][:])
 
-        def add_skip(t, lo, hi):
-            base = max(edge for edge in parts[t] if edge <= lo)
-            add_into_pairs(nc.gpsimd, t, slice(lo, hi), s_part[t, base][:, lo - base : hi - base])
-
-        nc.vector.memset(pair_vals[:, : AHEAD // P, LAST // 2], 0.0)
-
-        hidden(SECOND, (0, HEAD), "h_head")
-        h_first = keep.tile([P, S], F32, name="h_first")
-        for half in halves:
-            acc = psum.tile([P, S // 2], F32, name="acc", tag="acc")
-            product(acc[:], FIRST, half)
-            nc.scalar.activation(h_first[:, half], acc[:], ACT.Relu)
-        nc.vector.tensor_copy(window[FIRST][:].indirect(cell_t[:]), h_first[:])
-        hidden(SECOND, (HEAD, S // 2, S), "h_second")
-        add_skip(FIRST, 0, U)
-        add_skip(SECOND, 0, GATE)
-        add_skip(SECOND, GATE, U)
-        hidden(THIRD, (0, S), "h_third")
-        add_skip(THIRD, 0, AHEAD)
-        add_skip(THIRD, AHEAD, U)
-        hidden(LAST, (0, S), "s_part%d_0" % SECOND)
-
-        ident = keep.tile([P, P], F32, name="ident")
-        make_identity(nc, ident[:])
         s_bank = {}
-        for lo, hi in ((AHEAD, AHEAD + P), (AHEAD + P, U)):
-            turned_ps = psum.tile([P, hi - lo], F32, name="acc", tag="acc")
+        for number, (lo, hi) in enumerate(((AHEAD, AHEAD + P), (AHEAD + P, U))):
+            turned_ps = bank(number, [hi - lo])
             turned = keep.tile([P, hi - lo], F32, name="turned%d" % lo)
-            s_bank[lo] = held.tile([P, hi - lo], F32, name="s_bank", tag="s_bank%d" % lo)
+            s_bank[lo] = bank(6 + number, [hi - lo])
             for at in range(0, hi - lo, P):
-                nc.tensor.transpose(turned_ps[:, at : at + P], s_part[LAST, 0][:, lo + at : lo + at + P], ident[:])
+                nc.tensor.transpose(turned_ps[:, at : at + P], s_plane[LAST][:, lo + at : lo + at + P], ident[:])
             nc.scalar.copy(turned[:], turned_ps[:])
             for at in range(0, hi - lo, P):
                 nc.tensor.transpose(s_bank[lo][:, at : at + P], turned[:, at : at + P], ident[:])
 
-        out_rows = out.rearrange("(g p) v -> p g v", p=P)
-        chunks = [slice(lo, hi) for lo, hi in zip(EDGES, EDGES[1:])]
-        z_bf, z_mx = {}, {}
+        spans = (slice(0, AHEAD), slice(AHEAD, U))
+        pairs = [keep.tile([P, 2 * (span.stop - span.start)], F32, name="pairs%d" % span.start) for span in spans]
+
+        def pair_words(cells):
+            n = 0 if cells.start < AHEAD else 1
+            return pairs[n][:].rearrange("p (u v) -> p u v", u=2)[:, :, cells.start - spans[n].start : cells.stop - spans[n].start]
+
+        def turn_sum(a, g, number):
+            acc = bank(number, [4, P])
+            blocks = [slice(BANK * g + P * b, BANK * g + P * (b + 1)) for b in range(4)]
+            terms = [s_plane[a]] + ([window[HEAD_WINDOW]] if a == EVEN_LO else []) + [window[a]]
+            for n, term in enumerate(terms):
+                for b in range(4):
+                    nc.tensor.matmul(acc[:, b, :], term[:, blocks[b]], ident[:], start=n == 0 and b == 0,
+                                     stop=n == len(terms) - 1 and b == 3, is_transpose=True)
+            vals = turned_z[g].bitcast(BF16).rearrange("v (b u a m e) -> v a e b u m", u=2, a=2, m=P // 2, e=2)
+            nc.scalar.copy(vals[:, a, 0], acc[:].rearrange("v b (m u) -> v b u m", u=2))
+
+        def turn_back(g, u, number):
+            acc = bank(number, [BANK])
+            words = turned_z[g].rearrange("v (b u p) -> v b u p", u=2, p=P)
+            for b in range(4):
+                nc.tensor.transpose(acc[:, P * b : P * (b + 1)], words[:, b, u, :], ident[:])
+            return acc
+
+        def put_back(acc, u, cells):
+            nc.scalar.copy(pair_words(cells)[:, u], acc[:, cells.start % BANK : (cells.stop - 1) % BANK + 1])
+
+        def add_into_pairs(engine, t, cells, skip_ap):
+            target = pair_words(cells)[:, t - ODD].bitcast(BF16).rearrange("p (v e) -> p v e", e=2)[:, :, 1]
+            engine.tensor_tensor(target, window[t][:, cells], skip_ap, ADD)
 
         def weave(cells, name):
             woven = keep.tile([P, cells.stop - cells.start, 2], F32, name=name, align_bytes=64)
-            nc.scalar.copy(woven[:].rearrange("p (b v) u -> p b v u", v=P), pair_words[:, cells.start // P : cells.stop // P])
+            nc.scalar.copy(woven[:], pair_words(cells).rearrange("p u v -> p v u"))
             return woven
+
+        turn_sum(EVEN_LO, 0, 5)
+        turn_sum(EVEN_LO, 1, 4)
+        turn_sum(EVEN_HI, 0, 3)
+        turn_sum(EVEN_HI, 1, 2)
+        back = {(g, u): turn_back(g, u, number) for g, u, number in ((0, 0, 5), (0, 1, 4), (1, 0, 0), (1, 1, 1))}
+        put_back(back[0, 0], 0, spans[0])
+        add_into_pairs(nc.gpsimd, ODD, spans[0], s_plane[ODD][:, spans[0]])
+        put_back(back[0, 1], 1, spans[0])
+        put_back(back[0, 0], 0, slice(AHEAD, BANK))
+        put_back(back[1, 0], 0, slice(BANK, U))
+        add_into_pairs(nc.gpsimd, ODD, spans[1], s_plane[ODD][:, spans[1]])
+        ahead = weave(spans[0], "ahead")
+        put_back(back[0, 1], 1, slice(AHEAD, BANK))
+        put_back(back[1, 1], 1, slice(BANK, U))
+
+        out_rows = out.rearrange("(g p) v -> p g v", p=P)
+        chunks = [slice(lo, hi) for lo, hi in zip(EDGES, EDGES[1:])]
+        z_bf, z_mx = {}, {}
 
         def add_last(c):
             base = max(edge for edge in s_bank if edge <= chunks[c].start)
@@ -186,8 +235,7 @@ def tile_picked_unet_relu_e_kernel(tc, xT, w1, w2_words, w2_scales, skip, offs, 
             width = chunks[c].stop - chunks[c].start
             codes = keep.tile([P, width], U32, name="z_codes%d" % c, align_bytes=64)
             exps = keep.tile([P, width], U8, name="z_exp%d" % c, align_bytes=64)
-            nc.vector.quantize_mx(out=codes[:].bitcast(FP8X4), scales=exps[:],
-                                  in_=z_bf[c].rearrange("p v u -> p (v u)").bitcast(BF16))
+            quantise(codes[:], exps[:], z_bf[c].rearrange("p v u -> p (v u)").bitcast(BF16))
             z_mx[c] = codes, exps
 
         def second_product(acc, g, c):
@@ -196,27 +244,26 @@ def tile_picked_unet_relu_e_kernel(tc, xT, w1, w2_words, w2_scales, skip, offs, 
                                 lhsT_scale=w2_exp[:, P * g : P * (g + 1)],
                                 rhs=codes[:].bitcast(FP8X4), rhs_scale=exps[:], start=True, stop=True)
 
-        def finish_narrow(c):
+        def finish_narrow(c, number):
             res = keep.tile([P, 2, P], F32, name="res%d" % c)
-            acc = psum.tile([P, 2, P], F32, name="acc", tag="acc")
+            acc = bank(number, [2, P])
             for g in range(2):
                 second_product(acc[:, g, :], g, c)
             nc.scalar.copy(res[:], acc[:])
             nc.sync.dma_start(out_rows[:, :, chunks[c]], res[:])
 
-        def finish_wide(c, copies):
+        def finish_wide(c, numbers, copies):
             res = keep.tile([P, 2, 2 * P], F32, name="res%d" % c)
             for g in range(2):
-                acc = psum.tile([P, 2 * P], F32, name="acc", tag="acc")
+                acc = bank(numbers[g], [2 * P])
                 second_product(acc[:], g, c)
                 copies[g](res[:, g, :], acc[:])
                 nc.sync.dma_start(out_rows[:, g, chunks[c]], res[:, g, :])
 
-        ahead = weave(slice(0, AHEAD), "ahead")
         z_bf[0], z_bf[1] = ahead[:, chunks[0]], ahead[:, chunks[1]]
         ahead_vals = ahead[:].rearrange("p v u -> p (v u)").bitcast(BF16).rearrange("p (v t) -> p v t", t=PACK)
         add_last(2)
-        nc.gpsimd.tensor_tensor(ahead_vals[:, :, LAST], window[LAST][:, :AHEAD], s_part[LAST, 0][:, :AHEAD], ADD)
+        nc.gpsimd.tensor_tensor(ahead_vals[:, :, 3], window[LAST][:, :AHEAD], s_plane[LAST][:, :AHEAD], ADD)
         z_bf[2] = weave(chunks[2], "z_bf2")[:]
         for c in (3, 4):
             add_last(c)
@@ -226,10 +273,10 @@ def tile_picked_unet_relu_e_kernel(tc, xT, w1, w2_words, w2_scales, skip, offs, 
         quantise_z(2)
         quantise_z(0)
         quantise_z(1)
-        finish_narrow(2)
+        finish_narrow(2, 2)
         quantise_z(3)
-        finish_wide(0, by_scalar)
+        finish_wide(0, (3, 4), by_scalar)
         quantise_z(4)
-        finish_narrow(1)
-        finish_wide(3, by_scalar)
-        finish_wide(4, (nc.vector.tensor_copy, nc.scalar.copy))
+        finish_narrow(1, 5)
+        finish_wide(3, (0, 1), by_scalar)
+        finish_wide(4, (2, 3), (nc.vector.tensor_copy, nc.scalar.copy))

@@ -23,11 +23,11 @@ PER_COLUMN = 16
 HALF = H // 2
 BANK = 512
 
-EVEN_LO, EVEN_HI, ODD, LAST = 0, 1, 2, 3
+LOW_A, LOW_B, THIRD, LAST = 0, 1, 2, 3
 HEAD = 128
-HEAD_WINDOW = 4
+SPARE = 4
 AHEAD = 384
-EDGES = (0, 256, AHEAD, 512, 768, U)
+EDGES = (0, 128, AHEAD, 512, 768, U)
 
 
 def tile_picked_unet_relu_e_kernel(tc, xT, w1, w2_words, w2_scales, skip, offs, cell, out):
@@ -39,65 +39,75 @@ def tile_picked_unet_relu_e_kernel(tc, xT, w1, w2_words, w2_scales, skip, offs, 
         def bank(number, shape):
             return psum.tile([P] + shape, F32, name="bank", tag="bank%d" % number)
 
+        planes = (LOW_A, LOW_B, THIRD, LAST)
         offs_t = keep.tile([P, S // PER_COLUMN], U16, name="offs_t")
         cell_t = keep.tile([P, S // PER_COLUMN], U16, name="cell_t")
         x_rows = xT.rearrange("(p j) c -> j p c", j=PACK)
         w_rows = w1.rearrange("(p j) (a c) -> a p j c", j=PACK, a=2)
         w_cuts = ((0, slice(0, 2)), (0, slice(2, PACK)), (1, slice(0, PACK)))
-        s_even = skip.rearrange("(a q e) c -> e a q c", a=2, e=2)[0]
+        s_low = skip.rearrange("(a m t) c -> a t m c", a=2, t=PACK)
         s_slot = skip.rearrange("(p t) c -> t p c", t=PACK)
-        s_rows = {EVEN_LO: s_even[0], EVEN_HI: s_even[1], ODD: s_slot[1], LAST: s_slot[3]}
 
         x_plane = [keep.tile([P, T], F32, name="x_plane", tag="x_plane%d" % j) for j in range(PACK)]
         w_raw = [keep.tile([P, PACK, HALF], F32, name="w_raw%d" % a) for a in range(2)]
-        s_plane = {t: keep.tile([P, U], F32, name="s_plane%d" % t) for t in s_rows}
+        s_plane = {t: keep.tile([P, U], F32, name="s_plane%d" % t) for t in (LOW_A, LOW_B, LAST)}
         w2_codes = keep.tile([P, 2 * N], U8, name="w2_codes", align_bytes=64)
         w2_exp = keep.tile([P, N], U8, name="w2_exp", align_bytes=64)
+        spans = (slice(0, AHEAD), slice(AHEAD, U))
+        pairs = [keep.tile([P, 2 * (span.stop - span.start)], F32, name="pairs%d" % span.start) for span in spans]
+
+        def pair_words(cells):
+            n = 0 if cells.start < AHEAD else 1
+            return pairs[n][:].rearrange("p (u v) -> p u v", u=2)[:, :, cells.start - spans[n].start : cells.stop - spans[n].start]
 
         nc.sync.dma_start(x_plane[0][:], x_rows[0])
         nc.sync.dma_start(offs_t[:], offs)
+        nc.sync.dma_start(cell_t[:], cell)
         for j in range(1, PACK):
             nc.sync.dma_start(x_plane[j][:], x_rows[j])
         for a, js in w_cuts:
             nc.sync.dma_start(w_raw[a][:, js], w_rows[a][:, js])
-        nc.sync.dma_start(cell_t[:], cell)
-        for t in (LAST, EVEN_LO, EVEN_HI, ODD):
-            nc.sync.dma_start(s_plane[t][:], s_rows[t])
+        nc.sync.dma_start(s_plane[LAST][:], s_slot[LAST])
+        for a in (LOW_A, LOW_B):
+            for e in range(2):
+                nc.sync.dma_start(s_plane[a][e:P:2, :], s_low[a, e])
+        for span in spans:
+            nc.sync.dma_start(pair_words(span)[:, 1], s_slot[THIRD][:, span])
         nc.sync.dma_start(w2_codes[:], w2_words[0])
         nc.vector.memset(w2_exp[:].bitcast(I32), 0)
         for q in range(4):
             nc.sync.dma_start(w2_exp[32 * q : 32 * q + 4, :].bitcast(I32), w2_scales[0, 4 * q : 4 * q + 4, :].bitcast(I32))
 
         window = {}
-        for t in (HEAD_WINDOW, EVEN_LO, EVEN_HI, ODD):
+        for t in (SPARE, LOW_A, LOW_B, THIRD):
             window[t] = keep.tile([P, U], F32, name="window%d" % t)
             nc.vector.memset(window[t][:], 0.0)
         ident = keep.tile([P, P], F32, name="ident")
         make_identity(nc, ident[:])
 
-        even_bf = {0: keep.tile([P, P, PACK], BF16, name="even_bf", tag="even_bf", align_bytes=64)}
-        odd_bf = [keep.tile([P, 2, P // 2, PACK], BF16, name="odd_bf%d" % a, align_bytes=64) for a in range(2)]
-        w_codes = {t: keep.tile([P, P], U32, name="w_codes%d" % t, align_bytes=64) for t in s_rows}
-        w_exp = {t: keep.tile([P, P], U8, name="w_exp%d" % t, align_bytes=64) for t in s_rows}
+        low_bf = [keep.tile([P, P, PACK], BF16, name="low_bf%d" % a, align_bytes=64) for a in range(2)]
+        high_bf = [keep.tile([P, 2, P // 2, PACK], BF16, name="high_bf%d" % a, align_bytes=64) for a in range(2)]
+        w_codes = {t: keep.tile([P, P], U32, name="w_codes%d" % t, align_bytes=64) for t in planes}
+        w_exp = {t: keep.tile([P, P], U8, name="w_exp%d" % t, align_bytes=64) for t in planes}
 
-        def even_dealt(a, js):
-            return (even_bf[a][:, :, js].rearrange("p (m i) j -> p m j i", i=2),
-                    w_raw[a][:, js].rearrange("p j (m i e) -> p e m j i", i=2, e=2)[:, 0])
+        def deal_low(a, js):
+            nc.scalar.activation(low_bf[a][:, :, js].rearrange("p (m e) j -> p m j e", e=2),
+                                 w_raw[a][:, js].rearrange("p j (m u e) -> p u m j e", u=2, e=2)[:, 0], ACT.Copy)
 
-        def odd_dealt(a):
-            return (odd_bf[a][:].rearrange("p i m j -> p m j i"),
-                    w_raw[a][:].rearrange("p j (m i e) -> p e m j i", i=2, e=2)[:, 1])
+        def deal_high(a):
+            nc.scalar.activation(high_bf[a][:].rearrange("p e m j -> p m j e"),
+                                 w_raw[a][:].rearrange("p j (m u e) -> p u m j e", u=2, e=2)[:, 1], ACT.Copy)
 
         def quantise(codes, exps, values):
             nc.vector.quantize_mx(out=codes.bitcast(FP8X4), scales=exps, in_=values)
 
-        def quantise_even(a):
-            quantise(w_codes[a][:], w_exp[a][:], even_bf[a][:].rearrange("p q j -> p (q j)"))
+        def quantise_low(a):
+            quantise(w_codes[a][:], w_exp[a][:], low_bf[a][:].rearrange("p q j -> p (q j)"))
 
-        def quantise_odd(a):
+        def quantise_high(a):
             cols = slice(a * P // 2, (a + 1) * P // 2)
-            for i, t in enumerate((ODD, LAST)):
-                quantise(w_codes[t][:, cols], w_exp[t][:, cols], odd_bf[a][:, i].rearrange("p m j -> p (m j)"))
+            for e, t in enumerate((THIRD, LAST)):
+                quantise(w_codes[t][:, cols], w_exp[t][:, cols], high_bf[a][:, e].rearrange("p m j -> p (m j)"))
 
         x_bf = keep.tile([P, S, PACK], BF16, name="x_bf", align_bytes=64)
         x_codes = keep.tile([P, S], U32, name="x_codes", align_bytes=64)
@@ -115,49 +125,47 @@ def tile_picked_unet_relu_e_kernel(tc, xT, w1, w2_words, w2_scales, skip, offs, 
         for j in range(PACK - 1):
             gather(j, slice(0, S))
         pieces = (slice(0, HEAD), slice(HEAD, 2 * HEAD), slice(2 * HEAD, S))
-        turned_both = keep.tile([P, 2 * U], F32, name="turned_both", tag="x_plane0")
-        nc.gpsimd.memset(turned_both[:], 0.0)
-        turned_z = [turned_both[:, U * g : U * (g + 1)] for g in range(2)]
         window[LAST] = keep.tile([P, U], F32, name="window_last", tag="x_plane1")
         nc.gpsimd.memset(window[LAST][:], 0.0)
         halves = (slice(0, S // 2), slice(S // 2, S))
         for half in halves:
             gather(3, half)
         for cut in w_cuts[:2]:
-            nc.scalar.activation(*even_dealt(*cut), ACT.Copy)
-        nc.scalar.activation(*odd_dealt(0), ACT.Copy)
+            deal_low(*cut)
+        deal_high(0)
         quantise_x(halves[0])
-        quantise_even(0)
+        quantise_low(0)
         quantise_x(halves[1])
-        even_bf[1] = keep.tile([P, P, PACK], BF16, name="even_bf", tag="even_bf", align_bytes=64)
-        nc.vector.tensor_copy(*even_dealt(*w_cuts[2]))
-        quantise_odd(0)
+        quantise_high(0)
 
         def product(acc, t, entries):
             nc.tensor.matmul_mx(out=acc, lhsT=w_codes[t][:].bitcast(FP8X4), lhsT_scale=w_exp[t][:],
                                 rhs=x_codes[:, entries].bitcast(FP8X4), rhs_scale=x_exp[:, entries], start=True, stop=True)
 
-        hidden = {t: keep.tile([P, S], F32, name="hidden%d" % t) for t in s_rows}
+        hidden = {t: keep.tile([P, S], F32, name="hidden%d" % t) for t in planes}
         h_head = keep.tile([P, HEAD], F32, name="h_head")
 
-        def layer(t, entries, number, target):
+        def layer(t, entries, number):
             acc = bank(number, [entries.stop - entries.start])
             product(acc[:], t, entries)
-            nc.scalar.activation(target, acc[:], ACT.Relu)
+            nc.scalar.activation(hidden[t][:, entries], acc[:], ACT.Relu)
 
         def scatter(t, entries, source):
             nc.vector.tensor_copy(window[t][:].indirect(cell_t[:, columns(entries)]), source)
 
-        layer(EVEN_LO, pieces[0], 0, h_head[:])
-        layer(EVEN_LO, pieces[1], 1, hidden[EVEN_LO][:, pieces[1]])
-        layer(EVEN_LO, pieces[2], 2, hidden[EVEN_LO][:, pieces[2]])
-        nc.scalar.activation(*odd_dealt(1), ACT.Copy)
-        scatter(HEAD_WINDOW, pieces[0], h_head[:])
-        quantise_even(1)
-        scatter(EVEN_LO, slice(HEAD, S), hidden[EVEN_LO][:, HEAD:])
-        quantise_odd(1)
-        for number, t in ((3, EVEN_HI), (4, ODD), (5, LAST)):
-            layer(t, slice(0, S), number, hidden[t][:])
+        acc_head = bank(0, [HEAD])
+        product(acc_head[:], LOW_A, pieces[0])
+        nc.vector.tensor_scalar_max(h_head[:], acc_head[:], 0.0)
+        scatter(SPARE, pieces[0], h_head[:])
+        deal_low(*w_cuts[2])
+        quantise_low(1)
+        layer(LOW_A, pieces[1], 1)
+        layer(LOW_A, pieces[2], 2)
+        scatter(LOW_A, slice(HEAD, S), hidden[LOW_A][:, HEAD:])
+        deal_high(1)
+        quantise_high(1)
+        for number, t in ((3, LOW_B), (4, THIRD), (5, LAST)):
+            layer(t, slice(0, S), number)
             scatter(t, slice(0, S), hidden[t][:])
 
         s_bank = {}
@@ -171,57 +179,44 @@ def tile_picked_unet_relu_e_kernel(tc, xT, w1, w2_words, w2_scales, skip, offs, 
             for at in range(0, hi - lo, P):
                 nc.tensor.transpose(s_bank[lo][:, at : at + P], turned[:, at : at + P], ident[:])
 
-        spans = (slice(0, AHEAD), slice(AHEAD, U))
-        pairs = [keep.tile([P, 2 * (span.stop - span.start)], F32, name="pairs%d" % span.start) for span in spans]
+        turned_z = [keep.tile([P, 4, P], F32, name="turned_z%d" % g) for g in range(2)]
 
-        def pair_words(cells):
-            n = 0 if cells.start < AHEAD else 1
-            return pairs[n][:].rearrange("p (u v) -> p u v", u=2)[:, :, cells.start - spans[n].start : cells.stop - spans[n].start]
-
-        def turn_sum(a, g, number):
-            acc = bank(number, [4, P])
-            blocks = [slice(BANK * g + P * b, BANK * g + P * (b + 1)) for b in range(4)]
-            terms = [s_plane[a]] + ([window[HEAD_WINDOW]] if a == EVEN_LO else []) + [window[a]]
+        def turn_sum(a, terms, numbers):
+            acc = [bank(number, [4, P]) for number in numbers]
             for n, term in enumerate(terms):
-                for b in range(4):
-                    nc.tensor.matmul(acc[:, b, :], term[:, blocks[b]], ident[:], start=n == 0 and b == 0,
-                                     stop=n == len(terms) - 1 and b == 3, is_transpose=True)
-            vals = turned_z[g].bitcast(BF16).rearrange("v (b u a m e) -> v a e b u m", u=2, a=2, m=P // 2, e=2)
-            nc.scalar.copy(vals[:, a, 0], acc[:].rearrange("v b (m u) -> v b u m", u=2))
+                for g in range(2):
+                    for b in range(4):
+                        at = BANK * g + P * b
+                        nc.tensor.matmul(acc[g][:, b, :], term[:, at : at + P], ident[:], start=n == 0 and b == 0,
+                                         stop=n == len(terms) - 1 and b == 3, is_transpose=True)
+            for g in range(2):
+                nc.scalar.copy(turned_z[g][:].bitcast(BF16)[:, :, P * a : P * (a + 1)], acc[g][:])
 
-        def turn_back(g, u, number):
+        def turn_back(g, number):
             acc = bank(number, [BANK])
-            words = turned_z[g].rearrange("v (b u p) -> v b u p", u=2, p=P)
             for b in range(4):
-                nc.tensor.transpose(acc[:, P * b : P * (b + 1)], words[:, b, u, :], ident[:])
+                nc.tensor.transpose(acc[:, P * b : P * (b + 1)], turned_z[g][:, b, :], ident[:])
             return acc
 
-        def put_back(acc, u, cells):
-            nc.scalar.copy(pair_words(cells)[:, u], acc[:, cells.start % BANK : (cells.stop - 1) % BANK + 1])
+        def put_back(acc, cells):
+            nc.scalar.copy(pair_words(cells)[:, 0], acc[:, cells.start % BANK : (cells.stop - 1) % BANK + 1])
 
-        def add_into_pairs(engine, t, cells, skip_ap):
-            target = pair_words(cells)[:, t - ODD].bitcast(BF16).rearrange("p (v e) -> p v e", e=2)[:, :, 1]
-            engine.tensor_tensor(target, window[t][:, cells], skip_ap, ADD)
+        def pair_values(cells, e):
+            return pair_words(cells)[:, 1].bitcast(BF16).rearrange("p (v e) -> p v e", e=2)[:, :, e]
 
         def weave(cells, name):
             woven = keep.tile([P, cells.stop - cells.start, 2], F32, name=name, align_bytes=64)
             nc.scalar.copy(woven[:], pair_words(cells).rearrange("p u v -> p v u"))
             return woven
 
-        turn_sum(EVEN_LO, 0, 5)
-        turn_sum(EVEN_LO, 1, 4)
-        turn_sum(EVEN_HI, 0, 3)
-        turn_sum(EVEN_HI, 1, 2)
-        back = {(g, u): turn_back(g, u, number) for g, u, number in ((0, 0, 5), (0, 1, 4), (1, 0, 0), (1, 1, 1))}
-        put_back(back[0, 0], 0, spans[0])
-        add_into_pairs(nc.gpsimd, ODD, spans[0], s_plane[ODD][:, spans[0]])
-        put_back(back[0, 1], 1, spans[0])
-        put_back(back[0, 0], 0, slice(AHEAD, BANK))
-        put_back(back[1, 0], 0, slice(BANK, U))
-        add_into_pairs(nc.gpsimd, ODD, spans[1], s_plane[ODD][:, spans[1]])
-        ahead = weave(spans[0], "ahead")
-        put_back(back[0, 1], 1, slice(AHEAD, BANK))
-        put_back(back[1, 1], 1, slice(BANK, U))
+        turn_sum(LOW_A, (s_plane[LOW_A], window[SPARE], window[LOW_A]), (2, 3))
+        turn_sum(LOW_B, (s_plane[LOW_B], window[LOW_B]), (4, 5))
+        back = [turn_back(g, g) for g in range(2)]
+        put_back(back[0], spans[0])
+        put_back(back[0], slice(AHEAD, BANK))
+        put_back(back[1], slice(BANK, U))
+        for span in spans:
+            nc.gpsimd.tensor_tensor(pair_values(span, 0), window[THIRD][:, span], pair_words(span)[:, 1], ADD)
 
         out_rows = out.rearrange("(g p) v -> p g v", p=P)
         chunks = [slice(lo, hi) for lo, hi in zip(EDGES, EDGES[1:])]
@@ -229,7 +224,8 @@ def tile_picked_unet_relu_e_kernel(tc, xT, w1, w2_words, w2_scales, skip, offs, 
 
         def add_last(c):
             base = max(edge for edge in s_bank if edge <= chunks[c].start)
-            add_into_pairs(nc.vector, LAST, chunks[c], s_bank[base][:, chunks[c].start - base : chunks[c].stop - base])
+            nc.vector.tensor_tensor(pair_values(chunks[c], 1), window[LAST][:, chunks[c]],
+                                    s_bank[base][:, chunks[c].start - base : chunks[c].stop - base], ADD)
 
         def quantise_z(c):
             width = chunks[c].stop - chunks[c].start
@@ -260,23 +256,28 @@ def tile_picked_unet_relu_e_kernel(tc, xT, w1, w2_words, w2_scales, skip, offs, 
                 copies[g](res[:, g, :], acc[:])
                 nc.sync.dma_start(out_rows[:, g, chunks[c]], res[:, g, :])
 
-        z_bf[0], z_bf[1] = ahead[:, chunks[0]], ahead[:, chunks[1]]
-        ahead_vals = ahead[:].rearrange("p v u -> p (v u)").bitcast(BF16).rearrange("p (v t) -> p v t", t=PACK)
+        for c in (0, 1):
+            z_bf[c] = weave(chunks[c], "z_bf%d" % c)[:]
         add_last(2)
-        nc.gpsimd.tensor_tensor(ahead_vals[:, :, 3], window[LAST][:, :AHEAD], s_plane[LAST][:, :AHEAD], ADD)
+        for c in (0, 1):
+            values = z_bf[c].rearrange("p v u -> p (v u)").bitcast(BF16).rearrange("p (v t) -> p v t", t=PACK)
+            for at in range(chunks[c].start, chunks[c].stop, P):
+                here = at - chunks[c].start
+                nc.gpsimd.tensor_tensor(values[:, here : here + P, LAST], window[LAST][:, at : at + P],
+                                        s_plane[LAST][:, at : at + P], ADD)
         z_bf[2] = weave(chunks[2], "z_bf2")[:]
         for c in (3, 4):
             add_last(c)
             z_bf[c] = weave(chunks[c], "z_bf%d" % c)[:]
 
         by_scalar = (nc.scalar.copy, nc.scalar.copy)
-        quantise_z(2)
         quantise_z(0)
+        quantise_z(2)
+        finish_narrow(0, 2)
         quantise_z(1)
-        finish_narrow(2, 2)
+        finish_narrow(2, 5)
         quantise_z(3)
-        finish_wide(0, (3, 4), by_scalar)
+        finish_wide(1, (3, 4), by_scalar)
         quantise_z(4)
-        finish_narrow(1, 5)
         finish_wide(3, (0, 1), by_scalar)
         finish_wide(4, (2, 3), (nc.vector.tensor_copy, nc.scalar.copy))

@@ -1,7 +1,6 @@
 from contextlib import ExitStack
 
 import concourse.mybir as mybir
-from concourse.masks import make_identity
 
 K, T, S, H, N, U = 512, 2048, 512, 512, 256, 1024
 FLOPS = 2 * K * H * S + 2 * H * N * U
@@ -20,14 +19,7 @@ ADD = mybir.AluOpType.add
 P = 128
 PACK = 4
 PER_COLUMN = 16
-HALF = H // 2
-BANK = 512
-
-LOW_A, LOW_B, THIRD, LAST = 0, 1, 2, 3
-HEAD = 128
-SPARE = 4
-AHEAD = 384
-EDGES = (0, 128, AHEAD, 512, 768, U)
+EDGES = (0, 256, 512, 768, U)
 
 
 def tile_picked_unet_relu_e_kernel(tc, xT, w1, w2_words, w2_scales, skip, offs, cell, out):
@@ -39,245 +31,142 @@ def tile_picked_unet_relu_e_kernel(tc, xT, w1, w2_words, w2_scales, skip, offs, 
         def bank(number, shape):
             return psum.tile([P] + shape, F32, name="bank", tag="bank%d" % number)
 
-        planes = (LOW_A, LOW_B, THIRD, LAST)
         offs_t = keep.tile([P, S // PER_COLUMN], U16, name="offs_t")
         cell_t = keep.tile([P, S // PER_COLUMN], U16, name="cell_t")
         x_rows = xT.rearrange("(p j) c -> j p c", j=PACK)
-        w_rows = w1.rearrange("(p j) (a c) -> a p j c", j=PACK, a=2)
-        w_cuts = ((0, slice(0, 2)), (0, slice(2, PACK)), (1, slice(0, PACK)))
-        s_low = skip.rearrange("(a m t) c -> a t m c", a=2, t=PACK)
-        s_slot = skip.rearrange("(p t) c -> t p c", t=PACK)
-
-        x_plane = [keep.tile([P, T], F32, name="x_plane", tag="x_plane%d" % j) for j in range(PACK)]
-        w_raw = [keep.tile([P, PACK, HALF], F32, name="w_raw%d" % a) for a in range(2)]
-        s_plane = {t: keep.tile([P, U], F32, name="s_plane%d" % t) for t in (LOW_A, LOW_B, LAST)}
+        s_rows = skip.rearrange("(p t) c -> t p c", t=PACK)
+        x_plane = [keep.tile([P, T], F32, name="x_plane%d" % j) for j in range(PACK)]
+        s_plane = [keep.tile([P, U], F32, name="s_plane%d" % t) for t in range(PACK)]
+        w_raw = keep.tile([P, PACK, H], F32, name="w_raw")
         w2_codes = keep.tile([P, 2 * N], U8, name="w2_codes", align_bytes=64)
         w2_exp = keep.tile([P, N], U8, name="w2_exp", align_bytes=64)
-        spans = (slice(0, AHEAD), slice(AHEAD, U))
-        pairs = [keep.tile([P, 2 * (span.stop - span.start)], F32, name="pairs%d" % span.start) for span in spans]
 
-        def pair_words(cells):
-            n = 0 if cells.start < AHEAD else 1
-            return pairs[n][:].rearrange("p (u v) -> p u v", u=2)[:, :, cells.start - spans[n].start : cells.stop - spans[n].start]
-
-        nc.sync.dma_start(x_plane[0][:], x_rows[0])
+        nc.sync.dma_start(w_raw[:], w1.rearrange("(p j) c -> p j c", j=PACK))
         nc.sync.dma_start(offs_t[:], offs)
-        nc.sync.dma_start(cell_t[:], cell)
-        for j in range(1, PACK):
+        for j in range(PACK):
             nc.sync.dma_start(x_plane[j][:], x_rows[j])
-        for a, js in w_cuts:
-            nc.sync.dma_start(w_raw[a][:, js], w_rows[a][:, js])
-        nc.sync.dma_start(s_plane[LAST][:], s_slot[LAST])
-        for a in (LOW_A, LOW_B):
-            for e in range(2):
-                nc.sync.dma_start(s_plane[a][e:P:2, :], s_low[a, e])
-        for span in spans:
-            nc.sync.dma_start(pair_words(span)[:, 1], s_slot[THIRD][:, span])
+        nc.sync.dma_start(cell_t[:], cell)
+        for t in range(PACK):
+            nc.sync.dma_start(s_plane[t][:], s_rows[t])
         nc.sync.dma_start(w2_codes[:], w2_words[0])
         nc.vector.memset(w2_exp[:].bitcast(I32), 0)
         for q in range(4):
             nc.sync.dma_start(w2_exp[32 * q : 32 * q + 4, :].bitcast(I32), w2_scales[0, 4 * q : 4 * q + 4, :].bitcast(I32))
 
-        window = {}
-        for t in (SPARE, LOW_A, LOW_B, THIRD):
-            window[t] = keep.tile([P, U], F32, name="window%d" % t)
+        window = [keep.tile([P, U], F32, name="window%d" % t) for t in range(PACK)]
+        for t in range(PACK):
             nc.vector.memset(window[t][:], 0.0)
-        ident = keep.tile([P, P], F32, name="ident")
-        make_identity(nc, ident[:])
-
-        low_bf = [keep.tile([P, P, PACK], BF16, name="low_bf%d" % a, align_bytes=64) for a in range(2)]
-        high_bf = [keep.tile([P, 2, P // 2, PACK], BF16, name="high_bf%d" % a, align_bytes=64) for a in range(2)]
-        w_codes = {t: keep.tile([P, P], U32, name="w_codes%d" % t, align_bytes=64) for t in planes}
-        w_exp = {t: keep.tile([P, P], U8, name="w_exp%d" % t, align_bytes=64) for t in planes}
-
-        def deal_low(a, js):
-            nc.scalar.activation(low_bf[a][:, :, js].rearrange("p (m e) j -> p m j e", e=2),
-                                 w_raw[a][:, js].rearrange("p j (m u e) -> p u m j e", u=2, e=2)[:, 0], ACT.Copy)
-
-        def deal_high(a):
-            nc.scalar.activation(high_bf[a][:].rearrange("p e m j -> p m j e"),
-                                 w_raw[a][:].rearrange("p j (m u e) -> p u m j e", u=2, e=2)[:, 1], ACT.Copy)
 
         def quantise(codes, exps, values):
             nc.vector.quantize_mx(out=codes.bitcast(FP8X4), scales=exps, in_=values)
 
-        def quantise_low(a):
-            quantise(w_codes[a][:], w_exp[a][:], low_bf[a][:].rearrange("p q j -> p (q j)"))
-
-        def quantise_high(a):
-            cols = slice(a * P // 2, (a + 1) * P // 2)
-            for e, t in enumerate((THIRD, LAST)):
-                quantise(w_codes[t][:, cols], w_exp[t][:, cols], high_bf[a][:, e].rearrange("p m j -> p (m j)"))
+        w_bf = keep.tile([P, PACK, P, PACK], BF16, name="w_bf", align_bytes=64)
+        w_codes = keep.tile([P, H], U32, name="w_codes", align_bytes=64)
+        w_exp = keep.tile([P, H], U8, name="w_exp", align_bytes=64)
+        nc.scalar.activation(w_bf[:].rearrange("p t m j -> p m j t"), w_raw[:].rearrange("p j (m t) -> p m j t", t=PACK), ACT.Copy)
+        quantise(w_codes[:], w_exp[:], w_bf[:].rearrange("p t m j -> p (t m j)"))
 
         x_bf = keep.tile([P, S, PACK], BF16, name="x_bf", align_bytes=64)
+        x_late = keep.tile([P, S // 2], BF16, name="x_late")
         x_codes = keep.tile([P, S], U32, name="x_codes", align_bytes=64)
         x_exp = keep.tile([P, S], U8, name="x_exp", align_bytes=64)
+        whole = slice(0, S)
+        first, second = slice(0, S // 2), slice(S // 2, S)
 
         def columns(entries):
             return slice(entries.start // PER_COLUMN, entries.stop // PER_COLUMN)
 
-        def gather(j, entries):
-            nc.vector.tensor_copy(x_bf[:, entries, j], x_plane[j][:].indirect(offs_t[:, columns(entries)]))
-
-        def quantise_x(entries):
-            quantise(x_codes[:, entries], x_exp[:, entries], x_bf[:, entries].rearrange("p n j -> p (n j)"))
+        def picked(j, entries):
+            return x_plane[j][:].indirect(offs_t[:, columns(entries)])
 
         for j in range(PACK - 1):
-            gather(j, slice(0, S))
-        pieces = (slice(0, HEAD), slice(HEAD, 2 * HEAD), slice(2 * HEAD, S))
-        window[LAST] = keep.tile([P, U], F32, name="window_last", tag="x_plane1")
-        nc.gpsimd.memset(window[LAST][:], 0.0)
-        halves = (slice(0, S // 2), slice(S // 2, S))
-        for half in halves:
-            gather(3, half)
-        for cut in w_cuts[:2]:
-            deal_low(*cut)
-        deal_high(0)
-        quantise_x(halves[0])
-        quantise_low(0)
-        quantise_x(halves[1])
-        quantise_high(0)
+            nc.vector.tensor_copy(x_bf[:, whole, j], picked(j, whole))
+        nc.vector.tensor_copy(x_bf[:, first, PACK - 1], picked(PACK - 1, first))
+        nc.scalar.activation(x_late[:], picked(PACK - 1, second), ACT.Copy)
+        nc.vector.tensor_copy(x_bf[:, second, PACK - 1], x_late[:])
+        for half in (first, second):
+            quantise(x_codes[:, half], x_exp[:, half], x_bf[:, half].rearrange("p n j -> p (n j)"))
 
-        def product(acc, t, entries):
-            nc.tensor.matmul_mx(out=acc, lhsT=w_codes[t][:].bitcast(FP8X4), lhsT_scale=w_exp[t][:],
-                                rhs=x_codes[:, entries].bitcast(FP8X4), rhs_scale=x_exp[:, entries], start=True, stop=True)
+        hidden = {}
 
-        hidden = {t: keep.tile([P, S], F32, name="hidden%d" % t) for t in planes}
-        h_head = keep.tile([P, HEAD], F32, name="h_head")
-
-        def layer(t, entries, number):
+        def product(t, entries, number):
             acc = bank(number, [entries.stop - entries.start])
-            product(acc[:], t, entries)
-            nc.scalar.activation(hidden[t][:, entries], acc[:], ACT.Relu)
-
-        def scatter(t, entries, source):
-            nc.vector.tensor_copy(window[t][:].indirect(cell_t[:, columns(entries)]), source)
-
-        acc_head = bank(0, [HEAD])
-        product(acc_head[:], LOW_A, pieces[0])
-        nc.vector.tensor_scalar_max(h_head[:], acc_head[:], 0.0)
-        scatter(SPARE, pieces[0], h_head[:])
-        deal_low(*w_cuts[2])
-        quantise_low(1)
-        layer(LOW_A, pieces[1], 1)
-        layer(LOW_A, pieces[2], 2)
-        scatter(LOW_A, slice(HEAD, S), hidden[LOW_A][:, HEAD:])
-        deal_high(1)
-        quantise_high(1)
-        for number, t in ((3, LOW_B), (4, THIRD), (5, LAST)):
-            layer(t, slice(0, S), number)
-            scatter(t, slice(0, S), hidden[t][:])
-
-        s_bank = {}
-        for number, (lo, hi) in enumerate(((AHEAD, AHEAD + P), (AHEAD + P, U))):
-            turned_ps = bank(number, [hi - lo])
-            turned = keep.tile([P, hi - lo], F32, name="turned%d" % lo)
-            s_bank[lo] = bank(6 + number, [hi - lo])
-            for at in range(0, hi - lo, P):
-                nc.tensor.transpose(turned_ps[:, at : at + P], s_plane[LAST][:, lo + at : lo + at + P], ident[:])
-            nc.scalar.copy(turned[:], turned_ps[:])
-            for at in range(0, hi - lo, P):
-                nc.tensor.transpose(s_bank[lo][:, at : at + P], turned[:, at : at + P], ident[:])
-
-        turned_z = [keep.tile([P, 4, P], F32, name="turned_z%d" % g) for g in range(2)]
-
-        def turn_sum(a, terms, numbers):
-            acc = [bank(number, [4, P]) for number in numbers]
-            for n, term in enumerate(terms):
-                for g in range(2):
-                    for b in range(4):
-                        at = BANK * g + P * b
-                        nc.tensor.matmul(acc[g][:, b, :], term[:, at : at + P], ident[:], start=n == 0 and b == 0,
-                                         stop=n == len(terms) - 1 and b == 3, is_transpose=True)
-            for g in range(2):
-                nc.scalar.copy(turned_z[g][:].bitcast(BF16)[:, :, P * a : P * (a + 1)], acc[g][:])
-
-        def turn_back(g, number):
-            acc = bank(number, [BANK])
-            for b in range(4):
-                nc.tensor.transpose(acc[:, P * b : P * (b + 1)], turned_z[g][:, b, :], ident[:])
+            cols = slice(P * t, P * (t + 1))
+            nc.tensor.matmul_mx(out=acc[:], lhsT=w_codes[:, cols].bitcast(FP8X4), lhsT_scale=w_exp[:, cols],
+                                rhs=x_codes[:, entries].bitcast(FP8X4), rhs_scale=x_exp[:, entries], start=True, stop=True)
+            hidden[t, entries.start] = keep.tile([P, entries.stop - entries.start], F32, name="hidden%d_%d" % (t, entries.start))
             return acc
 
-        def put_back(acc, cells):
-            nc.scalar.copy(pair_words(cells)[:, 0], acc[:, cells.start % BANK : (cells.stop - 1) % BANK + 1])
+        def relu_scalar(t, entries, acc):
+            nc.scalar.activation(hidden[t, entries.start][:], acc[:], ACT.Relu)
 
-        def pair_values(cells, e):
-            return pair_words(cells)[:, 1].bitcast(BF16).rearrange("p (v e) -> p v e", e=2)[:, :, e]
+        def relu_vector(t, entries, acc):
+            nc.vector.tensor_scalar_max(hidden[t, entries.start][:], acc[:], 0.0)
 
-        def weave(cells, name):
-            woven = keep.tile([P, cells.stop - cells.start, 2], F32, name=name, align_bytes=64)
-            nc.scalar.copy(woven[:], pair_words(cells).rearrange("p u v -> p v u"))
-            return woven
+        def scatter_scalar(t, entries):
+            nc.scalar.activation(window[t][:].indirect(cell_t[:, columns(entries)]), hidden[t, entries.start][:], ACT.Copy)
 
-        turn_sum(LOW_A, (s_plane[LOW_A], window[SPARE], window[LOW_A]), (2, 3))
-        turn_sum(LOW_B, (s_plane[LOW_B], window[LOW_B]), (4, 5))
-        back = [turn_back(g, g) for g in range(2)]
-        put_back(back[0], spans[0])
-        put_back(back[0], slice(AHEAD, BANK))
-        put_back(back[1], slice(BANK, U))
-        for span in spans:
-            nc.gpsimd.tensor_tensor(pair_values(span, 0), window[THIRD][:, span], pair_words(span)[:, 1], ADD)
+        def scatter_vector(t, entries):
+            nc.vector.tensor_copy(window[t][:].indirect(cell_t[:, columns(entries)]), hidden[t, entries.start][:])
+
+        order = ((0, first), (1, first), (0, second), (2, whole), (1, second), (3, first), (3, second))
+        acc = {(t, entries.start): product(t, entries, number) for number, (t, entries) in enumerate(order)}
+        relu_scalar(0, first, acc[0, 0])
+        scatter_vector(0, first)
+        relu_scalar(1, first, acc[1, 0])
+        relu_scalar(0, second, acc[0, S // 2])
+        scatter_scalar(1, first)
+        relu_vector(2, whole, acc[2, 0])
+        scatter_vector(0, second)
+        relu_scalar(1, second, acc[1, S // 2])
+        scatter_scalar(1, second)
+        relu_vector(3, first, acc[3, 0])
+        scatter_vector(2, whole)
+        scatter_scalar(3, first)
+        relu_scalar(3, second, acc[3, S // 2])
+        scatter_scalar(3, second)
+
+        chunks = [slice(lo, hi) for lo, hi in zip(EDGES, EDGES[1:])]
+        pairs = [keep.tile([P, 2, c.stop - c.start], F32, name="pairs%d" % c.start) for c in chunks]
+
+        def add_skip(engine, t, c):
+            values = pairs[c][:, t // 2].bitcast(BF16).rearrange("p (v e) -> p v e", e=2)[:, :, t % 2]
+            engine.tensor_tensor(values, window[t][:, chunks[c]], s_plane[t][:, chunks[c]], ADD)
+
+        for t in (0, 1):
+            for c in range(len(chunks)):
+                add_skip(nc.gpsimd, t, c)
 
         out_rows = out.rearrange("(g p) v -> p g v", p=P)
-        chunks = [slice(lo, hi) for lo, hi in zip(EDGES, EDGES[1:])]
         z_bf, z_mx = {}, {}
 
-        def add_last(c):
-            base = max(edge for edge in s_bank if edge <= chunks[c].start)
-            nc.vector.tensor_tensor(pair_values(chunks[c], 1), window[LAST][:, chunks[c]],
-                                    s_bank[base][:, chunks[c].start - base : chunks[c].stop - base], ADD)
+        def weave(c):
+            width = chunks[c].stop - chunks[c].start
+            for t in (2, 3):
+                add_skip(nc.vector, t, c)
+            z_bf[c] = keep.tile([P, width, 2], F32, name="z_bf%d" % c, align_bytes=64)
+            nc.scalar.copy(z_bf[c][:], pairs[c][:].rearrange("p u v -> p v u"))
 
-        def quantise_z(c):
+        def finish(c, number):
             width = chunks[c].stop - chunks[c].start
             codes = keep.tile([P, width], U32, name="z_codes%d" % c, align_bytes=64)
             exps = keep.tile([P, width], U8, name="z_exp%d" % c, align_bytes=64)
-            quantise(codes[:], exps[:], z_bf[c].rearrange("p v u -> p (v u)").bitcast(BF16))
-            z_mx[c] = codes, exps
-
-        def second_product(acc, g, c):
-            codes, exps = z_mx[c]
-            nc.tensor.matmul_mx(out=acc, lhsT=w2_codes[:, 2 * P * g : 2 * P * (g + 1)].bitcast(FP4X4),
-                                lhsT_scale=w2_exp[:, P * g : P * (g + 1)],
-                                rhs=codes[:].bitcast(FP8X4), rhs_scale=exps[:], start=True, stop=True)
-
-        def finish_narrow(c, number):
-            res = keep.tile([P, 2, P], F32, name="res%d" % c)
-            acc = bank(number, [2, P])
+            quantise(codes[:], exps[:], z_bf[c][:].rearrange("p v u -> p (v u)").bitcast(BF16))
+            last = c == len(chunks) - 1
+            res = keep.tile([P, 2, width], F32, name="res%d" % c)
             for g in range(2):
-                second_product(acc[:, g, :], g, c)
-            nc.scalar.copy(res[:], acc[:])
-            nc.sync.dma_start(out_rows[:, :, chunks[c]], res[:])
-
-        def finish_wide(c, numbers, copies):
-            res = keep.tile([P, 2, 2 * P], F32, name="res%d" % c)
-            for g in range(2):
-                acc = bank(numbers[g], [2 * P])
-                second_product(acc[:], g, c)
-                copies[g](res[:, g, :], acc[:])
+                acc_out = bank((number + g) % 8, [width])
+                nc.tensor.matmul_mx(out=acc_out[:], lhsT=w2_codes[:, 2 * P * g : 2 * P * (g + 1)].bitcast(FP4X4),
+                                    lhsT_scale=w2_exp[:, P * g : P * (g + 1)],
+                                    rhs=codes[:].bitcast(FP8X4), rhs_scale=exps[:], start=True, stop=True)
+                if last and g == 0:
+                    nc.vector.tensor_copy(res[:, g, :], acc_out[:])
+                else:
+                    nc.scalar.copy(res[:, g, :], acc_out[:])
                 nc.sync.dma_start(out_rows[:, g, chunks[c]], res[:, g, :])
 
-        for c in (0, 1):
-            z_bf[c] = weave(chunks[c], "z_bf%d" % c)[:]
-        add_last(2)
-        for c in (0, 1):
-            values = z_bf[c].rearrange("p v u -> p (v u)").bitcast(BF16).rearrange("p (v t) -> p v t", t=PACK)
-            for at in range(chunks[c].start, chunks[c].stop, P):
-                here = at - chunks[c].start
-                nc.gpsimd.tensor_tensor(values[:, here : here + P, LAST], window[LAST][:, at : at + P],
-                                        s_plane[LAST][:, at : at + P], ADD)
-        z_bf[2] = weave(chunks[2], "z_bf2")[:]
-        for c in (3, 4):
-            add_last(c)
-            z_bf[c] = weave(chunks[c], "z_bf%d" % c)[:]
-
-        by_scalar = (nc.scalar.copy, nc.scalar.copy)
-        quantise_z(0)
-        quantise_z(2)
-        finish_narrow(0, 2)
-        quantise_z(1)
-        finish_narrow(2, 5)
-        quantise_z(3)
-        finish_wide(1, (3, 4), by_scalar)
-        quantise_z(4)
-        finish_wide(3, (0, 1), by_scalar)
-        finish_wide(4, (2, 3), (nc.vector.tensor_copy, nc.scalar.copy))
+        weave(0)
+        for c in range(1, len(chunks)):
+            weave(c)
+            finish(c - 1, 2 * (c - 1))
+        finish(len(chunks) - 1, 2 * (len(chunks) - 1))

@@ -1,6 +1,7 @@
 from contextlib import ExitStack
 
 import concourse.mybir as mybir
+from concourse.masks import make_identity
 
 K, T, S, H, N, U = 512, 2048, 512, 512, 256, 1024
 FLOPS = 2 * K * H * S + 2 * H * N * U
@@ -19,7 +20,8 @@ ADD = mybir.AluOpType.add
 P = 128
 PACK = 4
 PER_COLUMN = 16
-EDGES = (0, 256, 512, 768, U)
+WIDE = 256
+DIRECT = 3
 
 
 def tile_picked_unet_relu_e_kernel(tc, xT, w1, w2_words, w2_scales, skip, offs, cell, out):
@@ -34,9 +36,13 @@ def tile_picked_unet_relu_e_kernel(tc, xT, w1, w2_words, w2_scales, skip, offs, 
         offs_t = keep.tile([P, S // PER_COLUMN], U16, name="offs_t")
         cell_t = keep.tile([P, S // PER_COLUMN], U16, name="cell_t")
         x_rows = xT.rearrange("(p j) c -> j p c", j=PACK)
-        s_rows = skip.rearrange("(p t) c -> t p c", t=PACK)
         x_plane = [keep.tile([P, T], F32, name="x_plane%d" % j) for j in range(PACK)]
-        s_plane = [keep.tile([P, U], F32, name="s_plane%d" % t) for t in range(PACK)]
+        pairs = keep.tile([P, DIRECT * 2 * WIDE], F32, name="pairs")
+        pair_words = pairs[:].rearrange("p (c u v) -> p u c v", u=2, v=WIDE)
+        s_first = keep.tile([P, DIRECT, WIDE], F32, name="s_first")
+        s_high = [keep.tile([P, 2, WIDE], F32, name="s_high", tag="s_high%d" % c, align_bytes=64) for c in range(DIRECT)]
+        s_turn = keep.tile([P, PACK, WIDE], F32, name="s_turn")
+        s_cells = skip.rearrange("(p t) (c v) -> p t c v", t=PACK, v=WIDE)
         w_raw = keep.tile([P, PACK, H], F32, name="w_raw")
         w2_codes = keep.tile([P, 2 * N], U8, name="w2_codes", align_bytes=64)
         w2_exp = keep.tile([P, N], U8, name="w2_exp", align_bytes=64)
@@ -46,8 +52,11 @@ def tile_picked_unet_relu_e_kernel(tc, xT, w1, w2_words, w2_scales, skip, offs, 
         for j in range(PACK):
             nc.sync.dma_start(x_plane[j][:], x_rows[j])
         nc.sync.dma_start(cell_t[:], cell)
-        for t in range(PACK):
-            nc.sync.dma_start(s_plane[t][:], s_rows[t])
+        nc.sync.dma_start(s_turn[:], s_cells[:, :, DIRECT])
+        nc.sync.dma_start(s_first[:], s_cells[:, 0, :DIRECT])
+        nc.sync.dma_start(pair_words[:, 1], s_cells[:, 1, :DIRECT])
+        for c in range(DIRECT):
+            nc.sync.dma_start(s_high[c][:], s_cells[:, 2:, c])
         nc.sync.dma_start(w2_codes[:], w2_words[0])
         nc.vector.memset(w2_exp[:].bitcast(I32), 0)
         for q in range(4):
@@ -56,6 +65,8 @@ def tile_picked_unet_relu_e_kernel(tc, xT, w1, w2_words, w2_scales, skip, offs, 
         window = [keep.tile([P, U], F32, name="window%d" % t) for t in range(PACK)]
         for t in range(PACK):
             nc.vector.memset(window[t][:], 0.0)
+        ident = keep.tile([P, P], F32, name="ident")
+        make_identity(nc, ident[:])
 
         def quantise(codes, exps, values):
             nc.vector.quantize_mx(out=codes.bitcast(FP8X4), scales=exps, in_=values)
@@ -109,64 +120,88 @@ def tile_picked_unet_relu_e_kernel(tc, xT, w1, w2_words, w2_scales, skip, offs, 
         def scatter_vector(t, entries):
             nc.vector.tensor_copy(window[t][:].indirect(cell_t[:, columns(entries)]), hidden[t, entries.start][:])
 
-        order = ((0, first), (1, first), (0, second), (2, whole), (1, second), (3, first), (3, second))
-        acc = {(t, entries.start): product(t, entries, number) for number, (t, entries) in enumerate(order)}
+        back = bank(6, [2, WIDE])
+
+        def turn_pair(u, number, turned):
+            sums = bank(number, [2, 2, P])
+            terms = [(e, b, s_turn[:, 2 * u + e, P * b : P * (b + 1)]) for e in range(2) for b in range(2)]
+            terms += [(e, b, window[2 * u + e][:, DIRECT * WIDE + P * b : DIRECT * WIDE + P * (b + 1)]) for e in range(2) for b in range(2)]
+            for n, (e, b, term) in enumerate(terms):
+                nc.tensor.matmul(sums[:, b, e, :], term, ident[:], start=n == 0, stop=n == len(terms) - 1, is_transpose=True)
+            nc.scalar.copy(turned[:].bitcast(BF16).rearrange("p b (q e) -> p b q e", e=2), sums[:].rearrange("p b e q -> p b q e"))
+            for b in range(2):
+                nc.tensor.transpose(back[:, u, P * b : P * (b + 1)], turned[:, b, :], ident[:])
+
+        order = ((0, first, 0), (1, first, 1), (0, second, 2), (1, second, 4))
+        acc = {(t, entries.start): product(t, entries, number) for t, entries, number in order}
         relu_scalar(0, first, acc[0, 0])
         scatter_vector(0, first)
         relu_scalar(1, first, acc[1, 0])
         relu_scalar(0, second, acc[0, S // 2])
-        scatter_scalar(1, first)
-        relu_vector(2, whole, acc[2, 0])
+        relu_vector(1, second, acc[1, S // 2])
         scatter_vector(0, second)
-        relu_scalar(1, second, acc[1, S // 2])
+        scatter_scalar(1, first)
+        relu_scalar(2, first, product(2, first, 0))
         scatter_scalar(1, second)
-        relu_vector(3, first, acc[3, 0])
-        scatter_vector(2, whole)
+        relu_vector(3, first, product(3, first, 1))
+        scatter_vector(2, first)
+        relu_vector(2, second, product(2, second, 0))
+        relu_vector(3, second, product(3, second, 1))
         scatter_scalar(3, first)
-        relu_scalar(3, second, acc[3, S // 2])
+        turn_pair(0, 2, keep.tile([P, 2, P], F32, name="turned"))
+        scatter_vector(2, second)
         scatter_scalar(3, second)
 
-        chunks = [slice(lo, hi) for lo, hi in zip(EDGES, EDGES[1:])]
-        pairs = [keep.tile([P, 2, c.stop - c.start], F32, name="pairs%d" % c.start) for c in chunks]
-
-        def add_skip(engine, t, c):
-            values = pairs[c][:, t // 2].bitcast(BF16).rearrange("p (v e) -> p v e", e=2)[:, :, t % 2]
-            engine.tensor_tensor(values, window[t][:, chunks[c]], s_plane[t][:, chunks[c]], ADD)
-
-        for t in (0, 1):
-            for c in range(len(chunks)):
-                add_skip(nc.gpsimd, t, c)
+        pair_values = pairs[:].bitcast(BF16).rearrange("p (c u v e) -> p u e c v", u=2, v=WIDE, e=2)
+        by_chunk = [window[t][:].rearrange("p (c v) -> p c v", v=WIDE) for t in range(PACK)]
+        nc.gpsimd.tensor_tensor(pair_values[:, 0, 0], by_chunk[0][:, :DIRECT], s_first[:], ADD)
+        nc.gpsimd.tensor_tensor(pair_values[:, 0, 1], by_chunk[1][:, :DIRECT], pair_words[:, 1], ADD)
 
         out_rows = out.rearrange("(g p) v -> p g v", p=P)
         z_bf, z_mx = {}, {}
 
-        def weave(c):
-            width = chunks[c].stop - chunks[c].start
-            for t in (2, 3):
-                add_skip(nc.vector, t, c)
-            z_bf[c] = keep.tile([P, width, 2], F32, name="z_bf%d" % c, align_bytes=64)
-            nc.scalar.copy(z_bf[c][:], pairs[c][:].rearrange("p u v -> p v u"))
+        def add_skip(c, e):
+            nc.vector.tensor_tensor(pair_values[:, 1, e, c], by_chunk[2 + e][:, c], s_high[c][:, e], ADD)
 
-        def finish(c, number):
-            width = chunks[c].stop - chunks[c].start
-            codes = keep.tile([P, width], U32, name="z_codes%d" % c, align_bytes=64)
-            exps = keep.tile([P, width], U8, name="z_exp%d" % c, align_bytes=64)
+        def weave(c):
+            z_bf[c] = keep.tile([P, WIDE, 2], F32, name="z_bf%d" % c, align_bytes=64)
+            nc.scalar.copy(z_bf[c][:], pairs[:, 2 * WIDE * c : 2 * WIDE * (c + 1)].rearrange("p (u v) -> p v u", u=2))
+
+        def quantise_z(c):
+            codes = keep.tile([P, WIDE], U32, name="z_codes%d" % c, align_bytes=64)
+            exps = keep.tile([P, WIDE], U8, name="z_exp%d" % c, align_bytes=64)
             quantise(codes[:], exps[:], z_bf[c][:].rearrange("p v u -> p (v u)").bitcast(BF16))
-            last = c == len(chunks) - 1
-            res = keep.tile([P, 2, width], F32, name="res%d" % c)
+            z_mx[c] = codes, exps
+
+        def finish(c, number, copies):
+            codes, exps = z_mx[c]
+            res = keep.tile([P, 2, WIDE], F32, name="res%d" % c)
             for g in range(2):
-                acc_out = bank((number + g) % 8, [width])
+                acc_out = bank(number + g, [WIDE])
                 nc.tensor.matmul_mx(out=acc_out[:], lhsT=w2_codes[:, 2 * P * g : 2 * P * (g + 1)].bitcast(FP4X4),
                                     lhsT_scale=w2_exp[:, P * g : P * (g + 1)],
                                     rhs=codes[:].bitcast(FP8X4), rhs_scale=exps[:], start=True, stop=True)
-                if last and g == 0:
-                    nc.vector.tensor_copy(res[:, g, :], acc_out[:])
-                else:
-                    nc.scalar.copy(res[:, g, :], acc_out[:])
-                nc.sync.dma_start(out_rows[:, g, chunks[c]], res[:, g, :])
+                copies[g](res[:, g, :], acc_out[:])
+                nc.sync.dma_start(out_rows[:, g, WIDE * c : WIDE * (c + 1)], res[:, g, :])
 
+        by_scalar, by_vector = nc.scalar.copy, nc.vector.tensor_copy
+        add_skip(0, 0)
+        add_skip(0, 1)
         weave(0)
-        for c in range(1, len(chunks)):
-            weave(c)
-            finish(c - 1, 2 * (c - 1))
-        finish(len(chunks) - 1, 2 * (len(chunks) - 1))
+        turn_pair(1, 0, keep.tile([P, 2, P], F32, name="s_high", tag="s_high0", align_bytes=64))
+        add_skip(1, 0)
+        add_skip(1, 1)
+        weave(1)
+        quantise_z(0)
+        finish(0, 3, (by_scalar, by_scalar))
+        z_bf[DIRECT] = keep.tile([P, WIDE, 2], F32, name="z_turned", align_bytes=64)
+        nc.scalar.copy(z_bf[DIRECT][:], back[:].rearrange("p u v -> p v u"))
+        add_skip(2, 0)
+        add_skip(2, 1)
+        weave(2)
+        quantise_z(1)
+        finish(1, 1, (by_vector, by_vector))
+        quantise_z(DIRECT)
+        quantise_z(2)
+        finish(DIRECT, 3, (by_vector, by_scalar))
+        finish(2, 1, (by_vector, by_scalar))

@@ -105,7 +105,7 @@ def tile_picked_unet_relu_e_kernel(tc, xT, w1, w2_words, w2_scales, skip, offs, 
             cols = slice(P * t, P * (t + 1))
             nc.tensor.matmul_mx(out=acc[:], lhsT=w_codes[:, cols].bitcast(FP8X4), lhsT_scale=w_exp[:, cols],
                                 rhs=x_codes[:, entries].bitcast(FP8X4), rhs_scale=x_exp[:, entries], start=True, stop=True)
-            hidden[t, entries.start] = keep.tile([P, entries.stop - entries.start], F32, name="hidden%d_%d" % (t, entries.start))
+            hidden[t, entries.start] = keep.tile([P, entries.stop - entries.start], F32, name="hidden", tag="hidden%d_%d" % (t, entries.start))
             return acc
 
         def relu_scalar(t, entries, acc):
@@ -132,7 +132,7 @@ def tile_picked_unet_relu_e_kernel(tc, xT, w1, w2_words, w2_scales, skip, offs, 
             for b in range(2):
                 nc.tensor.transpose(back[:, u, P * b : P * (b + 1)], turned[:, b, :], ident[:])
 
-        order = ((0, first, 0), (1, first, 1), (0, second, 2), (1, second, 4))
+        order = ((0, first, 0), (1, first, 1), (0, second, 2), (1, second, 4), (2, second, 5))
         acc = {(t, entries.start): product(t, entries, number) for t, entries, number in order}
         relu_scalar(0, first, acc[0, 0])
         scatter_vector(0, first)
@@ -141,16 +141,16 @@ def tile_picked_unet_relu_e_kernel(tc, xT, w1, w2_words, w2_scales, skip, offs, 
         relu_vector(1, second, acc[1, S // 2])
         scatter_vector(0, second)
         scatter_scalar(1, first)
-        relu_scalar(2, first, product(2, first, 0))
+        relu_scalar(2, second, acc[2, S // 2])
         scatter_scalar(1, second)
+        relu_scalar(2, first, product(2, first, 0))
         relu_vector(3, first, product(3, first, 1))
-        scatter_vector(2, first)
-        relu_vector(2, second, product(2, second, 0))
+        scatter_vector(2, second)
         relu_vector(3, second, product(3, second, 1))
         scatter_scalar(3, first)
-        turn_pair(0, 2, keep.tile([P, 2, P], F32, name="turned"))
-        scatter_vector(2, second)
+        scatter_vector(2, first)
         scatter_scalar(3, second)
+        turn_pair(0, 2, keep.tile([P, 2, P], F32, name="hidden", tag="hidden3_256"))
 
         pair_values = pairs[:].bitcast(BF16).rearrange("p (c u v e) -> p u e c v", u=2, v=WIDE, e=2)
         by_chunk = [window[t][:].rearrange("p (c v) -> p c v", v=WIDE) for t in range(PACK)]
@@ -163,9 +163,9 @@ def tile_picked_unet_relu_e_kernel(tc, xT, w1, w2_words, w2_scales, skip, offs, 
         def add_skip(c, e):
             nc.vector.tensor_tensor(pair_values[:, 1, e, c], by_chunk[2 + e][:, c], s_high[c][:, e], ADD)
 
-        def weave(c):
+        def weave(c, copy):
             z_bf[c] = keep.tile([P, WIDE, 2], F32, name="z_bf%d" % c, align_bytes=64)
-            nc.scalar.copy(z_bf[c][:], pairs[:, 2 * WIDE * c : 2 * WIDE * (c + 1)].rearrange("p (u v) -> p v u", u=2))
+            copy(z_bf[c][:], pairs[:, 2 * WIDE * c : 2 * WIDE * (c + 1)].rearrange("p (u v) -> p v u", u=2))
 
         def quantise_z(c):
             codes = keep.tile([P, WIDE], U32, name="z_codes%d" % c, align_bytes=64)
@@ -173,11 +173,11 @@ def tile_picked_unet_relu_e_kernel(tc, xT, w1, w2_words, w2_scales, skip, offs, 
             quantise(codes[:], exps[:], z_bf[c][:].rearrange("p v u -> p (v u)").bitcast(BF16))
             z_mx[c] = codes, exps
 
-        def finish(c, number, copies):
+        def finish(c, numbers, copies):
             codes, exps = z_mx[c]
             res = keep.tile([P, 2, WIDE], F32, name="res%d" % c)
             for g in range(2):
-                acc_out = bank(number + g, [WIDE])
+                acc_out = bank(numbers[g], [WIDE])
                 nc.tensor.matmul_mx(out=acc_out[:], lhsT=w2_codes[:, 2 * P * g : 2 * P * (g + 1)].bitcast(FP4X4),
                                     lhsT_scale=w2_exp[:, P * g : P * (g + 1)],
                                     rhs=codes[:].bitcast(FP8X4), rhs_scale=exps[:], start=True, stop=True)
@@ -187,21 +187,21 @@ def tile_picked_unet_relu_e_kernel(tc, xT, w1, w2_words, w2_scales, skip, offs, 
         by_scalar, by_vector = nc.scalar.copy, nc.vector.tensor_copy
         add_skip(0, 0)
         add_skip(0, 1)
-        weave(0)
+        weave(0, by_scalar)
         turn_pair(1, 0, keep.tile([P, 2, P], F32, name="s_high", tag="s_high0", align_bytes=64))
         add_skip(1, 0)
         add_skip(1, 1)
-        weave(1)
+        weave(1, by_scalar)
         quantise_z(0)
-        finish(0, 3, (by_scalar, by_scalar))
+        finish(0, (3, 4), (by_scalar, by_scalar))
         z_bf[DIRECT] = keep.tile([P, WIDE, 2], F32, name="z_turned", align_bytes=64)
         nc.scalar.copy(z_bf[DIRECT][:], back[:].rearrange("p u v -> p v u"))
         add_skip(2, 0)
         add_skip(2, 1)
-        weave(2)
+        weave(2, by_scalar)
         quantise_z(1)
-        finish(1, 1, (by_vector, by_vector))
+        finish(1, (1, 2), (by_vector, by_vector))
         quantise_z(DIRECT)
         quantise_z(2)
-        finish(DIRECT, 3, (by_vector, by_scalar))
-        finish(2, 1, (by_vector, by_scalar))
+        finish(DIRECT, (5, 7), (by_vector, by_scalar))
+        finish(2, (0, 3), (by_vector, by_scalar))

@@ -20,6 +20,7 @@ ADD = mybir.AluOpType.add
 P = 128
 PACK = 4
 PER_COLUMN = 16
+HEAD = 128
 WIDE = 256
 DIRECT = 3
 
@@ -98,27 +99,26 @@ def tile_picked_unet_relu_e_kernel(tc, xT, w1, w2_words, w2_scales, skip, offs, 
         for half in (first, second):
             quantise(x_codes[:, half], x_exp[:, half], x_bf[:, half].rearrange("p n j -> p (n j)"))
 
-        hidden = {}
+        hidden = [keep.tile([P, S], F32, name="hidden", tag="hidden%d" % t) for t in range(PACK)]
 
         def product(t, entries, number):
             acc = bank(number, [entries.stop - entries.start])
             cols = slice(P * t, P * (t + 1))
             nc.tensor.matmul_mx(out=acc[:], lhsT=w_codes[:, cols].bitcast(FP8X4), lhsT_scale=w_exp[:, cols],
                                 rhs=x_codes[:, entries].bitcast(FP8X4), rhs_scale=x_exp[:, entries], start=True, stop=True)
-            hidden[t, entries.start] = keep.tile([P, entries.stop - entries.start], F32, name="hidden", tag="hidden%d_%d" % (t, entries.start))
             return acc
 
         def relu_scalar(t, entries, acc):
-            nc.scalar.activation(hidden[t, entries.start][:], acc[:], ACT.Relu)
+            nc.scalar.activation(hidden[t][:, entries], acc[:], ACT.Relu)
 
         def relu_vector(t, entries, acc):
-            nc.vector.tensor_scalar_max(hidden[t, entries.start][:], acc[:], 0.0)
+            nc.vector.tensor_scalar_max(hidden[t][:, entries], acc[:], 0.0)
 
         def scatter_scalar(t, entries):
-            nc.scalar.activation(window[t][:].indirect(cell_t[:, columns(entries)]), hidden[t, entries.start][:], ACT.Copy)
+            nc.scalar.activation(window[t][:].indirect(cell_t[:, columns(entries)]), hidden[t][:, entries], ACT.Copy)
 
         def scatter_vector(t, entries):
-            nc.vector.tensor_copy(window[t][:].indirect(cell_t[:, columns(entries)]), hidden[t, entries.start][:])
+            nc.vector.tensor_copy(window[t][:].indirect(cell_t[:, columns(entries)]), hidden[t][:, entries])
 
         back = bank(6, [2, WIDE])
 
@@ -132,7 +132,8 @@ def tile_picked_unet_relu_e_kernel(tc, xT, w1, w2_words, w2_scales, skip, offs, 
             for b in range(2):
                 nc.tensor.transpose(back[:, u, P * b : P * (b + 1)], turned[:, b, :], ident[:])
 
-        order = ((0, first, 0), (1, first, 1), (0, second, 2), (1, second, 4), (2, second, 5))
+        head, rest = slice(0, HEAD), slice(HEAD, S)
+        order = ((0, first, 0), (1, first, 1), (0, second, 2), (1, second, 4), (3, whole, 3), (2, whole, 5))
         acc = {(t, entries.start): product(t, entries, number) for t, entries, number in order}
         relu_scalar(0, first, acc[0, 0])
         scatter_vector(0, first)
@@ -141,16 +142,13 @@ def tile_picked_unet_relu_e_kernel(tc, xT, w1, w2_words, w2_scales, skip, offs, 
         relu_vector(1, second, acc[1, S // 2])
         scatter_vector(0, second)
         scatter_scalar(1, first)
-        relu_scalar(2, second, acc[2, S // 2])
+        relu_scalar(3, whole, acc[3, 0])
+        relu_scalar(2, whole, acc[2, 0])
         scatter_scalar(1, second)
-        relu_scalar(2, first, product(2, first, 0))
-        relu_vector(3, first, product(3, first, 1))
-        scatter_vector(2, second)
-        relu_vector(3, second, product(3, second, 1))
-        scatter_scalar(3, first)
-        scatter_vector(2, first)
-        scatter_scalar(3, second)
-        turn_pair(0, 2, keep.tile([P, 2, P], F32, name="hidden", tag="hidden3_256"))
+        scatter_vector(3, head)
+        scatter_vector(2, whole)
+        scatter_scalar(3, rest)
+        turn_pair(0, 2, keep.tile([P, 2, P], F32, name="hidden", tag="hidden3"))
 
         pair_values = pairs[:].bitcast(BF16).rearrange("p (c u v e) -> p u e c v", u=2, v=WIDE, e=2)
         by_chunk = [window[t][:].rearrange("p (c v) -> p c v", v=WIDE) for t in range(PACK)]
@@ -185,15 +183,15 @@ def tile_picked_unet_relu_e_kernel(tc, xT, w1, w2_words, w2_scales, skip, offs, 
                 nc.sync.dma_start(out_rows[:, g, WIDE * c : WIDE * (c + 1)], res[:, g, :])
 
         by_scalar, by_vector = nc.scalar.copy, nc.vector.tensor_copy
-        add_skip(0, 0)
         add_skip(0, 1)
+        add_skip(0, 0)
         weave(0, by_scalar)
-        turn_pair(1, 0, keep.tile([P, 2, P], F32, name="s_high", tag="s_high0", align_bytes=64))
+        turn_pair(1, 5, keep.tile([P, 2, P], F32, name="s_high", tag="s_high0", align_bytes=64))
         add_skip(1, 0)
         add_skip(1, 1)
         weave(1, by_scalar)
         quantise_z(0)
-        finish(0, (3, 4), (by_scalar, by_scalar))
+        finish(0, (7, 4), (by_scalar, by_scalar))
         z_bf[DIRECT] = keep.tile([P, WIDE, 2], F32, name="z_turned", align_bytes=64)
         nc.scalar.copy(z_bf[DIRECT][:], back[:].rearrange("p u v -> p v u"))
         add_skip(2, 0)
@@ -203,5 +201,5 @@ def tile_picked_unet_relu_e_kernel(tc, xT, w1, w2_words, w2_scales, skip, offs, 
         finish(1, (1, 2), (by_vector, by_vector))
         quantise_z(DIRECT)
         quantise_z(2)
-        finish(DIRECT, (5, 7), (by_vector, by_scalar))
-        finish(2, (0, 3), (by_vector, by_scalar))
+        finish(DIRECT, (0, 3), (by_vector, by_scalar))
+        finish(2, (5, 7), (by_vector, by_scalar))

@@ -79,7 +79,8 @@ def tile_picked_unet_relu_e_kernel(tc, xT, w1, w2_words, w2_scales, skip, offs, 
         quantise(w_codes[:], w_exp[:], w_bf[:].rearrange("p t m j -> p (t m j)"))
 
         x_bf = keep.tile([P, S, PACK], BF16, name="x_bf", align_bytes=64)
-        x_late = keep.tile([P, S // 2], BF16, name="x_late")
+        x_late = keep.tile([P, HEAD], BF16, name="x_late")
+        x_own = keep.tile([P, 2, HEAD], BF16, name="x_own")
         x_codes = keep.tile([P, S], U32, name="x_codes", align_bytes=64)
         x_exp = keep.tile([P, S], U8, name="x_exp", align_bytes=64)
         whole = slice(0, S)
@@ -91,11 +92,16 @@ def tile_picked_unet_relu_e_kernel(tc, xT, w1, w2_words, w2_scales, skip, offs, 
         def picked(j, entries):
             return x_plane[j][:].indirect(offs_t[:, columns(entries)])
 
-        for j in range(PACK - 1):
+        third, fourth = slice(S // 2, S - HEAD), slice(S - HEAD, S)
+        for j in range(2):
             nc.vector.tensor_copy(x_bf[:, whole, j], picked(j, whole))
-        nc.vector.tensor_copy(x_bf[:, first, PACK - 1], picked(PACK - 1, first))
-        nc.scalar.activation(x_late[:], picked(PACK - 1, second), ACT.Copy)
-        nc.vector.tensor_copy(x_bf[:, second, PACK - 1], x_late[:])
+        nc.vector.tensor_copy(x_bf[:, : fourth.start, 2], picked(2, slice(0, fourth.start)))
+        nc.scalar.activation(x_own[:, 0], picked(2, fourth), ACT.Copy)
+        nc.vector.tensor_copy(x_bf[:, first, 3], picked(3, first))
+        nc.scalar.activation(x_late[:], picked(3, third), ACT.Copy)
+        nc.scalar.activation(x_own[:, 1], picked(3, fourth), ACT.Copy)
+        nc.vector.tensor_copy(x_bf[:, third, 3], x_late[:])
+        nc.scalar.copy(x_bf[:, fourth, 2:], x_own[:].rearrange("p e n -> p n e"))
         for half in (first, second):
             quantise(x_codes[:, half], x_exp[:, half], x_bf[:, half].rearrange("p n j -> p (n j)"))
 

@@ -38,11 +38,12 @@ def tile_picked_unet_relu_e_kernel(tc, xT, w1, w2_words, w2_scales, skip, offs, 
         cell_t = keep.tile([P, S // PER_COLUMN], U16, name="cell_t")
         x_rows = xT.rearrange("(p j) c -> j p c", j=PACK)
         x_plane = [keep.tile([P, T], F32, name="x_plane%d" % j) for j in range(PACK)]
-        pairs = keep.tile([P, DIRECT * 2 * WIDE], F32, name="pairs")
-        pair_words = pairs[:].rearrange("p (c u v) -> p u c v", u=2, v=WIDE)
-        s_first = keep.tile([P, DIRECT, WIDE], F32, name="s_first")
+        near = DIRECT * WIDE
+        pairs = keep.tile([P, 2 * near], F32, name="pairs")
+        s_first = keep.tile([P, near], F32, name="s_first")
         s_high = [keep.tile([P, 2, WIDE], F32, name="s_high", tag="s_high%d" % c, align_bytes=64) for c in range(DIRECT)]
         s_turn = keep.tile([P, PACK, WIDE], F32, name="s_turn")
+        s_rows = skip.rearrange("(p t) c -> t p c", t=PACK)
         s_cells = skip.rearrange("(p t) (c v) -> p t c v", t=PACK, v=WIDE)
         w_raw = keep.tile([P, PACK, H], F32, name="w_raw")
         w2_codes = keep.tile([P, 2 * N], U8, name="w2_codes", align_bytes=64)
@@ -54,8 +55,8 @@ def tile_picked_unet_relu_e_kernel(tc, xT, w1, w2_words, w2_scales, skip, offs, 
             nc.sync.dma_start(x_plane[j][:], x_rows[j])
         nc.sync.dma_start(cell_t[:], cell)
         nc.sync.dma_start(s_turn[:], s_cells[:, :, DIRECT])
-        nc.sync.dma_start(s_first[:], s_cells[:, 0, :DIRECT])
-        nc.sync.dma_start(pair_words[:, 1], s_cells[:, 1, :DIRECT])
+        nc.sync.dma_start(s_first[:], s_rows[0][:, :near])
+        nc.sync.dma_start(pairs[:, near:], s_rows[1][:, :near])
         for c in range(DIRECT):
             nc.sync.dma_start(s_high[c][:], s_cells[:, 2:, c])
         nc.sync.dma_start(w2_codes[:], w2_words[0])
@@ -156,20 +157,22 @@ def tile_picked_unet_relu_e_kernel(tc, xT, w1, w2_words, w2_scales, skip, offs, 
         scatter_scalar(3, rest)
         turn_pair(0, 2, keep.tile([P, 2, P], F32, name="hidden", tag="hidden3"))
 
-        pair_values = pairs[:].bitcast(BF16).rearrange("p (c u v e) -> p u e c v", u=2, v=WIDE, e=2)
-        by_chunk = [window[t][:].rearrange("p (c v) -> p c v", v=WIDE) for t in range(PACK)]
-        nc.gpsimd.tensor_tensor(pair_values[:, 0, 0], by_chunk[0][:, :DIRECT], s_first[:], ADD)
-        nc.gpsimd.tensor_tensor(pair_values[:, 0, 1], by_chunk[1][:, :DIRECT], pair_words[:, 1], ADD)
+        pair_values = pairs[:].bitcast(BF16).rearrange("p (v e) -> p e v", e=2)
+        nc.gpsimd.tensor_tensor(pair_values[:, 0, :near], window[0][:, :near], s_first[:], ADD)
+        nc.gpsimd.tensor_tensor(pair_values[:, 1, :near], window[1][:, :near], pairs[:, near:], ADD)
+        high_at = [near + WIDE * (c % 2) for c in range(DIRECT)]
 
         out_rows = out.rearrange("(g p) v -> p g v", p=P)
         z_bf, z_mx = {}, {}
 
         def add_skip(c, e):
-            nc.vector.tensor_tensor(pair_values[:, 1, e, c], by_chunk[2 + e][:, c], s_high[c][:, e], ADD)
+            nc.vector.tensor_tensor(pair_values[:, e, high_at[c] : high_at[c] + WIDE], window[2 + e][:, WIDE * c : WIDE * (c + 1)], s_high[c][:, e], ADD)
 
         def weave(c, copy):
             z_bf[c] = keep.tile([P, WIDE, 2], F32, name="z_bf%d" % c, align_bytes=64)
-            copy(z_bf[c][:], pairs[:, 2 * WIDE * c : 2 * WIDE * (c + 1)].rearrange("p (u v) -> p v u", u=2))
+            slots = pairs[:].rearrange("p (s v) -> p v s", v=WIDE)
+            step = high_at[c] // WIDE - c
+            copy(z_bf[c][:], slots[:, :, c : c + step + 1 : step])
 
         def quantise_z(c):
             codes = keep.tile([P, WIDE], U32, name="z_codes%d" % c, align_bytes=64)
@@ -197,15 +200,15 @@ def tile_picked_unet_relu_e_kernel(tc, xT, w1, w2_words, w2_scales, skip, offs, 
         add_skip(1, 1)
         weave(1, by_scalar)
         quantise_z(0)
-        finish(0, (7, 4), (by_scalar, by_scalar))
-        z_bf[DIRECT] = keep.tile([P, WIDE, 2], F32, name="z_turned", align_bytes=64)
-        nc.scalar.copy(z_bf[DIRECT][:], back[:].rearrange("p u v -> p v u"))
         add_skip(2, 0)
         add_skip(2, 1)
-        weave(2, by_scalar)
+        finish(0, (7, 4), (by_scalar, by_scalar))
         quantise_z(1)
-        finish(1, (1, 2), (by_vector, by_vector))
+        z_bf[DIRECT] = keep.tile([P, WIDE, 2], F32, name="z_turned", align_bytes=64)
+        nc.scalar.copy(z_bf[DIRECT][:], back[:].rearrange("p u v -> p v u"))
+        weave(2, by_vector)
         quantise_z(DIRECT)
         quantise_z(2)
+        finish(1, (1, 2), (by_scalar, by_scalar))
         finish(DIRECT, (0, 3), (by_vector, by_scalar))
         finish(2, (5, 7), (by_vector, by_scalar))

@@ -106,7 +106,7 @@ def tile_picked_unet_relu_e_kernel(tc, xT, w1, w2_words, w2_scales, skip, offs, 
         for half in (first, second):
             quantise(x_codes[:, half], x_exp[:, half], x_bf[:, half].rearrange("p n j -> p (n j)"))
 
-        hidden = [keep.tile([P, S], F32, name="hidden", tag="hidden%d" % t) for t in range(PACK)]
+        hidden = [keep.tile([P, S], F32, name="hidden", tag="hidden%d" % t, align_bytes=64) for t in range(PACK)]
 
         def product(t, entries, number):
             acc = bank(number, [entries.stop - entries.start])
@@ -129,15 +129,20 @@ def tile_picked_unet_relu_e_kernel(tc, xT, w1, w2_words, w2_scales, skip, offs, 
 
         back = bank(6, [2, WIDE])
 
-        def turn_pair(u, number, turned):
-            sums = bank(number, [2, 2, P])
-            terms = [(e, b, s_turn[:, 2 * u + e, P * b : P * (b + 1)]) for e in range(2) for b in range(2)]
-            terms += [(e, b, window[2 * u + e][:, DIRECT * WIDE + P * b : DIRECT * WIDE + P * (b + 1)]) for e in range(2) for b in range(2)]
+        def turn_pair(u, blocks, number):
+            parts = [(e, b) for e in (1, 0) for b in range(blocks.start, blocks.stop)]
+            sums = bank(number, [blocks.stop - blocks.start, 2, P])
+            terms = [(e, b, s_turn[:, 2 * u + e, P * b : P * (b + 1)]) for e, b in parts]
+            terms += [(e, b, window[2 * u + e][:, near + P * b : near + P * (b + 1)]) for e, b in (parts if u else parts[::-1])]
             for n, (e, b, term) in enumerate(terms):
-                nc.tensor.matmul(sums[:, b, e, :], term, ident[:], start=n == 0, stop=n == len(terms) - 1, is_transpose=True)
+                nc.tensor.matmul(sums[:, b - blocks.start, e, :], term, ident[:], start=n == 0, stop=n == len(terms) - 1, is_transpose=True)
+            return sums
+
+        def turn_back(u, blocks, sums, tag):
+            turned = keep.tile([P, blocks.stop - blocks.start, P], F32, name="turned", tag=tag, align_bytes=64)
             nc.scalar.copy(turned[:].bitcast(BF16).rearrange("p b (q e) -> p b q e", e=2), sums[:].rearrange("p b e q -> p b q e"))
-            for b in range(2):
-                nc.tensor.transpose(back[:, u, P * b : P * (b + 1)], turned[:, b, :], ident[:])
+            for b in range(blocks.start, blocks.stop):
+                nc.tensor.transpose(back[:, u, P * b : P * (b + 1)], turned[:, b - blocks.start, :], ident[:])
 
         head, rest = slice(0, HEAD), slice(HEAD, S)
         order = ((0, first, 0), (1, first, 1), (0, second, 2), (1, second, 4), (3, whole, 3), (2, whole, 5))
@@ -155,7 +160,9 @@ def tile_picked_unet_relu_e_kernel(tc, xT, w1, w2_words, w2_scales, skip, offs, 
         scatter_vector(3, head)
         scatter_vector(2, whole)
         scatter_scalar(3, rest)
-        turn_pair(0, 2, keep.tile([P, 2, P], F32, name="hidden", tag="hidden3"))
+        turn_back(0, slice(0, 2), turn_pair(0, slice(0, 2), 2), "hidden3")
+        sums_high = [turn_pair(1, slice(b, b + 1), number) for b, number in enumerate((5, 3))]
+        turn_back(1, slice(0, 1), sums_high[0], "turned")
 
         pair_values = pairs[:].bitcast(BF16).rearrange("p (v e) -> p e v", e=2)
         nc.gpsimd.tensor_tensor(pair_values[:, 0, :near], window[0][:, :near], s_first[:], ADD)
@@ -195,7 +202,7 @@ def tile_picked_unet_relu_e_kernel(tc, xT, w1, w2_words, w2_scales, skip, offs, 
         add_skip(0, 1)
         add_skip(0, 0)
         weave(0, by_scalar)
-        turn_pair(1, 5, keep.tile([P, 2, P], F32, name="s_high", tag="s_high0", align_bytes=64))
+        turn_back(1, slice(1, 2), sums_high[1], "s_high0")
         add_skip(1, 0)
         add_skip(1, 1)
         weave(1, by_scalar)

@@ -45,14 +45,17 @@ def tile_picked_unet_relu_e_kernel(tc, xT, w1, w2_words, w2_scales, skip, offs, 
         s_turn = keep.tile([P, PACK, WIDE], F32, name="s_turn")
         s_rows = skip.rearrange("(p t) c -> t p c", t=PACK)
         s_cells = skip.rearrange("(p t) (c v) -> p t c v", t=PACK, v=WIDE)
-        w_raw = keep.tile([P, PACK, H], F32, name="w_raw")
+        w_rows = w1.rearrange("(p j) c -> p j c", j=PACK)
+        w_early = keep.tile([P, 2, H], F32, name="w_early")
+        w_late = keep.tile([P, 2, H], F32, name="w_late", tag="w_late", align_bytes=64)
         w2_codes = keep.tile([P, 2 * N], U8, name="w2_codes", align_bytes=64)
         w2_exp = keep.tile([P, N], U8, name="w2_exp", align_bytes=64)
 
-        nc.sync.dma_start(w_raw[:], w1.rearrange("(p j) c -> p j c", j=PACK))
+        nc.sync.dma_start(w_early[:], w_rows[:, :2])
         nc.sync.dma_start(offs_t[:], offs)
         for j in range(PACK):
             nc.sync.dma_start(x_plane[j][:], x_rows[j])
+        nc.sync.dma_start(w_late[:], w_rows[:, 2:])
         nc.sync.dma_start(cell_t[:], cell)
         nc.sync.dma_start(s_turn[:], s_cells[:, :, DIRECT])
         nc.sync.dma_start(s_first[:], s_rows[0][:, :near])
@@ -73,19 +76,22 @@ def tile_picked_unet_relu_e_kernel(tc, xT, w1, w2_words, w2_scales, skip, offs, 
         def quantise(codes, exps, values):
             nc.vector.quantize_mx(out=codes.bitcast(FP8X4), scales=exps, in_=values)
 
-        w_bf = keep.tile([P, PACK, P, PACK], BF16, name="w_bf", align_bytes=64)
-        w_codes = keep.tile([P, H], U32, name="w_codes", align_bytes=64)
-        w_exp = keep.tile([P, H], U8, name="w_exp", align_bytes=64)
-        nc.scalar.activation(w_bf[:].rearrange("p t m j -> p m j t"), w_raw[:].rearrange("p j (m t) -> p m j t", t=PACK), ACT.Copy)
-        quantise(w_codes[:], w_exp[:], w_bf[:].rearrange("p t m j -> p (t m j)"))
-
-        x_bf = keep.tile([P, S, PACK], BF16, name="x_bf", align_bytes=64)
-        x_late = keep.tile([P, HEAD], BF16, name="x_late")
-        x_own = keep.tile([P, 2, HEAD], BF16, name="x_own")
-        x_codes = keep.tile([P, S], U32, name="x_codes", align_bytes=64)
-        x_exp = keep.tile([P, S], U8, name="x_exp", align_bytes=64)
         whole = slice(0, S)
         first, second = slice(0, S // 2), slice(S // 2, S)
+        groups = (slice(0, 1), slice(1, 2), slice(2, 4))
+        w_bf = [keep.tile([P, g.stop - g.start, P, PACK], BF16, name="w_bf%d" % g.start, align_bytes=64) for g in groups]
+        w_codes = [keep.tile([P, g.stop - g.start, P], U32, name="w_codes%d" % g.start, align_bytes=64) for g in groups]
+        w_exp = [keep.tile([P, g.stop - g.start, P], U8, name="w_exp%d" % g.start, align_bytes=64) for g in groups]
+
+        def dealt(n, raw, slots):
+            return w_bf[n][:, :, :, slots].rearrange("p t m e -> p m e t"), raw[:].rearrange("p e (m t) -> p m e t", t=PACK)[:, :, :, groups[n]]
+
+        def quantise_w(n):
+            quantise(w_codes[n][:].rearrange("p t m -> p (t m)"), w_exp[n][:].rearrange("p t m -> p (t m)"),
+                     w_bf[n][:].rearrange("p t m j -> p (t m j)"))
+
+        for n in range(len(groups)):
+            nc.scalar.activation(*dealt(n, w_early, slice(0, 2)), ACT.Copy)
 
         def columns(entries):
             return slice(entries.start // PER_COLUMN, entries.stop // PER_COLUMN)
@@ -93,26 +99,37 @@ def tile_picked_unet_relu_e_kernel(tc, xT, w1, w2_words, w2_scales, skip, offs, 
         def picked(j, entries):
             return x_plane[j][:].indirect(offs_t[:, columns(entries)])
 
-        third, fourth = slice(S // 2, S - HEAD), slice(S - HEAD, S)
+        x_bf = [keep.tile([P, S // 2, PACK], BF16, name="x_bf%d" % n, align_bytes=64) for n in range(2)]
+        x_own = keep.tile([P, 2, S // 2], BF16, name="x_own")
+        x_exp = [keep.tile([P, S // 2], U8, name="x_exp%d" % n, align_bytes=64) for n in range(2)]
         for j in range(2):
-            nc.vector.tensor_copy(x_bf[:, whole, j], picked(j, whole))
-        nc.vector.tensor_copy(x_bf[:, : fourth.start, 2], picked(2, slice(0, fourth.start)))
-        nc.scalar.activation(x_own[:, 0], picked(2, fourth), ACT.Copy)
-        nc.vector.tensor_copy(x_bf[:, first, 3], picked(3, first))
-        nc.scalar.activation(x_late[:], picked(3, third), ACT.Copy)
-        nc.scalar.activation(x_own[:, 1], picked(3, fourth), ACT.Copy)
-        nc.vector.tensor_copy(x_bf[:, third, 3], x_late[:])
-        nc.scalar.copy(x_bf[:, fourth, 2:], x_own[:].rearrange("p e n -> p n e"))
-        for half in (first, second):
-            quantise(x_codes[:, half], x_exp[:, half], x_bf[:, half].rearrange("p n j -> p (n j)"))
+            nc.vector.tensor_copy(x_bf[0][:, :, j], picked(j, first))
+            nc.vector.tensor_copy(x_bf[1][:, :, j], picked(j, second))
+        for j in range(2, PACK):
+            nc.vector.tensor_copy(x_bf[0][:, :, j], picked(j, first))
+            nc.scalar.activation(x_own[:, j - 2], picked(j, second), ACT.Copy)
+        nc.scalar.copy(x_bf[1][:, :, 2:], x_own[:].rearrange("p e n -> p n e"))
+        x_codes = [keep.tile([P, S // 2], U32, name="x_codes0", align_bytes=64)]
+        quantise(x_codes[0][:], x_exp[0][:], x_bf[0][:].rearrange("p n j -> p (n j)"))
+        for n in range(2):
+            nc.vector.tensor_copy(*dealt(n, w_late, slice(2, 4)))
+        nc.scalar.copy(*dealt(2, w_late, slice(2, 4)))
+        quantise_w(0)
+        quantise_w(1)
+        x_codes.append(keep.tile([P, S // 2], U32, name="x_codes1", tag="w_late", align_bytes=64))
+        quantise(x_codes[1][:], x_exp[1][:], x_bf[1][:].rearrange("p n j -> p (n j)"))
+        quantise_w(2)
 
         hidden = [keep.tile([P, S], F32, name="hidden", tag="hidden%d" % t, align_bytes=64) for t in range(PACK)]
 
         def product(t, entries, number):
             acc = bank(number, [entries.stop - entries.start])
-            cols = slice(P * t, P * (t + 1))
-            nc.tensor.matmul_mx(out=acc[:], lhsT=w_codes[:, cols].bitcast(FP8X4), lhsT_scale=w_exp[:, cols],
-                                rhs=x_codes[:, entries].bitcast(FP8X4), rhs_scale=x_exp[:, entries], start=True, stop=True)
+            n = min(t, 2)
+            for start in range(entries.start, entries.stop, S // 2):
+                half = start // (S // 2)
+                nc.tensor.matmul_mx(out=acc[:, start - entries.start : start - entries.start + S // 2],
+                                    lhsT=w_codes[n][:, t - n].bitcast(FP8X4), lhsT_scale=w_exp[n][:, t - n],
+                                    rhs=x_codes[half][:].bitcast(FP8X4), rhs_scale=x_exp[half][:], start=True, stop=True)
             return acc
 
         def relu_scalar(t, entries, acc):

@@ -78,17 +78,17 @@ def tile_picked_unet_relu_e_kernel(tc, xT, w1, w2_words, w2_scales, skip, offs, 
 
         whole = slice(0, S)
         first, second = slice(0, S // 2), slice(S // 2, S)
-        groups = (slice(0, 1), slice(1, 2), slice(2, 4))
+        groups = (slice(0, 2), slice(2, 4))
         w_bf = [keep.tile([P, g.stop - g.start, P, PACK], BF16, name="w_bf%d" % g.start, align_bytes=64) for g in groups]
         w_codes = [keep.tile([P, g.stop - g.start, P], U32, name="w_codes%d" % g.start, align_bytes=64) for g in groups]
         w_exp = [keep.tile([P, g.stop - g.start, P], U8, name="w_exp%d" % g.start, align_bytes=64) for g in groups]
 
         def dealt(n, raw, slots):
-            return w_bf[n][:, :, :, slots].rearrange("p t m e -> p m e t"), raw[:].rearrange("p e (m t) -> p m e t", t=PACK)[:, :, :, groups[n]]
+            return w_bf[n][:, :, :, slots].rearrange("p t m e -> p m t e"), raw[:].rearrange("p e (m t) -> p m t e", t=PACK)[:, :, groups[n]]
 
-        def quantise_w(n):
-            quantise(w_codes[n][:].rearrange("p t m -> p (t m)"), w_exp[n][:].rearrange("p t m -> p (t m)"),
-                     w_bf[n][:].rearrange("p t m j -> p (t m j)"))
+        def quantise_w(n, planes):
+            quantise(w_codes[n][:, planes].rearrange("p t m -> p (t m)"), w_exp[n][:, planes].rearrange("p t m -> p (t m)"),
+                     w_bf[n][:, planes].rearrange("p t m j -> p (t m j)"))
 
         for n in range(len(groups)):
             nc.scalar.activation(*dealt(n, w_early, slice(0, 2)), ACT.Copy)
@@ -99,36 +99,39 @@ def tile_picked_unet_relu_e_kernel(tc, xT, w1, w2_words, w2_scales, skip, offs, 
         def picked(j, entries):
             return x_plane[j][:].indirect(offs_t[:, columns(entries)])
 
-        x_bf = [keep.tile([P, S // 2, PACK], BF16, name="x_bf%d" % n, align_bytes=64) for n in range(2)]
-        x_own = keep.tile([P, 2, S // 2], BF16, name="x_own")
+        x_bf = keep.tile([P, S, PACK], BF16, name="x_bf", align_bytes=64)
+        x_late = keep.tile([P, HEAD], BF16, name="x_late")
+        x_own = keep.tile([P, 2, HEAD], BF16, name="x_own")
         x_exp = [keep.tile([P, S // 2], U8, name="x_exp%d" % n, align_bytes=64) for n in range(2)]
+        third, fourth = slice(S // 2, S - HEAD), slice(S - HEAD, S)
         for j in range(2):
-            nc.vector.tensor_copy(x_bf[0][:, :, j], picked(j, first))
-            nc.vector.tensor_copy(x_bf[1][:, :, j], picked(j, second))
-        for j in range(2, PACK):
-            nc.vector.tensor_copy(x_bf[0][:, :, j], picked(j, first))
-            nc.scalar.activation(x_own[:, j - 2], picked(j, second), ACT.Copy)
-        nc.scalar.copy(x_bf[1][:, :, 2:], x_own[:].rearrange("p e n -> p n e"))
+            nc.vector.tensor_copy(x_bf[:, whole, j], picked(j, whole))
+        nc.vector.tensor_copy(x_bf[:, : fourth.start, 2], picked(2, slice(0, fourth.start)))
+        nc.scalar.activation(x_own[:, 0], picked(2, fourth), ACT.Copy)
+        nc.vector.tensor_copy(x_bf[:, first, 3], picked(3, first))
+        nc.scalar.activation(x_late[:], picked(3, third), ACT.Copy)
+        nc.scalar.activation(x_own[:, 1], picked(3, fourth), ACT.Copy)
+        nc.vector.tensor_copy(x_bf[:, third, 3], x_late[:])
+        nc.scalar.copy(x_bf[:, fourth, 2:], x_own[:].rearrange("p e n -> p n e"))
         x_codes = [keep.tile([P, S // 2], U32, name="x_codes0", align_bytes=64)]
-        quantise(x_codes[0][:], x_exp[0][:], x_bf[0][:].rearrange("p n j -> p (n j)"))
-        for n in range(2):
-            nc.vector.tensor_copy(*dealt(n, w_late, slice(2, 4)))
-        nc.scalar.copy(*dealt(2, w_late, slice(2, 4)))
-        quantise_w(0)
-        quantise_w(1)
+        quantise(x_codes[0][:], x_exp[0][:], x_bf[:, first].rearrange("p n j -> p (n j)"))
+        nc.vector.tensor_copy(*dealt(0, w_late, slice(2, 4)))
+        nc.scalar.copy(*dealt(1, w_late, slice(2, 4)))
+        quantise_w(0, slice(0, 1))
+        quantise_w(0, slice(1, 2))
         x_codes.append(keep.tile([P, S // 2], U32, name="x_codes1", tag="w_late", align_bytes=64))
-        quantise(x_codes[1][:], x_exp[1][:], x_bf[1][:].rearrange("p n j -> p (n j)"))
-        quantise_w(2)
+        quantise(x_codes[1][:], x_exp[1][:], x_bf[:, second].rearrange("p n j -> p (n j)"))
+        quantise_w(1, slice(0, 2))
 
         hidden = [keep.tile([P, S], F32, name="hidden", tag="hidden%d" % t, align_bytes=64) for t in range(PACK)]
 
         def product(t, entries, number):
             acc = bank(number, [entries.stop - entries.start])
-            n = min(t, 2)
+            n = t // 2
             for start in range(entries.start, entries.stop, S // 2):
                 half = start // (S // 2)
                 nc.tensor.matmul_mx(out=acc[:, start - entries.start : start - entries.start + S // 2],
-                                    lhsT=w_codes[n][:, t - n].bitcast(FP8X4), lhsT_scale=w_exp[n][:, t - n],
+                                    lhsT=w_codes[n][:, t % 2].bitcast(FP8X4), lhsT_scale=w_exp[n][:, t % 2],
                                     rhs=x_codes[half][:].bitcast(FP8X4), rhs_scale=x_exp[half][:], start=True, stop=True)
             return acc
 

@@ -46,16 +46,16 @@ def tile_picked_unet_relu_e_kernel(tc, xT, w1, w2_words, w2_scales, skip, offs, 
         s_rows = skip.rearrange("(p t) c -> t p c", t=PACK)
         s_cells = skip.rearrange("(p t) (c v) -> p t c v", t=PACK, v=WIDE)
         w_rows = w1.rearrange("(p j) c -> p j c", j=PACK)
-        w_early = keep.tile([P, 2, H], F32, name="w_early")
-        w_late = keep.tile([P, 2, H], F32, name="w_late", tag="w_late", align_bytes=64)
+        w_early = keep.tile([P, 1, H], F32, name="w_early")
+        w_late = keep.tile([P, PACK - 1, H], F32, name="w_late", tag="w_late", align_bytes=64)
         w2_codes = keep.tile([P, 2 * N], U8, name="w2_codes", align_bytes=64)
         w2_exp = keep.tile([P, N], U8, name="w2_exp", align_bytes=64)
 
-        nc.sync.dma_start(w_early[:], w_rows[:, :2])
+        nc.sync.dma_start(w_early[:], w_rows[:, :1])
         nc.sync.dma_start(offs_t[:], offs)
         for j in range(PACK):
             nc.sync.dma_start(x_plane[j][:], x_rows[j])
-        nc.sync.dma_start(w_late[:], w_rows[:, 2:])
+        nc.sync.dma_start(w_late[:], w_rows[:, 1:])
         nc.sync.dma_start(cell_t[:], cell)
         nc.sync.dma_start(s_turn[:], s_cells[:, :, DIRECT])
         nc.sync.dma_start(s_first[:], s_rows[0][:, :near])
@@ -91,7 +91,7 @@ def tile_picked_unet_relu_e_kernel(tc, xT, w1, w2_words, w2_scales, skip, offs, 
                      w_bf[n][:, planes].rearrange("p t m j -> p (t m j)"))
 
         for n in range(len(groups)):
-            nc.scalar.activation(*dealt(n, w_early, slice(0, 2)), ACT.Copy)
+            nc.scalar.activation(*dealt(n, w_early, slice(0, 1)), ACT.Copy)
 
         def columns(entries):
             return slice(entries.start // PER_COLUMN, entries.stop // PER_COLUMN)
@@ -115,8 +115,8 @@ def tile_picked_unet_relu_e_kernel(tc, xT, w1, w2_words, w2_scales, skip, offs, 
         nc.scalar.copy(x_bf[:, fourth, 2:], x_own[:].rearrange("p e n -> p n e"))
         x_codes = [keep.tile([P, S // 2], U32, name="x_codes0", align_bytes=64)]
         quantise(x_codes[0][:], x_exp[0][:], x_bf[:, first].rearrange("p n j -> p (n j)"))
-        nc.vector.tensor_copy(*dealt(0, w_late, slice(2, 4)))
-        nc.scalar.copy(*dealt(1, w_late, slice(2, 4)))
+        nc.vector.tensor_copy(*dealt(0, w_late, slice(1, PACK)))
+        nc.scalar.copy(*dealt(1, w_late, slice(1, PACK)))
         quantise_w(0, slice(0, 1))
         quantise_w(0, slice(1, 2))
         x_codes.append(keep.tile([P, S // 2], U32, name="x_codes1", tag="w_late", align_bytes=64))

@@ -21,6 +21,9 @@ P = 128
 PACK = 4
 PER_COLUMN = 16
 HEAD = 128
+OPEN = 320
+LEAD = 288
+SHARE = 160
 WIDE = 256
 DIRECT = 3
 
@@ -125,21 +128,14 @@ def tile_picked_unet_relu_e_kernel(tc, xT, w1, w2_words, w2_scales, skip, offs, 
 
         hidden = [keep.tile([P, S], F32, name="hidden", tag="hidden%d" % t, align_bytes=64) for t in range(PACK)]
 
-        def product(t, entries, number):
-            acc = bank(number, [entries.stop - entries.start])
-            n = t // 2
-            for start in range(entries.start, entries.stop, S // 2):
-                half = start // (S // 2)
-                nc.tensor.matmul_mx(out=acc[:, start - entries.start : start - entries.start + S // 2],
-                                    lhsT=w_codes[n][:, t % 2].bitcast(FP8X4), lhsT_scale=w_exp[n][:, t % 2],
-                                    rhs=x_codes[half][:].bitcast(FP8X4), rhs_scale=x_exp[half][:], start=True, stop=True)
-            return acc
+        def product(acc, t, entries):
+            n = entries.start // (S // 2)
+            part = slice(entries.start - n * (S // 2), entries.stop - n * (S // 2))
+            nc.tensor.matmul_mx(out=acc, lhsT=w_codes[t // 2][:, t % 2].bitcast(FP8X4), lhsT_scale=w_exp[t // 2][:, t % 2],
+                                rhs=x_codes[n][:, part].bitcast(FP8X4), rhs_scale=x_exp[n][:, part], start=True, stop=True)
 
         def relu_scalar(t, entries, acc):
-            nc.scalar.activation(hidden[t][:, entries], acc[:], ACT.Relu)
-
-        def relu_vector(t, entries, acc):
-            nc.vector.tensor_scalar_max(hidden[t][:, entries], acc[:], 0.0)
+            nc.scalar.activation(hidden[t][:, entries], acc, ACT.Relu)
 
         def scatter_scalar(t, entries):
             nc.scalar.activation(window[t][:].indirect(cell_t[:, columns(entries)]), hidden[t][:, entries], ACT.Copy)
@@ -165,21 +161,34 @@ def tile_picked_unet_relu_e_kernel(tc, xT, w1, w2_words, w2_scales, skip, offs, 
                 nc.tensor.transpose(back[:, u, P * b : P * (b + 1)], turned[:, b - blocks.start, :], ident[:])
 
         head, rest = slice(0, HEAD), slice(HEAD, S)
-        order = ((0, first, 0), (1, first, 1), (0, second, 2), (1, second, 4), (3, whole, 3), (2, whole, 5))
-        acc = {(t, entries.start): product(t, entries, number) for t, entries, number in order}
-        relu_scalar(0, first, acc[0, 0])
-        scatter_vector(0, first)
-        relu_scalar(1, first, acc[1, 0])
-        relu_scalar(0, second, acc[0, S // 2])
-        relu_vector(1, second, acc[1, S // 2])
-        scatter_vector(0, second)
-        scatter_scalar(1, first)
-        relu_scalar(3, whole, acc[3, 0])
-        relu_scalar(2, whole, acc[2, 0])
-        scatter_scalar(1, second)
-        scatter_vector(3, head)
+        acc = bank(0, [HEAD])
+        product(acc[:], 0, head)
+        relu_scalar(0, head, acc[:])
+        scatter_vector(0, head)
+        acc = bank(1, [S // 2])
+        product(acc[:], 1, first)
+        relu_scalar(1, first, acc[:])
+        acc0, acc1 = bank(2, [S - HEAD]), bank(4, [OPEN - S // 2])
+        product(acc0[:, :HEAD], 0, slice(HEAD, S // 2))
+        product(acc1[:], 1, slice(S // 2, OPEN))
+        product(acc0[:, HEAD:], 0, second)
+        relu_scalar(1, slice(S // 2, OPEN), acc1[:])
+        relu_scalar(0, rest, acc0[:])
+        acc = bank(0, [S - OPEN])
+        product(acc[:, : fourth.start - OPEN], 1, slice(OPEN, fourth.start))
+        product(acc[:, fourth.start - OPEN :], 1, fourth)
+        nc.vector.tensor_scalar_max(hidden[1][:, OPEN:], acc[:], 0.0)
+        scatter_vector(0, rest)
+        scatter_scalar(1, slice(0, LEAD))
+        for t, number in ((3, 3), (2, 5)):
+            acc = bank(number, [S])
+            for part in (first, second):
+                product(acc[:, part], t, part)
+            relu_scalar(t, whole, acc[:])
+        scatter_scalar(1, slice(LEAD, S))
+        scatter_vector(3, slice(0, SHARE))
         scatter_vector(2, whole)
-        scatter_scalar(3, rest)
+        scatter_scalar(3, slice(SHARE, S))
         turn_back(0, slice(0, 2), turn_pair(0, slice(0, 2), 2), "hidden3")
         sums_high = [turn_pair(1, slice(b, b + 1), number) for b, number in enumerate((5, 3))]
         turn_back(1, slice(0, 1), sums_high[0], "turned")

@@ -82,16 +82,17 @@ def tile_picked_unet_relu_e_kernel(tc, xT, w1, w2_words, w2_scales, skip, offs, 
         whole = slice(0, S)
         first, second = slice(0, S // 2), slice(S // 2, S)
         groups = (slice(0, 2), slice(2, 4))
-        w_bf = [keep.tile([P, g.stop - g.start, P, PACK], BF16, name="w_bf%d" % g.start, align_bytes=64) for g in groups]
+        w_bf = [keep.tile([P, 2 * H], BF16, name="w_bf%d" % g.start, align_bytes=64) for g in groups]
         w_codes = [keep.tile([P, g.stop - g.start, P], U32, name="w_codes%d" % g.start, align_bytes=64) for g in groups]
         w_exp = [keep.tile([P, g.stop - g.start, P], U8, name="w_exp%d" % g.start, align_bytes=64) for g in groups]
 
-        def dealt(n, raw, slots):
-            return w_bf[n][:, :, :, slots].rearrange("p t m e -> p m t e"), raw[:].rearrange("p e (m t) -> p m t e", t=PACK)[:, :, groups[n]]
+        def dealt(n, raw, slots, rows=slice(0, P)):
+            return (w_bf[n][:].rearrange("p (t m j) -> p m t j", t=2, j=PACK)[:, rows, :, slots],
+                    raw[:].rearrange("p e (m t) -> p m t e", t=PACK)[:, rows, groups[n]])
 
         def quantise_w(n, planes):
             quantise(w_codes[n][:, planes].rearrange("p t m -> p (t m)"), w_exp[n][:, planes].rearrange("p t m -> p (t m)"),
-                     w_bf[n][:, planes].rearrange("p t m j -> p (t m j)"))
+                     w_bf[n][:, H * planes.start : H * planes.stop])
 
         for n in range(len(groups)):
             nc.scalar.activation(*dealt(n, w_early, slice(0, 1)), ACT.Copy)
@@ -119,7 +120,8 @@ def tile_picked_unet_relu_e_kernel(tc, xT, w1, w2_words, w2_scales, skip, offs, 
         x_codes = [keep.tile([P, S // 2], U32, name="x_codes0", align_bytes=64)]
         quantise(x_codes[0][:], x_exp[0][:], x_bf[:, first].rearrange("p n j -> p (n j)"))
         nc.vector.tensor_copy(*dealt(0, w_late, slice(1, PACK)))
-        nc.scalar.copy(*dealt(1, w_late, slice(1, PACK)))
+        nc.scalar.copy(*dealt(1, w_late, slice(1, PACK), slice(P // 2, P)))
+        nc.vector.tensor_copy(*dealt(1, w_late, slice(1, PACK), slice(0, P // 2)))
         quantise_w(0, slice(0, 1))
         quantise_w(0, slice(1, 2))
         x_codes.append(keep.tile([P, S // 2], U32, name="x_codes1", tag="w_late", align_bytes=64))

@@ -21,6 +21,7 @@ P = 128
 PACK = 4
 PER_COLUMN = 16
 HEAD = 128
+LOWER = 64
 OPEN = 320
 LEAD = 288
 SHARE = 160
@@ -113,15 +114,15 @@ def tile_picked_unet_relu_e_kernel(tc, xT, w1, w2_words, w2_scales, skip, offs, 
         nc.vector.tensor_copy(x_bf[:, : fourth.start, 2], picked(2, slice(0, fourth.start)))
         nc.scalar.activation(x_own[:, 0], picked(2, fourth), ACT.Copy)
         nc.vector.tensor_copy(x_bf[:, first, 3], picked(3, first))
-        nc.scalar.activation(x_late[:], picked(3, third), ACT.Copy)
         nc.scalar.activation(x_own[:, 1], picked(3, fourth), ACT.Copy)
+        nc.scalar.activation(x_late[:], picked(3, third), ACT.Copy)
         nc.vector.tensor_copy(x_bf[:, third, 3], x_late[:])
         nc.scalar.copy(x_bf[:, fourth, 2:], x_own[:].rearrange("p e n -> p n e"))
         x_codes = [keep.tile([P, S // 2], U32, name="x_codes0", align_bytes=64)]
         quantise(x_codes[0][:], x_exp[0][:], x_bf[:, first].rearrange("p n j -> p (n j)"))
         nc.vector.tensor_copy(*dealt(0, w_late, slice(1, PACK)))
-        nc.scalar.copy(*dealt(1, w_late, slice(1, PACK), slice(P // 2, P)))
-        nc.vector.tensor_copy(*dealt(1, w_late, slice(1, PACK), slice(0, P // 2)))
+        nc.scalar.copy(*dealt(1, w_late, slice(1, PACK), slice(LOWER, P)))
+        nc.vector.tensor_copy(*dealt(1, w_late, slice(1, PACK), slice(0, LOWER)))
         quantise_w(0, slice(0, 1))
         quantise_w(0, slice(1, 2))
         x_codes.append(keep.tile([P, S // 2], U32, name="x_codes1", tag="w_late", align_bytes=64))

@@ -21,7 +21,7 @@ P = 128
 PACK = 4
 PER_COLUMN = 16
 HEAD = 128
-LOWER = 64
+LOWER = 40
 OPEN = 320
 LEAD = 288
 SHARE = 160

from contextlib import ExitStack

import concourse.mybir as mybir
from concourse.masks import make_identity

K, T, S, H, N, U = 512, 2048, 512, 512, 256, 1024
FLOPS = 2 * K * H * S + 2 * H * N * U

F32 = mybir.dt.float32
BF16 = mybir.dt.bfloat16
I32 = mybir.dt.int32
U32 = mybir.dt.uint32
U16 = mybir.dt.uint16
U8 = mybir.dt.uint8
FP8X4 = mybir.dt.float8_e4m3fn_x4
FP4X4 = mybir.dt.float4_e2m1fn_x4
ACT = mybir.ActivationFunctionType
ADD = mybir.AluOpType.add

P = 128
PACK = 4
PER_COLUMN = 16
HEAD = 128
LOWER = 40
OPEN = 320
LEAD = 288
SHARE = 160
WIDE = 256
DIRECT = 3


def tile_picked_unet_relu_e_kernel(tc, xT, w1, w2_words, w2_scales, skip, offs, cell, out):
    nc = tc.nc
    with ExitStack() as ctx:
        keep = ctx.enter_context(tc.tile_pool(name="keep", bufs=1))
        psum = ctx.enter_context(tc.psum_pool(name="psum", bufs=1))

        def bank(number, shape):
            return psum.tile([P] + shape, F32, name="bank", tag="bank%d" % number)

        offs_t = keep.tile([P, S // PER_COLUMN], U16, name="offs_t")
        cell_t = keep.tile([P, S // PER_COLUMN], U16, name="cell_t")
        x_rows = xT.rearrange("(p j) c -> j p c", j=PACK)
        x_plane = [keep.tile([P, T], F32, name="x_plane%d" % j) for j in range(PACK)]
        near = DIRECT * WIDE
        pairs = keep.tile([P, 2 * near], F32, name="pairs")
        s_first = keep.tile([P, near], F32, name="s_first")
        s_high = [keep.tile([P, 2, WIDE], F32, name="s_high", tag="s_high%d" % c, align_bytes=64) for c in range(DIRECT)]
        s_turn = keep.tile([P, PACK, WIDE], F32, name="s_turn")
        s_rows = skip.rearrange("(p t) c -> t p c", t=PACK)
        s_cells = skip.rearrange("(p t) (c v) -> p t c v", t=PACK, v=WIDE)
        w_rows = w1.rearrange("(p j) c -> p j c", j=PACK)
        w_early = keep.tile([P, 1, H], F32, name="w_early")
        w_late = keep.tile([P, PACK - 1, H], F32, name="w_late", tag="w_late", align_bytes=64)
        w2_codes = keep.tile([P, 2 * N], U8, name="w2_codes", align_bytes=64)
        w2_exp = keep.tile([P, N], U8, name="w2_exp", align_bytes=64)

        nc.sync.dma_start(w_early[:], w_rows[:, :1])
        nc.sync.dma_start(offs_t[:], offs)
        for j in range(PACK):
            nc.sync.dma_start(x_plane[j][:], x_rows[j])
        nc.sync.dma_start(w_late[:], w_rows[:, 1:])
        nc.sync.dma_start(cell_t[:], cell)
        nc.sync.dma_start(s_turn[:], s_cells[:, :, DIRECT])
        nc.sync.dma_start(s_first[:], s_rows[0][:, :near])
        nc.sync.dma_start(pairs[:, near:], s_rows[1][:, :near])
        for c in range(DIRECT):
            nc.sync.dma_start(s_high[c][:], s_cells[:, 2:, c])
        nc.sync.dma_start(w2_codes[:], w2_words[0])
        nc.vector.memset(w2_exp[:].bitcast(I32), 0)
        for q in range(4):
            nc.sync.dma_start(w2_exp[32 * q : 32 * q + 4, :].bitcast(I32), w2_scales[0, 4 * q : 4 * q + 4, :].bitcast(I32))

        window = [keep.tile([P, U], F32, name="window%d" % t) for t in range(PACK)]
        for t in range(PACK):
            nc.vector.memset(window[t][:], 0.0)
        ident = keep.tile([P, P], F32, name="ident")
        make_identity(nc, ident[:])

        def quantise(codes, exps, values):
            nc.vector.quantize_mx(out=codes.bitcast(FP8X4), scales=exps, in_=values)

        whole = slice(0, S)
        first, second = slice(0, S // 2), slice(S // 2, S)
        groups = (slice(0, 2), slice(2, 4))
        w_bf = [keep.tile([P, 2 * H], BF16, name="w_bf%d" % g.start, align_bytes=64) for g in groups]
        w_codes = [keep.tile([P, g.stop - g.start, P], U32, name="w_codes%d" % g.start, align_bytes=64) for g in groups]
        w_exp = [keep.tile([P, g.stop - g.start, P], U8, name="w_exp%d" % g.start, align_bytes=64) for g in groups]

        def dealt(n, raw, slots, rows=slice(0, P)):
            return (w_bf[n][:].rearrange("p (t m j) -> p m t j", t=2, j=PACK)[:, rows, :, slots],
                    raw[:].rearrange("p e (m t) -> p m t e", t=PACK)[:, rows, groups[n]])

        def quantise_w(n, planes):
            quantise(w_codes[n][:, planes].rearrange("p t m -> p (t m)"), w_exp[n][:, planes].rearrange("p t m -> p (t m)"),
                     w_bf[n][:, H * planes.start : H * planes.stop])

        for n in range(len(groups)):
            nc.scalar.activation(*dealt(n, w_early, slice(0, 1)), ACT.Copy)

        def columns(entries):
            return slice(entries.start // PER_COLUMN, entries.stop // PER_COLUMN)

        def picked(j, entries):
            return x_plane[j][:].indirect(offs_t[:, columns(entries)])

        x_bf = keep.tile([P, S, PACK], BF16, name="x_bf", align_bytes=64)
        x_late = keep.tile([P, HEAD], BF16, name="x_late")
        x_own = keep.tile([P, 2, HEAD], BF16, name="x_own")
        x_exp = [keep.tile([P, S // 2], U8, name="x_exp%d" % n, align_bytes=64) for n in range(2)]
        third, fourth = slice(S // 2, S - HEAD), slice(S - HEAD, S)
        for j in range(2):
            nc.vector.tensor_copy(x_bf[:, whole, j], picked(j, whole))
        nc.vector.tensor_copy(x_bf[:, : fourth.start, 2], picked(2, slice(0, fourth.start)))
        nc.scalar.activation(x_own[:, 0], picked(2, fourth), ACT.Copy)
        nc.vector.tensor_copy(x_bf[:, first, 3], picked(3, first))
        nc.scalar.activation(x_own[:, 1], picked(3, fourth), ACT.Copy)
        nc.scalar.activation(x_late[:], picked(3, third), ACT.Copy)
        nc.vector.tensor_copy(x_bf[:, third, 3], x_late[:])
        nc.scalar.copy(x_bf[:, fourth, 2:], x_own[:].rearrange("p e n -> p n e"))
        x_codes = [keep.tile([P, S // 2], U32, name="x_codes0", align_bytes=64)]
        quantise(x_codes[0][:], x_exp[0][:], x_bf[:, first].rearrange("p n j -> p (n j)"))
        nc.vector.tensor_copy(*dealt(0, w_late, slice(1, PACK)))
        nc.scalar.copy(*dealt(1, w_late, slice(1, PACK), slice(LOWER, P)))
        nc.vector.tensor_copy(*dealt(1, w_late, slice(1, PACK), slice(0, LOWER)))
        quantise_w(0, slice(0, 1))
        quantise_w(0, slice(1, 2))
        x_codes.append(keep.tile([P, S // 2], U32, name="x_codes1", tag="w_late", align_bytes=64))
        quantise(x_codes[1][:], x_exp[1][:], x_bf[:, second].rearrange("p n j -> p (n j)"))
        quantise_w(1, slice(0, 2))

        hidden = [keep.tile([P, S], F32, name="hidden", tag="hidden%d" % t, align_bytes=64) for t in range(PACK)]

        def product(acc, t, entries):
            n = entries.start // (S // 2)
            part = slice(entries.start - n * (S // 2), entries.stop - n * (S // 2))
            nc.tensor.matmul_mx(out=acc, lhsT=w_codes[t // 2][:, t % 2].bitcast(FP8X4), lhsT_scale=w_exp[t // 2][:, t % 2],
                                rhs=x_codes[n][:, part].bitcast(FP8X4), rhs_scale=x_exp[n][:, part], start=True, stop=True)

        def relu_scalar(t, entries, acc):
            nc.scalar.activation(hidden[t][:, entries], acc, ACT.Relu)

        def scatter_scalar(t, entries):
            nc.scalar.activation(window[t][:].indirect(cell_t[:, columns(entries)]), hidden[t][:, entries], ACT.Copy)

        def scatter_vector(t, entries):
            nc.vector.tensor_copy(window[t][:].indirect(cell_t[:, columns(entries)]), hidden[t][:, entries])

        back = bank(6, [2, WIDE])

        def turn_pair(u, blocks, number):
            parts = [(e, b) for e in (1, 0) for b in range(blocks.start, blocks.stop)]
            sums = bank(number, [blocks.stop - blocks.start, 2, P])
            terms = [(e, b, s_turn[:, 2 * u + e, P * b : P * (b + 1)]) for e, b in parts]
            terms += [(e, b, window[2 * u + e][:, near + P * b : near + P * (b + 1)]) for e, b in (parts if u else parts[::-1])]
            for n, (e, b, term) in enumerate(terms):
                nc.tensor.matmul(sums[:, b - blocks.start, e, :], term, ident[:], start=n == 0, stop=n == len(terms) - 1, is_transpose=True)
            return sums

        def turn_back(u, blocks, sums, tag):
            turned = keep.tile([P, blocks.stop - blocks.start, P], F32, name="turned", tag=tag, align_bytes=64)
            nc.scalar.copy(turned[:].bitcast(BF16).rearrange("p b (q e) -> p b q e", e=2), sums[:].rearrange("p b e q -> p b q e"))
            for b in range(blocks.start, blocks.stop):
                nc.tensor.transpose(back[:, u, P * b : P * (b + 1)], turned[:, b - blocks.start, :], ident[:])

        head, rest = slice(0, HEAD), slice(HEAD, S)
        acc = bank(0, [HEAD])
        product(acc[:], 0, head)
        relu_scalar(0, head, acc[:])
        scatter_vector(0, head)
        acc = bank(1, [S // 2])
        product(acc[:], 1, first)
        relu_scalar(1, first, acc[:])
        acc0, acc1 = bank(2, [S - HEAD]), bank(4, [OPEN - S // 2])
        product(acc0[:, :HEAD], 0, slice(HEAD, S // 2))
        product(acc1[:], 1, slice(S // 2, OPEN))
        product(acc0[:, HEAD:], 0, second)
        relu_scalar(1, slice(S // 2, OPEN), acc1[:])
        relu_scalar(0, rest, acc0[:])
        acc = bank(0, [S - OPEN])
        product(acc[:, : fourth.start - OPEN], 1, slice(OPEN, fourth.start))
        product(acc[:, fourth.start - OPEN :], 1, fourth)
        nc.vector.tensor_scalar_max(hidden[1][:, OPEN:], acc[:], 0.0)
        scatter_vector(0, rest)
        scatter_scalar(1, slice(0, LEAD))
        for t, number in ((3, 3), (2, 5)):
            acc = bank(number, [S])
            for part in (first, second):
                product(acc[:, part], t, part)
            relu_scalar(t, whole, acc[:])
        scatter_scalar(1, slice(LEAD, S))
        scatter_vector(3, slice(0, SHARE))
        scatter_vector(2, whole)
        scatter_scalar(3, slice(SHARE, S))
        turn_back(0, slice(0, 2), turn_pair(0, slice(0, 2), 2), "hidden3")
        sums_high = [turn_pair(1, slice(b, b + 1), number) for b, number in enumerate((5, 3))]
        turn_back(1, slice(0, 1), sums_high[0], "turned")

        pair_values = pairs[:].bitcast(BF16).rearrange("p (v e) -> p e v", e=2)
        nc.gpsimd.tensor_tensor(pair_values[:, 0, :near], window[0][:, :near], s_first[:], ADD)
        nc.gpsimd.tensor_tensor(pair_values[:, 1, :near], window[1][:, :near], pairs[:, near:], ADD)
        high_at = [near + WIDE * (c % 2) for c in range(DIRECT)]

        out_rows = out.rearrange("(g p) v -> p g v", p=P)
        z_bf, z_mx = {}, {}

        def add_skip(c, e):
            nc.vector.tensor_tensor(pair_values[:, e, high_at[c] : high_at[c] + WIDE], window[2 + e][:, WIDE * c : WIDE * (c + 1)], s_high[c][:, e], ADD)

        def weave(c, copy):
            z_bf[c] = keep.tile([P, WIDE, 2], F32, name="z_bf%d" % c, align_bytes=64)
            slots = pairs[:].rearrange("p (s v) -> p v s", v=WIDE)
            step = high_at[c] // WIDE - c
            copy(z_bf[c][:], slots[:, :, c : c + step + 1 : step])

        def quantise_z(c):
            codes = keep.tile([P, WIDE], U32, name="z_codes%d" % c, align_bytes=64)
            exps = keep.tile([P, WIDE], U8, name="z_exp%d" % c, align_bytes=64)
            quantise(codes[:], exps[:], z_bf[c][:].rearrange("p v u -> p (v u)").bitcast(BF16))
            z_mx[c] = codes, exps

        def finish(c, numbers, copies):
            codes, exps = z_mx[c]
            res = keep.tile([P, 2, WIDE], F32, name="res%d" % c)
            for g in range(2):
                acc_out = bank(numbers[g], [WIDE])
                nc.tensor.matmul_mx(out=acc_out[:], lhsT=w2_codes[:, 2 * P * g : 2 * P * (g + 1)].bitcast(FP4X4),
                                    lhsT_scale=w2_exp[:, P * g : P * (g + 1)],
                                    rhs=codes[:].bitcast(FP8X4), rhs_scale=exps[:], start=True, stop=True)
                copies[g](res[:, g, :], acc_out[:])
                nc.sync.dma_start(out_rows[:, g, WIDE * c : WIDE * (c + 1)], res[:, g, :])

        by_scalar, by_vector = nc.scalar.copy, nc.vector.tensor_copy
        add_skip(0, 1)
        add_skip(0, 0)
        weave(0, by_scalar)
        turn_back(1, slice(1, 2), sums_high[1], "s_high0")
        add_skip(1, 0)
        add_skip(1, 1)
        weave(1, by_scalar)
        quantise_z(0)
        add_skip(2, 0)
        add_skip(2, 1)
        finish(0, (7, 4), (by_scalar, by_scalar))
        quantise_z(1)
        z_bf[DIRECT] = keep.tile([P, WIDE, 2], F32, name="z_turned", align_bytes=64)
        nc.scalar.copy(z_bf[DIRECT][:], back[:].rearrange("p u v -> p v u"))
        weave(2, by_vector)
        quantise_z(DIRECT)
        quantise_z(2)
        finish(1, (1, 2), (by_scalar, by_scalar))
        finish(DIRECT, (0, 3), (by_vector, by_scalar))
        finish(2, (5, 7), (by_vector, by_scalar))
